import numpy as np
import ml_dtypes


def mxq(x, axis, fmt="e4m3"):
    dtype, down = {"e4m3": (ml_dtypes.float8_e4m3fn, 7), "e5m2": (ml_dtypes.float8_e5m2, 14)}[fmt]
    v = np.moveaxis(np.asarray(x, np.float32).astype(ml_dtypes.bfloat16).astype(np.float64), axis, -1)
    blocks = v.reshape(v.shape[:-1] + (-1, 32))
    amax = np.abs(blocks).max(-1, keepdims=True)
    byte = np.maximum(np.where(amax > 0, np.frexp(amax)[1] - 1 + 127, 0) - down, 1)
    scale = np.exp2(byte - 127.0)
    codes = (blocks / scale).astype(np.float32).astype(dtype).astype(np.float64)
    return np.moveaxis((codes * scale).reshape(v.shape), -1, axis)


WIDE = False


def mx_kscale(k):
    if not WIDE:
        return np.ones(k)
    levels = np.array([10, -10, 5, -5, 0])
    if k % 512:
        return np.exp2(np.random.permutation(np.resize(levels, k // 32))).repeat(32)
    a = np.empty((k // 512, 16))
    for p in range(k // 512):
        a[p, :8] = np.random.permutation(np.resize(levels, 8))
        for g in range(8):
            far = levels[np.abs(levels - a[p, g]) >= 10]
            a[p, g + 8] = far[np.random.randint(len(far))]
    return np.exp2(a.ravel()).repeat(32)


def f64(x):
    return np.asarray(x).astype(np.float64)


def striped(idx):
    return np.tile(idx.reshape(-1, 16).T, (8, 1)).astype(np.uint16)


def unstriped(offs):
    return offs[:16].T.reshape(-1).astype(np.int64)


E2M1 = np.array([0.0, 0.5, 1.0, 1.5, 2.0, 3.0, 4.0, 6.0, -0.0, -0.5, -1.0, -1.5, -2.0, -3.0, -4.0, -6.0])


def pack_weight(w, fmt):
    k, n = w.shape
    w = f64(np.asarray(w, np.float32).astype(ml_dtypes.bfloat16)).reshape(k // 32, 32, n)
    amax = np.abs(w).max(1)
    if fmt == "e4m3":
        byte = np.frexp(amax)[1] - 1 + 127 - 7
    else:
        mant, ex = np.frexp(amax / 6.0)
        byte = np.where(mant > 0.5, ex, ex - 1) + 127
    byte = np.clip(np.where(amax > 0, byte, 1), 1, 254)
    scaled = (w * np.exp2(127.0 - byte)[:, None, :]).reshape(k, n).astype(np.float32)
    by_word = np.ascontiguousarray(scaled.reshape(k // 512, 128, 4, n).transpose(0, 1, 3, 2))
    if fmt == "e4m3":
        words = by_word.astype(ml_dtypes.float8_e4m3fn).view(np.uint8)
    else:
        c = by_word.astype(ml_dtypes.float4_e2m1fn).view(np.uint8) & 0xF
        words = (c[..., 0::2] | (c[..., 1::2] << 4)).reshape(k // 512, 128, 2 * n)
    return np.ascontiguousarray(words), np.ascontiguousarray(byte.astype(np.uint8).reshape(k // 512, 16, n))


def unpack_weight(words, scales, fmt):
    g, _, n = scales.shape
    words = np.ascontiguousarray(words).reshape(g, 128, n, -1)
    if fmt == "e4m3":
        vals = words.view(ml_dtypes.float8_e4m3fn).astype(np.float64)
    else:
        nib = np.empty((g, 128, n, 4), np.uint8)
        nib[..., 0::2] = words & 0xF
        nib[..., 1::2] = words >> 4
        vals = E2M1[nib]
    vals = vals * np.repeat(np.exp2(scales.astype(np.float64) - 127.0), 8, axis=1)[..., None]
    return vals.transpose(0, 1, 3, 2).reshape(g * 512, n)


def sigmoid(v):
    return 1.0 / (1.0 + np.exp(-np.maximum(v, -700.0)))


K, T, E, C, H, N = 512, 1024, 6, 128, 512, 512


def by_expert(wq, xq):
    return np.concatenate([wq[e].T @ xq[:, e * C:(e + 1) * C] for e in range(E)], axis=1)


def setup_inputs():
    n = np.random.standard_normal
    s = mx_kscale(K)[:, None]
    u = mx_kscale(H)
    w1 = [pack_weight(m, "e2m1") for m in n((E, K, H)) / np.sqrt(K) / s[None]]
    w3 = [pack_weight(m, "e2m1") for m in n((E, K, H)) / np.sqrt(K) / s[None] * u[None, None, :]]
    w2 = [pack_weight(m, "e2m1") for m in n((E, H, N)) / np.sqrt(H) / u[None, :, None]]
    x = pack_weight(n((K, T)) * s, "e4m3")
    return {
        "x_words": x[0],
        "x_scales": x[1],
        "w1_words": np.stack([m[0] for m in w1]),
        "w1_scales": np.stack([m[1] for m in w1]),
        "w3_words": np.stack([m[0] for m in w3]),
        "w3_scales": np.stack([m[1] for m in w3]),
        "w2_words": np.stack([m[0] for m in w2]),
        "w2_scales": np.stack([m[1] for m in w2]),
        "gate": np.tile(np.random.uniform(0.2, 1.0, E * C), (N, 1)).astype(np.float32),
        "offs": striped(np.random.permutation(T)[:E * C]),
        "dst": striped(np.random.permutation(T)[:E * C]),
    }


def reference(x_words, x_scales, w1_words, w1_scales, w3_words, w3_scales, w2_words, w2_scales, gate, offs, dst):
    idx = unstriped(offs)
    w1 = np.stack([unpack_weight(w1_words[e], w1_scales[e], "e2m1") for e in range(E)])
    w3 = np.stack([unpack_weight(w3_words[e], w3_scales[e], "e2m1") for e in range(E)])
    w2 = np.stack([unpack_weight(w2_words[e], w2_scales[e], "e2m1") for e in range(E)])
    xq = unpack_weight(x_words, x_scales, "e4m3")[:, idx]
    h = sigmoid(by_expert(w1, xq))
    h = h * by_expert(w3, xq)
    y = by_expert(w2, mxq(h, 0, "e4m3"))
    out = np.zeros((N, T))
    out[:, unstriped(dst)] = f64(gate) * y
    return out

@@ -1,0 +1,167 @@
+from contextlib import ExitStack
+
+import concourse.mybir as mybir
+from concourse.masks import make_identity
+
+K, T, E, C, H, N = 512, 1024, 6, 128, 512, 512
+FLOPS = 2 * E * C * (2 * K * H + H * N)
+
+F32 = mybir.dt.float32
+BF16 = mybir.dt.bfloat16
+I32 = mybir.dt.int32
+U32 = mybir.dt.uint32
+U16 = mybir.dt.uint16
+U8 = mybir.dt.uint8
+FP8X4 = mybir.dt.float8_e4m3fn_x4
+FP4X4 = mybir.dt.float4_e2m1fn_x4
+MULT = mybir.AluOpType.mult
+SIGMOID = mybir.ActivationFunctionType.Sigmoid
+
+P = 128
+NT = N // P
+LIST_COLS = C // 16
+GATHER_GROUPS = ((0, 1), (1, 2), (2, 4), (4, 6))
+SCATTER_GROUPS = ((0, 1), (1, 3), (3, 6))
+WEIGHT_GROUPS = ((0, 2), (2, 6))
+
+
+def tile_moe_two_glu_sigmoid_kernel(tc, x_words, x_scales, w1_words, w1_scales, w3_words, w3_scales, w2_words, w2_scales, gate, offs, dst, out):
+    nc = tc.nc
+    with ExitStack() as ctx:
+        keep = ctx.enter_context(tc.tile_pool(name="keep", bufs=1))
+        ring = ctx.enter_context(tc.tile_pool(name="ring", bufs=3))
+        psum = ctx.enter_context(tc.psum_pool(name="psum", bufs=2))
+
+        offs_sb = keep.tile([P, E * LIST_COLS], U16, name="offs_sb")
+        dst_sb = keep.tile([P, E * LIST_COLS], U16, name="dst_sb")
+        x_sb = keep.tile([P, T], I32, name="x_sb", align_bytes=64)
+        x_plane = keep.tile([P, T], U8, name="x_plane", align_bytes=64)
+        planes = {}
+        for name in ("w1", "w3", "w2"):
+            planes[name] = keep.tile([P, E, H], U8, name=name + "_plane", align_bytes=64)
+        words = {}
+        for name in ("w1", "w3", "w2"):
+            for lo, hi in WEIGHT_GROUPS:
+                words[name, lo] = keep.tile([P, hi - lo, 2 * H], U8, name="%s_words%d" % (name, lo), align_bytes=64)
+        gates = {}
+        results = {}
+        for lo, hi in SCATTER_GROUPS:
+            gates[lo] = keep.tile([P, NT, (hi - lo) * C], F32, name="gate%d" % lo, align_bytes=64)
+            results[lo] = keep.tile([P, NT, (hi - lo) * C], F32, name="result%d" % lo, align_bytes=64)
+        windows = [keep.tile([P, T], F32, name="window%d" % t, align_bytes=64) for t in range(NT)]
+        identity = keep.tile([P, P], F32, name="identity", align_bytes=64)
+        warm_in = keep.tile([P, 8], F32, name="warm_in")
+        warm_out = keep.tile([P, 8], F32, name="warm_out")
+
+        def group_of(groups, e):
+            return [g for g in groups if g[0] <= e < g[1]][0]
+
+        def load_plane(plane, rows):
+            for r in range(4):
+                nc.sync.dma_start(plane.bitcast(I32)[r:P:32], rows.bitcast(I32)[r])
+
+        def load_weight_plane(name, scales):
+            load_plane(planes[name][:], scales.rearrange("e s (q r) n -> r q (e s) n", r=4))
+
+        def load_words(name, dram, group):
+            lo, hi = group
+            nc.sync.dma_start(words[name, lo][:].bitcast(I32), dram[lo:hi].rearrange("e s p b -> p (e s) b").bitcast(I32))
+
+        def load_gate(group):
+            lo, hi = group
+            nc.sync.dma_start(gates[lo][:], gate[:, lo * C : hi * C].rearrange("(t p) j -> p t j", p=P))
+
+        nc.vector.memset(x_plane[:].bitcast(I32), 0)
+        for name in ("w1", "w3", "w2"):
+            nc.vector.memset(planes[name][:].bitcast(I32), 0)
+        nc.gpsimd.memset(warm_in[:], 0.0)
+        nc.scalar.activation(warm_out[:], warm_in[:], SIGMOID)
+        make_identity(nc, identity[:])
+
+        nc.sync.dma_start(offs_sb[:], offs)
+        nc.sync.dma_start(x_sb[:], x_words[0].rearrange("p n t -> p (n t)").bitcast(I32))
+        load_plane(x_plane[:], x_scales.rearrange("o (q r) n -> r q (o n)", r=4))
+        load_words("w1", w1_words, WEIGHT_GROUPS[0])
+        load_words("w3", w3_words, WEIGHT_GROUPS[0])
+        load_weight_plane("w1", w1_scales)
+        load_weight_plane("w3", w3_scales)
+        load_words("w1", w1_words, WEIGHT_GROUPS[1])
+        load_words("w3", w3_words, WEIGHT_GROUPS[1])
+        load_weight_plane("w2", w2_scales)
+        load_words("w2", w2_words, WEIGHT_GROUPS[0])
+        nc.sync.dma_start(dst_sb[:], dst)
+        load_gate(SCATTER_GROUPS[0])
+        load_words("w2", w2_words, WEIGHT_GROUPS[1])
+        load_gate(SCATTER_GROUPS[1])
+        load_gate(SCATTER_GROUPS[2])
+
+        slot_words = {}
+        slot_scales = {}
+
+        def gather(group):
+            lo, hi = group
+            slot_words[lo] = keep.tile([P, (hi - lo) * C], U32, name="slot_words%d" % lo, align_bytes=64)
+            slot_scales[lo] = keep.tile([P, (hi - lo) * C], U8, name="slot_scales%d" % lo, align_bytes=64)
+            entries = offs_sb[:, lo * LIST_COLS : hi * LIST_COLS]
+            nc.vector.tensor_copy(slot_words[lo][:], x_sb[:].bitcast(U32).indirect(entries))
+            nc.vector.tensor_copy(slot_scales[lo][:], x_plane[:].indirect(entries))
+
+        for e in range(E):
+            g_lo = group_of(GATHER_GROUPS, e)[0]
+            w_lo = group_of(WEIGHT_GROUPS, e)[0]
+            s_lo = group_of(SCATTER_GROUPS, e)[0]
+            if e == g_lo:
+                gather(group_of(GATHER_GROUPS, e))
+            slots = slice((e - g_lo) * C, (e - g_lo + 1) * C)
+
+            sums = {}
+            for name in ("w1", "w3"):
+                sums[name] = psum.tile([P, H], F32, name="sum_" + name)
+                nc.tensor.matmul_mx(
+                    out=sums[name][:],
+                    lhsT=slot_words[g_lo][:, slots].bitcast(FP8X4),
+                    lhsT_scale=slot_scales[g_lo][:, slots],
+                    rhs=words[name, w_lo][:, e - w_lo, :].bitcast(FP4X4),
+                    rhs_scale=planes[name][:, e, :],
+                    start=True,
+                    stop=True,
+                )
+            sig = ring.tile([P, 2, P, 2], F32, name="sig", align_bytes=64)
+            nc.scalar.activation(sig[:], sums["w1"][:].rearrange("p (q u v) -> p u q v", u=2, v=2), SIGMOID)
+            h_t = ring.tile([P, 2, P, 2], BF16, name="h_t", align_bytes=64)
+            nc.vector.tensor_tensor(h_t[:], sums["w3"][:].rearrange("p (q u v) -> p u q v", u=2, v=2), sig[:], MULT)
+
+            pairs = h_t[:].rearrange("p u q v -> p (u q v)").bitcast(F32)
+            turned = psum.tile([P, 2, C], F32, name="turned")
+            for u in range(2):
+                nc.tensor.transpose(turned[:, u, :], pairs[:, u * P : (u + 1) * P], identity[:])
+            h = ring.tile([P, 4 * C], BF16, name="h", align_bytes=64)
+            nc.scalar.copy(h[:].bitcast(F32).rearrange("p (c u) -> p c u", u=2), turned[:].rearrange("p u c -> p c u"))
+            h_words = ring.tile([P, C], U32, name="h_words", align_bytes=64)
+            h_scales = ring.tile([P, C], U8, name="h_scales", align_bytes=64)
+            nc.vector.quantize_mx(out=h_words[:].bitcast(FP8X4), scales=h_scales[:], in_=h[:])
+
+            y = psum.tile([P, NT, C], F32, name="y")
+            for t in range(NT):
+                nc.tensor.matmul_mx(
+                    out=y[:, t, :],
+                    lhsT=words["w2", w_lo][:, e - w_lo, 2 * P * t : 2 * P * (t + 1)].bitcast(FP4X4),
+                    lhsT_scale=planes["w2"][:, e, P * t : P * (t + 1)],
+                    rhs=h_words[:].bitcast(FP8X4),
+                    rhs_scale=h_scales[:],
+                    start=True,
+                    stop=True,
+                )
+            cols = slice((e - s_lo) * C, (e - s_lo + 1) * C)
+            nc.vector.tensor_tensor(results[s_lo][:, :, cols], y[:], gates[s_lo][:, :, cols], MULT)
+
+        for t in range(2):
+            nc.vector.memset(windows[t][:], 0.0)
+        for t in range(2, NT):
+            nc.scalar.copy(windows[t][:], windows[0][:])
+        for lo, hi in SCATTER_GROUPS:
+            entries = dst_sb[:, lo * LIST_COLS : hi * LIST_COLS]
+            for t in range(NT):
+                nc.vector.tensor_copy(windows[t][:].indirect(entries), results[lo][:, t, :])
+        for t in range(NT):
+            nc.sync.dma_start(out[t * P : (t + 1) * P, :], windows[t][:])

@@ -21,8 +21,9 @@ P = 128
 NT = N // P
 LIST_COLS = C // 16
 GATHER_GROUPS = ((0, 1), (1, 2), (2, 4), (4, 6))
-SCATTER_GROUPS = ((0, 1), (1, 3), (3, 6))
-WEIGHT_GROUPS = ((0, 2), (2, 6))
+SCATTERS = ((0, 0, 1), (1, 0, 1), (2, 0, 1), (3, 0, 2), (0, 1, 2), (1, 1, 3), (2, 1, 4), (3, 2, 4), (0, 2, 5), (0, 5, 6), (1, 3, 6), (2, 4, 6), (3, 4, 6))
+GATE_GROUPS = ((0, 3), (3, 6))
+WEIGHT_GROUPS = ((0, 3), (3, 6))
 
 
 def tile_moe_two_glu_sigmoid_kernel(tc, x_words, x_scales, w1_words, w1_scales, w3_words, w3_scales, w2_words, w2_scales, gate, offs, dst, out):
@@ -39,19 +40,18 @@ def tile_moe_two_glu_sigmoid_kernel(tc, x_words, x_scales, w1_words, w1_scales, 
         planes = {}
         for name in ("w1", "w3", "w2"):
             planes[name] = keep.tile([P, E, H], U8, name=name + "_plane", align_bytes=64)
+        warm_in = keep.tile([P, 8], F32, name="warm_in")
+        warm_out = keep.tile([P, 8], F32, name="warm_out")
+        nc.gpsimd.memset(warm_in[:], 0.0)
+        nc.scalar.activation(warm_out[:], warm_in[:], SIGMOID)
+        gates = keep.tile([P, NT, E * C], F32, name="gates", align_bytes=64)
         words = {}
         for name in ("w1", "w3", "w2"):
             for lo, hi in WEIGHT_GROUPS:
-                words[name, lo] = keep.tile([P, hi - lo, 2 * H], U8, name="%s_words%d" % (name, lo), align_bytes=64)
-        gates = {}
-        results = {}
-        for lo, hi in SCATTER_GROUPS:
-            gates[lo] = keep.tile([P, NT, (hi - lo) * C], F32, name="gate%d" % lo, align_bytes=64)
-            results[lo] = keep.tile([P, NT, (hi - lo) * C], F32, name="result%d" % lo, align_bytes=64)
+                words[name, lo] = keep.tile([P, hi - lo, 2 * H], U8, name="%s_words%d" % (name, lo), align_bytes=64)[:]
+        results = keep.tile([P, NT, E * C], F32, name="results", align_bytes=64)
         windows = [keep.tile([P, T], F32, name="window%d" % t, align_bytes=64) for t in range(NT)]
         identity = keep.tile([P, P], F32, name="identity", align_bytes=64)
-        warm_in = keep.tile([P, 8], F32, name="warm_in")
-        warm_out = keep.tile([P, 8], F32, name="warm_out")
 
         def group_of(groups, e):
             return [g for g in groups if g[0] <= e < g[1]][0]
@@ -63,62 +63,61 @@ def tile_moe_two_glu_sigmoid_kernel(tc, x_words, x_scales, w1_words, w1_scales, 
         def load_weight_plane(name, scales):
             load_plane(planes[name][:], scales.rearrange("e s (q r) n -> r q (e s) n", r=4))
 
-        def load_words(name, dram, group):
+        def load_words(name, dram, group, queue=nc.sync):
             lo, hi = group
-            nc.sync.dma_start(words[name, lo][:].bitcast(I32), dram[lo:hi].rearrange("e s p b -> p (e s) b").bitcast(I32))
+            queue.dma_start(words[name, lo].bitcast(I32), dram[lo:hi].rearrange("e s p b -> p (e s) b").bitcast(I32))
 
         def load_gate(group):
             lo, hi = group
-            nc.sync.dma_start(gates[lo][:], gate[:, lo * C : hi * C].rearrange("(t p) j -> p t j", p=P))
+            nc.sync.dma_start(gates[:, :, lo * C : hi * C], gate[:, lo * C : hi * C].rearrange("(t p) j -> p t j", p=P))
 
         nc.vector.memset(x_plane[:].bitcast(I32), 0)
         for name in ("w1", "w3", "w2"):
             nc.vector.memset(planes[name][:].bitcast(I32), 0)
-        nc.gpsimd.memset(warm_in[:], 0.0)
-        nc.scalar.activation(warm_out[:], warm_in[:], SIGMOID)
+        load_words("w1", w1_words, WEIGHT_GROUPS[0], nc.gpsimd)
+        load_words("w3", w3_words, WEIGHT_GROUPS[0], nc.gpsimd)
         make_identity(nc, identity[:])
 
         nc.sync.dma_start(offs_sb[:], offs)
         nc.sync.dma_start(x_sb[:], x_words[0].rearrange("p n t -> p (n t)").bitcast(I32))
         load_plane(x_plane[:], x_scales.rearrange("o (q r) n -> r q (o n)", r=4))
-        load_words("w1", w1_words, WEIGHT_GROUPS[0])
-        load_words("w3", w3_words, WEIGHT_GROUPS[0])
         load_weight_plane("w1", w1_scales)
         load_weight_plane("w3", w3_scales)
-        load_words("w1", w1_words, WEIGHT_GROUPS[1])
-        load_words("w3", w3_words, WEIGHT_GROUPS[1])
+        nc.sync.dma_start(dst_sb[:], dst)
+        load_gate(GATE_GROUPS[0])
         load_weight_plane("w2", w2_scales)
         load_words("w2", w2_words, WEIGHT_GROUPS[0])
-        nc.sync.dma_start(dst_sb[:], dst)
-        load_gate(SCATTER_GROUPS[0])
+        load_words("w1", w1_words, WEIGHT_GROUPS[1])
+        load_words("w3", w3_words, WEIGHT_GROUPS[1])
         load_words("w2", w2_words, WEIGHT_GROUPS[1])
-        load_gate(SCATTER_GROUPS[1])
-        load_gate(SCATTER_GROUPS[2])
+        load_gate(GATE_GROUPS[1])
 
         slot_words = {}
         slot_scales = {}
 
         def gather(group):
             lo, hi = group
-            slot_words[lo] = keep.tile([P, (hi - lo) * C], U32, name="slot_words%d" % lo, align_bytes=64)
+            slot_words[lo] = ring.tile([P, (hi - lo) * C], U32, name="slot_words", align_bytes=64, bufs=3)
             slot_scales[lo] = keep.tile([P, (hi - lo) * C], U8, name="slot_scales%d" % lo, align_bytes=64)
             entries = offs_sb[:, lo * LIST_COLS : hi * LIST_COLS]
             nc.vector.tensor_copy(slot_words[lo][:], x_sb[:].bitcast(U32).indirect(entries))
             nc.vector.tensor_copy(slot_scales[lo][:], x_plane[:].indirect(entries))
 
-        for e in range(E):
+        banks = [psum.tile([P, NT, C], F32, name="bank%d" % b, bufs=1) for b in range(2)]
+        quantised = {}
+
+        def first_layer(e):
             g_lo = group_of(GATHER_GROUPS, e)[0]
             w_lo = group_of(WEIGHT_GROUPS, e)[0]
-            s_lo = group_of(SCATTER_GROUPS, e)[0]
             if e == g_lo:
                 gather(group_of(GATHER_GROUPS, e))
             slots = slice((e - g_lo) * C, (e - g_lo + 1) * C)
 
-            sums = {}
+            pair = psum.tile([P, 2, H], F32, name="pair")
+            sums = {"w1": pair[:, 0, :], "w3": pair[:, 1, :]}
             for name in ("w1", "w3"):
-                sums[name] = psum.tile([P, H], F32, name="sum_" + name)
                 nc.tensor.matmul_mx(
-                    out=sums[name][:],
+                    out=sums[name],
                     lhsT=slot_words[g_lo][:, slots].bitcast(FP8X4),
                     lhsT_scale=slot_scales[g_lo][:, slots],
                     rhs=words[name, w_lo][:, e - w_lo, :].bitcast(FP4X4),
@@ -127,21 +126,25 @@ def tile_moe_two_glu_sigmoid_kernel(tc, x_words, x_scales, w1_words, w1_scales, 
                     stop=True,
                 )
             sig = ring.tile([P, 2, P, 2], F32, name="sig", align_bytes=64)
-            nc.scalar.activation(sig[:], sums["w1"][:].rearrange("p (q u v) -> p u q v", u=2, v=2), SIGMOID)
-            h_t = ring.tile([P, 2, P, 2], BF16, name="h_t", align_bytes=64)
-            nc.vector.tensor_tensor(h_t[:], sums["w3"][:].rearrange("p (q u v) -> p u q v", u=2, v=2), sig[:], MULT)
+            nc.scalar.activation(sig[:], sums["w1"].rearrange("p (q u v) -> p u q v", u=2, v=2), SIGMOID)
+            h_t = ring.tile([P, 2, P, 2], BF16, name="h_t", align_bytes=64, bufs=E)
+            nc.vector.tensor_tensor(h_t[:], sums["w3"].rearrange("p (q u v) -> p u q v", u=2, v=2), sig[:], MULT)
 
             pairs = h_t[:].rearrange("p u q v -> p (u q v)").bitcast(F32)
-            turned = psum.tile([P, 2, C], F32, name="turned")
+            turned = banks[e % 2][:, 0:2, :]
             for u in range(2):
                 nc.tensor.transpose(turned[:, u, :], pairs[:, u * P : (u + 1) * P], identity[:])
             h = ring.tile([P, 4 * C], BF16, name="h", align_bytes=64)
-            nc.scalar.copy(h[:].bitcast(F32).rearrange("p (c u) -> p c u", u=2), turned[:].rearrange("p u c -> p c u"))
+            nc.scalar.copy(h[:].bitcast(F32).rearrange("p (c u) -> p c u", u=2), turned.rearrange("p u c -> p c u"))
             h_words = ring.tile([P, C], U32, name="h_words", align_bytes=64)
             h_scales = ring.tile([P, C], U8, name="h_scales", align_bytes=64)
             nc.vector.quantize_mx(out=h_words[:].bitcast(FP8X4), scales=h_scales[:], in_=h[:])
+            quantised[e] = (h_words, h_scales)
 
-            y = psum.tile([P, NT, C], F32, name="y")
+        def second_layer(e):
+            w_lo = group_of(WEIGHT_GROUPS, e)[0]
+            h_words, h_scales = quantised[e]
+            y = banks[0] if e == 0 else banks[(e + 1) % 2]
             for t in range(NT):
                 nc.tensor.matmul_mx(
                     out=y[:, t, :],
@@ -152,16 +155,22 @@ def tile_moe_two_glu_sigmoid_kernel(tc, x_words, x_scales, w1_words, w1_scales, 
                     start=True,
                     stop=True,
                 )
-            cols = slice((e - s_lo) * C, (e - s_lo + 1) * C)
-            nc.vector.tensor_tensor(results[s_lo][:, :, cols], y[:], gates[s_lo][:, :, cols], MULT)
+            for t0, t1 in ((0, 1), (1, NT)) if e == 0 else ((0, NT),):
+                nc.scalar.copy(results[:, t0:t1, e * C : (e + 1) * C], y[:, t0:t1, :])
 
-        for t in range(2):
-            nc.vector.memset(windows[t][:], 0.0)
-        for t in range(2, NT):
-            nc.scalar.copy(windows[t][:], windows[0][:])
-        for lo, hi in SCATTER_GROUPS:
+        first_layer(0)
+        for e in range(E):
+            if e + 1 < E:
+                first_layer(e + 1)
+            second_layer(e)
+
+        for t in (1, 0):
+            nc.scalar.copy(windows[t][:], warm_in[:, 0:1].to_broadcast([P, T]))
+        for t in (2, 3):
+            nc.gpsimd.memset(windows[t][:], 0.0)
+        for t, lo, hi in SCATTERS:
             entries = dst_sb[:, lo * LIST_COLS : hi * LIST_COLS]
-            for t in range(NT):
-                nc.vector.tensor_copy(windows[t][:].indirect(entries), results[lo][:, t, :])
+            cols = slice(lo * C, hi * C)
+            nc.vector.tensor_tensor(windows[t][:].indirect(entries), results[:, t, cols], gates[:, t, cols], MULT)
         for t in range(NT):
             nc.sync.dma_start(out[t * P : (t + 1) * P, :], windows[t][:])

@@ -74,14 +74,14 @@ def tile_moe_two_glu_sigmoid_kernel(tc, x_words, x_scales, w1_words, w1_scales, 
         nc.vector.memset(x_plane[:].bitcast(I32), 0)
         for name in ("w1", "w3", "w2"):
             nc.vector.memset(planes[name][:].bitcast(I32), 0)
-        load_words("w1", w1_words, WEIGHT_GROUPS[0], nc.gpsimd)
-        load_words("w3", w3_words, WEIGHT_GROUPS[0], nc.gpsimd)
         make_identity(nc, identity[:])
 
         nc.sync.dma_start(offs_sb[:], offs)
         nc.sync.dma_start(x_sb[:], x_words[0].rearrange("p n t -> p (n t)").bitcast(I32))
         load_plane(x_plane[:], x_scales.rearrange("o (q r) n -> r q (o n)", r=4))
+        load_words("w1", w1_words, WEIGHT_GROUPS[0])
         load_weight_plane("w1", w1_scales)
+        load_words("w3", w3_words, WEIGHT_GROUPS[0])
         load_weight_plane("w3", w3_scales)
         nc.sync.dma_start(dst_sb[:], dst)
         load_gate(GATE_GROUPS[0])
@@ -164,10 +164,8 @@ def tile_moe_two_glu_sigmoid_kernel(tc, x_words, x_scales, w1_words, w1_scales, 
                 first_layer(e + 1)
             second_layer(e)
 
-        for t in (1, 0):
+        for t in range(NT):
             nc.scalar.copy(windows[t][:], warm_in[:, 0:1].to_broadcast([P, T]))
-        for t in (2, 3):
-            nc.gpsimd.memset(windows[t][:], 0.0)
         for t, lo, hi in SCATTERS:
             entries = dst_sb[:, lo * LIST_COLS : hi * LIST_COLS]
             cols = slice(lo * C, hi * C)

@@ -21,9 +21,7 @@ P = 128
 NT = N // P
 LIST_COLS = C // 16
 GATHER_GROUPS = ((0, 1), (1, 2), (2, 4), (4, 6))
-SCATTERS = ((0, 0, 1), (1, 0, 1), (2, 0, 1), (3, 0, 2), (0, 1, 2), (1, 1, 3), (2, 1, 4), (3, 2, 4), (0, 2, 5), (0, 5, 6), (1, 3, 6), (2, 4, 6), (3, 4, 6))
-GATE_GROUPS = ((0, 3), (3, 6))
-WEIGHT_GROUPS = ((0, 3), (3, 6))
+SCATTERS = ((0, 0, 1), (1, 0, 1), (2, 0, 1), (0, 1, 2), (3, 0, 2), (1, 1, 3), (3, 2, 4), (2, 1, 5), (0, 2, 6), (1, 3, 6), (2, 5, 6), (3, 4, 6))
 
 
 def tile_moe_two_glu_sigmoid_kernel(tc, x_words, x_scales, w1_words, w1_scales, w3_words, w3_scales, w2_words, w2_scales, gate, offs, dst, out):
@@ -47,8 +45,7 @@ def tile_moe_two_glu_sigmoid_kernel(tc, x_words, x_scales, w1_words, w1_scales, 
         gates = keep.tile([P, NT, E * C], F32, name="gates", align_bytes=64)
         words = {}
         for name in ("w1", "w3", "w2"):
-            for lo, hi in WEIGHT_GROUPS:
-                words[name, lo] = keep.tile([P, hi - lo, 2 * H], U8, name="%s_words%d" % (name, lo), align_bytes=64)[:]
+            words[name] = keep.tile([P, E, 2 * H], U8, name=name + "_words", align_bytes=64)
         results = keep.tile([P, NT, E * C], F32, name="results", align_bytes=64)
         windows = [keep.tile([P, T], F32, name="window%d" % t, align_bytes=64) for t in range(NT)]
         identity = keep.tile([P, P], F32, name="identity", align_bytes=64)
@@ -63,12 +60,10 @@ def tile_moe_two_glu_sigmoid_kernel(tc, x_words, x_scales, w1_words, w1_scales, 
         def load_weight_plane(name, scales):
             load_plane(planes[name][:], scales.rearrange("e s (q r) n -> r q (e s) n", r=4))
 
-        def load_words(name, dram, group, queue=nc.sync):
-            lo, hi = group
-            queue.dma_start(words[name, lo].bitcast(I32), dram[lo:hi].rearrange("e s p b -> p (e s) b").bitcast(I32))
+        def load_words(name, dram, lo, hi):
+            nc.sync.dma_start(words[name][:, lo:hi, :].bitcast(I32), dram[lo:hi].rearrange("e s p b -> p (e s) b").bitcast(I32))
 
-        def load_gate(group):
-            lo, hi = group
+        def load_gate(lo, hi):
             nc.sync.dma_start(gates[:, :, lo * C : hi * C], gate[:, lo * C : hi * C].rearrange("(t p) j -> p t j", p=P))
 
         nc.vector.memset(x_plane[:].bitcast(I32), 0)
@@ -79,18 +74,19 @@ def tile_moe_two_glu_sigmoid_kernel(tc, x_words, x_scales, w1_words, w1_scales, 
         nc.sync.dma_start(offs_sb[:], offs)
         nc.sync.dma_start(x_sb[:], x_words[0].rearrange("p n t -> p (n t)").bitcast(I32))
         load_plane(x_plane[:], x_scales.rearrange("o (q r) n -> r q (o n)", r=4))
-        load_words("w1", w1_words, WEIGHT_GROUPS[0])
+        load_words("w1", w1_words, 0, 3)
         load_weight_plane("w1", w1_scales)
-        load_words("w3", w3_words, WEIGHT_GROUPS[0])
+        load_words("w3", w3_words, 0, 3)
         load_weight_plane("w3", w3_scales)
         nc.sync.dma_start(dst_sb[:], dst)
-        load_gate(GATE_GROUPS[0])
         load_weight_plane("w2", w2_scales)
-        load_words("w2", w2_words, WEIGHT_GROUPS[0])
-        load_words("w1", w1_words, WEIGHT_GROUPS[1])
-        load_words("w3", w3_words, WEIGHT_GROUPS[1])
-        load_words("w2", w2_words, WEIGHT_GROUPS[1])
-        load_gate(GATE_GROUPS[1])
+        load_gate(0, 1)
+        load_words("w2", w2_words, 0, 2)
+        load_words("w1", w1_words, 3, 6)
+        load_words("w3", w3_words, 3, 6)
+        load_gate(1, 3)
+        load_words("w2", w2_words, 2, 6)
+        load_gate(3, 6)
 
         slot_words = {}
         slot_scales = {}
@@ -104,11 +100,11 @@ def tile_moe_two_glu_sigmoid_kernel(tc, x_words, x_scales, w1_words, w1_scales, 
             nc.vector.tensor_copy(slot_scales[lo][:], x_plane[:].indirect(entries))
 
         banks = [psum.tile([P, NT, C], F32, name="bank%d" % b, bufs=1) for b in range(2)]
+        first_bank = psum.tile([P, C], F32, name="first_bank", bufs=1)
         quantised = {}
 
         def first_layer(e):
             g_lo = group_of(GATHER_GROUPS, e)[0]
-            w_lo = group_of(WEIGHT_GROUPS, e)[0]
             if e == g_lo:
                 gather(group_of(GATHER_GROUPS, e))
             slots = slice((e - g_lo) * C, (e - g_lo + 1) * C)
@@ -120,7 +116,7 @@ def tile_moe_two_glu_sigmoid_kernel(tc, x_words, x_scales, w1_words, w1_scales, 
                     out=sums[name],
                     lhsT=slot_words[g_lo][:, slots].bitcast(FP8X4),
                     lhsT_scale=slot_scales[g_lo][:, slots],
-                    rhs=words[name, w_lo][:, e - w_lo, :].bitcast(FP4X4),
+                    rhs=words[name][:, e, :].bitcast(FP4X4),
                     rhs_scale=planes[name][:, e, :],
                     start=True,
                     stop=True,
@@ -142,21 +138,23 @@ def tile_moe_two_glu_sigmoid_kernel(tc, x_words, x_scales, w1_words, w1_scales, 
             quantised[e] = (h_words, h_scales)
 
         def second_layer(e):
-            w_lo = group_of(WEIGHT_GROUPS, e)[0]
             h_words, h_scales = quantised[e]
             y = banks[0] if e == 0 else banks[(e + 1) % 2]
+            sums = [first_bank[:] if (e, t) == (0, 0) else y[:, t, :] for t in range(NT)]
             for t in range(NT):
                 nc.tensor.matmul_mx(
-                    out=y[:, t, :],
-                    lhsT=words["w2", w_lo][:, e - w_lo, 2 * P * t : 2 * P * (t + 1)].bitcast(FP4X4),
+                    out=sums[t],
+                    lhsT=words["w2"][:, e, 2 * P * t : 2 * P * (t + 1)].bitcast(FP4X4),
                     lhsT_scale=planes["w2"][:, e, P * t : P * (t + 1)],
                     rhs=h_words[:].bitcast(FP8X4),
                     rhs_scale=h_scales[:],
                     start=True,
                     stop=True,
                 )
-            for t0, t1 in ((0, 1), (1, NT)) if e == 0 else ((0, NT),):
-                nc.scalar.copy(results[:, t0:t1, e * C : (e + 1) * C], y[:, t0:t1, :])
+            t0 = 1 if e == 0 else 0
+            if e == 0:
+                nc.scalar.copy(results[:, 0, 0:C], first_bank[:])
+            nc.scalar.copy(results[:, t0:NT, e * C : (e + 1) * C], y[:, t0:NT, :])
 
         first_layer(0)
         for e in range(E):

@@ -20,28 +20,41 @@ SIGMOID = mybir.ActivationFunctionType.Sigmoid
 P = 128
 NT = N // P
 LIST_COLS = C // 16
-GATHER_GROUPS = ((0, 1), (1, 2), (2, 4), (4, 6))
-SCATTERS = ((0, 0, 1), (1, 0, 1), (2, 0, 1), (0, 1, 2), (3, 0, 2), (1, 1, 3), (3, 2, 4), (2, 1, 5), (0, 2, 6), (1, 3, 6), (2, 5, 6), (3, 4, 6))
+PLANE_ROWS = 4
+PAIR_BUFS = 3
+RING_BUFS = 3
+
+WORD_GROUPS = ((0, 4), (4, 6))
+SCALE_GROUPS = ((0, 2), (2, 6))
+
+SCATTERS = (
+    (0, 0, 1), (1, 0, 1), (2, 0, 1), (3, 0, 1),
+    (0, 1, 2), (1, 1, 2), (3, 1, 2),
+    (2, 1, 3), (1, 2, 3),
+    (3, 2, 4), (1, 3, 4),
+    (0, 2, 5), (2, 3, 5),
+    (0, 5, 6), (2, 5, 6), (1, 4, 6), (3, 4, 6),
+)
 
 
-def tile_moe_two_glu_sigmoid_kernel(tc, x_words, x_scales, w1_words, w1_scales, w3_words, w3_scales, w2_words, w2_scales, gate, offs, dst, out):
+def tile_moe_two_glu_sigmoid_kernel(
+    tc, x_words, x_scales, w1_words, w1_scales, w3_words, w3_scales, w2_words, w2_scales, gate, offs, dst, out
+):
     nc = tc.nc
     with ExitStack() as ctx:
         keep = ctx.enter_context(tc.tile_pool(name="keep", bufs=1))
-        ring = ctx.enter_context(tc.tile_pool(name="ring", bufs=3))
-        psum = ctx.enter_context(tc.psum_pool(name="psum", bufs=2))
+        ring = ctx.enter_context(tc.tile_pool(name="ring", bufs=RING_BUFS))
+        psum = ctx.enter_context(tc.psum_pool(name="psum", bufs=PAIR_BUFS))
 
         offs_sb = keep.tile([P, E * LIST_COLS], U16, name="offs_sb")
         dst_sb = keep.tile([P, E * LIST_COLS], U16, name="dst_sb")
         x_sb = keep.tile([P, T], I32, name="x_sb", align_bytes=64)
-        x_plane = keep.tile([P, T], U8, name="x_plane", align_bytes=64)
+        x_plane = keep.tile([P, T], U8, name="x_plane", tag="x_plane", align_bytes=64)
         planes = {}
         for name in ("w1", "w3", "w2"):
             planes[name] = keep.tile([P, E, H], U8, name=name + "_plane", align_bytes=64)
-        warm_in = keep.tile([P, 8], F32, name="warm_in")
-        warm_out = keep.tile([P, 8], F32, name="warm_out")
-        nc.gpsimd.memset(warm_in[:], 0.0)
-        nc.scalar.activation(warm_out[:], warm_in[:], SIGMOID)
+        zero = keep.tile([P, 8], F32, name="zero")
+        nc.gpsimd.memset(zero[:], 0.0)
         gates = keep.tile([P, NT, E * C], F32, name="gates", align_bytes=64)
         words = {}
         for name in ("w1", "w3", "w2"):
@@ -50,18 +63,18 @@ def tile_moe_two_glu_sigmoid_kernel(tc, x_words, x_scales, w1_words, w1_scales, 
         windows = [keep.tile([P, T], F32, name="window%d" % t, align_bytes=64) for t in range(NT)]
         identity = keep.tile([P, P], F32, name="identity", align_bytes=64)
 
-        def group_of(groups, e):
-            return [g for g in groups if g[0] <= e < g[1]][0]
+        def first_of(groups, e):
+            return [lo for lo, hi in groups if lo <= e < hi][0]
 
         def load_plane(plane, rows):
-            for r in range(4):
+            for r in range(PLANE_ROWS):
                 nc.sync.dma_start(plane.bitcast(I32)[r:P:32], rows.bitcast(I32)[r])
 
         def load_weight_plane(name, scales):
-            load_plane(planes[name][:], scales.rearrange("e s (q r) n -> r q (e s) n", r=4))
+            load_plane(planes[name][:], scales.rearrange("e s (q r) n -> r q (e s) n", r=PLANE_ROWS))
 
         def load_words(name, dram, lo, hi):
-            nc.sync.dma_start(words[name][:, lo:hi, :].bitcast(I32), dram[lo:hi].rearrange("e s p b -> p (e s) b").bitcast(I32))
+            nc.sync.dma_start(words[name][:, lo:hi, :].bitcast(I32), dram.bitcast(I32)[lo:hi].rearrange("e s p b -> p (e s) b"))
 
         def load_gate(lo, hi):
             nc.sync.dma_start(gates[:, :, lo * C : hi * C], gate[:, lo * C : hi * C].rearrange("(t p) j -> p t j", p=P))
@@ -73,63 +86,67 @@ def tile_moe_two_glu_sigmoid_kernel(tc, x_words, x_scales, w1_words, w1_scales, 
 
         nc.sync.dma_start(offs_sb[:], offs)
         nc.sync.dma_start(x_sb[:], x_words[0].rearrange("p n t -> p (n t)").bitcast(I32))
-        load_plane(x_plane[:], x_scales.rearrange("o (q r) n -> r q (o n)", r=4))
-        load_words("w1", w1_words, 0, 3)
+        load_plane(x_plane[:], x_scales.rearrange("o (q r) n -> r q (o n)", r=PLANE_ROWS))
+        load_words("w1", w1_words, 0, 2)
         load_weight_plane("w1", w1_scales)
         load_words("w3", w3_words, 0, 3)
         load_weight_plane("w3", w3_scales)
+        load_words("w1", w1_words, 2, 3)
         nc.sync.dma_start(dst_sb[:], dst)
         load_weight_plane("w2", w2_scales)
         load_gate(0, 1)
         load_words("w2", w2_words, 0, 2)
-        load_words("w1", w1_words, 3, 6)
-        load_words("w3", w3_words, 3, 6)
+        load_words("w1", w1_words, 3, E)
+        load_words("w3", w3_words, 3, E)
         load_gate(1, 3)
-        load_words("w2", w2_words, 2, 6)
-        load_gate(3, 6)
+        load_words("w2", w2_words, 2, E)
+        load_gate(3, E)
 
         slot_words = {}
         slot_scales = {}
 
-        def gather(group):
-            lo, hi = group
-            slot_words[lo] = ring.tile([P, (hi - lo) * C], U32, name="slot_words", align_bytes=64, bufs=3)
+        def gather_words(lo, hi, tag):
+            slot_words[lo] = keep.tile([P, (hi - lo) * C], U32, name="slot_words%d" % lo, tag=tag, align_bytes=64)
+            nc.vector.tensor_copy(slot_words[lo][:], x_sb[:].bitcast(U32).indirect(offs_sb[:, lo * LIST_COLS : hi * LIST_COLS]))
+
+        def gather_scales(lo, hi):
             slot_scales[lo] = keep.tile([P, (hi - lo) * C], U8, name="slot_scales%d" % lo, align_bytes=64)
-            entries = offs_sb[:, lo * LIST_COLS : hi * LIST_COLS]
-            nc.vector.tensor_copy(slot_words[lo][:], x_sb[:].bitcast(U32).indirect(entries))
-            nc.vector.tensor_copy(slot_scales[lo][:], x_plane[:].indirect(entries))
+            nc.vector.tensor_copy(slot_scales[lo][:], x_plane[:].indirect(offs_sb[:, lo * LIST_COLS : hi * LIST_COLS]))
+
+        gather_words(*WORD_GROUPS[0], "slot_words0")
+        for group in SCALE_GROUPS:
+            gather_scales(*group)
+        gather_words(*WORD_GROUPS[1], "x_plane")
 
         banks = [psum.tile([P, NT, C], F32, name="bank%d" % b, bufs=1) for b in range(2)]
-        first_bank = psum.tile([P, C], F32, name="first_bank", bufs=1)
         quantised = {}
 
         def first_layer(e):
-            g_lo = group_of(GATHER_GROUPS, e)[0]
-            if e == g_lo:
-                gather(group_of(GATHER_GROUPS, e))
-            slots = slice((e - g_lo) * C, (e - g_lo + 1) * C)
+            w_lo = first_of(WORD_GROUPS, e)
+            s_lo = first_of(SCALE_GROUPS, e)
 
             pair = psum.tile([P, 2, H], F32, name="pair")
             sums = {"w1": pair[:, 0, :], "w3": pair[:, 1, :]}
             for name in ("w1", "w3"):
                 nc.tensor.matmul_mx(
                     out=sums[name],
-                    lhsT=slot_words[g_lo][:, slots].bitcast(FP8X4),
-                    lhsT_scale=slot_scales[g_lo][:, slots],
+                    lhsT=slot_words[w_lo][:, (e - w_lo) * C : (e - w_lo + 1) * C].bitcast(FP8X4),
+                    lhsT_scale=slot_scales[s_lo][:, (e - s_lo) * C : (e - s_lo + 1) * C],
                     rhs=words[name][:, e, :].bitcast(FP4X4),
                     rhs_scale=planes[name][:, e, :],
                     start=True,
                     stop=True,
                 )
+
             sig = ring.tile([P, 2, P, 2], F32, name="sig", align_bytes=64)
             nc.scalar.activation(sig[:], sums["w1"].rearrange("p (q u v) -> p u q v", u=2, v=2), SIGMOID)
             h_t = ring.tile([P, 2, P, 2], BF16, name="h_t", align_bytes=64, bufs=E)
             nc.vector.tensor_tensor(h_t[:], sums["w3"].rearrange("p (q u v) -> p u q v", u=2, v=2), sig[:], MULT)
 
-            pairs = h_t[:].rearrange("p u q v -> p (u q v)").bitcast(F32)
+            value_pairs = h_t[:].rearrange("p u q v -> p (u q v)").bitcast(F32)
             turned = banks[e % 2][:, 0:2, :]
             for u in range(2):
-                nc.tensor.transpose(turned[:, u, :], pairs[:, u * P : (u + 1) * P], identity[:])
+                nc.tensor.transpose(turned[:, u, :], value_pairs[:, u * P : (u + 1) * P], identity[:])
             h = ring.tile([P, 4 * C], BF16, name="h", align_bytes=64)
             nc.scalar.copy(h[:].bitcast(F32).rearrange("p (c u) -> p c u", u=2), turned.rearrange("p u c -> p c u"))
             h_words = ring.tile([P, C], U32, name="h_words", align_bytes=64)
@@ -139,11 +156,11 @@ def tile_moe_two_glu_sigmoid_kernel(tc, x_words, x_scales, w1_words, w1_scales, 
 
         def second_layer(e):
             h_words, h_scales = quantised[e]
-            y = banks[0] if e == 0 else banks[(e + 1) % 2]
-            sums = [first_bank[:] if (e, t) == (0, 0) else y[:, t, :] for t in range(NT)]
+            y = banks[(e + 1) % 2]
+            early = banks[0][:, 0, :]
             for t in range(NT):
                 nc.tensor.matmul_mx(
-                    out=sums[t],
+                    out=early if (e, t) == (0, 0) else y[:, t, :],
                     lhsT=words["w2"][:, e, 2 * P * t : 2 * P * (t + 1)].bitcast(FP4X4),
                     lhsT_scale=planes["w2"][:, e, P * t : P * (t + 1)],
                     rhs=h_words[:].bitcast(FP8X4),
@@ -153,7 +170,7 @@ def tile_moe_two_glu_sigmoid_kernel(tc, x_words, x_scales, w1_words, w1_scales, 
                 )
             t0 = 1 if e == 0 else 0
             if e == 0:
-                nc.scalar.copy(results[:, 0, 0:C], first_bank[:])
+                nc.scalar.copy(results[:, 0, 0:C], early)
             nc.scalar.copy(results[:, t0:NT, e * C : (e + 1) * C], y[:, t0:NT, :])
 
         first_layer(0)
@@ -163,7 +180,7 @@ def tile_moe_two_glu_sigmoid_kernel(tc, x_words, x_scales, w1_words, w1_scales, 
             second_layer(e)
 
         for t in range(NT):
-            nc.scalar.copy(windows[t][:], warm_in[:, 0:1].to_broadcast([P, T]))
+            nc.scalar.copy(windows[t][:], zero[:, 0:1].to_broadcast([P, T]))
         for t, lo, hi in SCATTERS:
             entries = dst_sb[:, lo * LIST_COLS : hi * LIST_COLS]
             cols = slice(lo * C, hi * C)

@@ -24,17 +24,8 @@ PLANE_ROWS = 4
 PAIR_BUFS = 3
 RING_BUFS = 3
 
-WORD_GROUPS = ((0, 4), (4, 6))
-SCALE_GROUPS = ((0, 2), (2, 6))
-
-SCATTERS = (
-    (0, 0, 1), (1, 0, 1), (2, 0, 1), (3, 0, 1),
-    (0, 1, 2), (1, 1, 2), (3, 1, 2),
-    (2, 1, 3), (1, 2, 3),
-    (3, 2, 4), (1, 3, 4),
-    (0, 2, 5), (2, 3, 5),
-    (0, 5, 6), (2, 5, 6), (1, 4, 6), (3, 4, 6),
-)
+GATHER_GROUPS = ((0, 2), (2, 6))
+SCATTER_GROUPS = ((0, 1), (1, 3), (3, 6))
 
 
 def tile_moe_two_glu_sigmoid_kernel(
@@ -54,8 +45,10 @@ def tile_moe_two_glu_sigmoid_kernel(
         for name in ("w1", "w3", "w2"):
             planes[name] = keep.tile([P, E, H], U8, name=name + "_plane", align_bytes=64)
         zero = keep.tile([P, 8], F32, name="zero")
+        warm = keep.tile([P, 8], F32, name="warm")
         nc.gpsimd.memset(zero[:], 0.0)
-        gates = keep.tile([P, NT, E * C], F32, name="gates", align_bytes=64)
+        nc.scalar.activation(warm[:, 0:1], zero[:, 0:1], SIGMOID)
+        gates = keep.tile([P, E * C], F32, name="gates", align_bytes=64)
         words = {}
         for name in ("w1", "w3", "w2"):
             words[name] = keep.tile([P, E, 2 * H], U8, name=name + "_words", align_bytes=64)
@@ -63,21 +56,18 @@ def tile_moe_two_glu_sigmoid_kernel(
         windows = [keep.tile([P, T], F32, name="window%d" % t, align_bytes=64) for t in range(NT)]
         identity = keep.tile([P, P], F32, name="identity", align_bytes=64)
 
-        def first_of(groups, e):
-            return [lo for lo, hi in groups if lo <= e < hi][0]
-
-        def load_plane(plane, rows):
-            for r in range(PLANE_ROWS):
+        def load_plane(plane, rows, lo, hi):
+            for r in range(lo, hi):
                 nc.sync.dma_start(plane.bitcast(I32)[r:P:32], rows.bitcast(I32)[r])
 
-        def load_weight_plane(name, scales):
-            load_plane(planes[name][:], scales.rearrange("e s (q r) n -> r q (e s) n", r=PLANE_ROWS))
+        def load_weight_plane(name, scales, lo=0, hi=PLANE_ROWS):
+            load_plane(planes[name][:], scales.rearrange("e s (q r) n -> r q (e s) n", r=PLANE_ROWS), lo, hi)
 
         def load_words(name, dram, lo, hi):
             nc.sync.dma_start(words[name][:, lo:hi, :].bitcast(I32), dram.bitcast(I32)[lo:hi].rearrange("e s p b -> p (e s) b"))
 
         def load_gate(lo, hi):
-            nc.sync.dma_start(gates[:, :, lo * C : hi * C], gate[:, lo * C : hi * C].rearrange("(t p) j -> p t j", p=P))
+            nc.sync.dma_start(gates[:, lo * C : hi * C], gate[0:P, lo * C : hi * C])
 
         nc.vector.memset(x_plane[:].bitcast(I32), 0)
         for name in ("w1", "w3", "w2"):
@@ -86,104 +76,102 @@ def tile_moe_two_glu_sigmoid_kernel(
 
         nc.sync.dma_start(offs_sb[:], offs)
         nc.sync.dma_start(x_sb[:], x_words[0].rearrange("p n t -> p (n t)").bitcast(I32))
-        load_plane(x_plane[:], x_scales.rearrange("o (q r) n -> r q (o n)", r=PLANE_ROWS))
+        load_plane(x_plane[:], x_scales.rearrange("o (q r) n -> r q (o n)", r=PLANE_ROWS), 0, PLANE_ROWS)
         load_words("w1", w1_words, 0, 2)
         load_weight_plane("w1", w1_scales)
-        load_words("w3", w3_words, 0, 3)
+        load_words("w3", w3_words, 0, 2)
         load_weight_plane("w3", w3_scales)
-        load_words("w1", w1_words, 2, 3)
-        nc.sync.dma_start(dst_sb[:], dst)
+        for lo in (2, 4):
+            load_words("w1", w1_words, lo, lo + 2)
+            load_words("w3", w3_words, lo, lo + 2)
         load_weight_plane("w2", w2_scales)
-        load_gate(0, 1)
         load_words("w2", w2_words, 0, 2)
-        load_words("w1", w1_words, 3, E)
-        load_words("w3", w3_words, 3, E)
-        load_gate(1, 3)
+        nc.sync.dma_start(dst_sb[:], dst)
+        load_gate(0, 2)
         load_words("w2", w2_words, 2, E)
-        load_gate(3, E)
+        load_gate(2, E)
 
         slot_words = {}
         slot_scales = {}
 
-        def gather_words(lo, hi, tag):
-            slot_words[lo] = keep.tile([P, (hi - lo) * C], U32, name="slot_words%d" % lo, tag=tag, align_bytes=64)
-            nc.vector.tensor_copy(slot_words[lo][:], x_sb[:].bitcast(U32).indirect(offs_sb[:, lo * LIST_COLS : hi * LIST_COLS]))
+        def gather(into, name, dtype, window, lo, hi, tag):
+            gathered = keep.tile([P, (hi - lo) * C], dtype, name="%s%d" % (name, lo), tag=tag, align_bytes=64)
+            nc.vector.tensor_copy(gathered[:], window.indirect(offs_sb[:, lo * LIST_COLS : hi * LIST_COLS]))
+            for e in range(lo, hi):
+                into[e] = gathered[:, (e - lo) * C : (e - lo + 1) * C]
 
-        def gather_scales(lo, hi):
-            slot_scales[lo] = keep.tile([P, (hi - lo) * C], U8, name="slot_scales%d" % lo, align_bytes=64)
-            nc.vector.tensor_copy(slot_scales[lo][:], x_plane[:].indirect(offs_sb[:, lo * LIST_COLS : hi * LIST_COLS]))
-
-        gather_words(*WORD_GROUPS[0], "slot_words0")
-        for group in SCALE_GROUPS:
-            gather_scales(*group)
-        gather_words(*WORD_GROUPS[1], "x_plane")
+        gather(slot_words, "slot_words", U32, x_sb[:].bitcast(U32), *GATHER_GROUPS[0], "slot_words0")
+        for lo, hi in GATHER_GROUPS:
+            gather(slot_scales, "slot_scales", U8, x_plane[:], lo, hi, "slot_scales%d" % lo)
+        gather(slot_words, "slot_words", U32, x_sb[:].bitcast(U32), *GATHER_GROUPS[1], "x_plane")
 
         banks = [psum.tile([P, NT, C], F32, name="bank%d" % b, bufs=1) for b in range(2)]
         quantised = {}
 
         def first_layer(e):
-            w_lo = first_of(WORD_GROUPS, e)
-            s_lo = first_of(SCALE_GROUPS, e)
-
             pair = psum.tile([P, 2, H], F32, name="pair")
             sums = {"w1": pair[:, 0, :], "w3": pair[:, 1, :]}
             for name in ("w1", "w3"):
                 nc.tensor.matmul_mx(
                     out=sums[name],
-                    lhsT=slot_words[w_lo][:, (e - w_lo) * C : (e - w_lo + 1) * C].bitcast(FP8X4),
-                    lhsT_scale=slot_scales[s_lo][:, (e - s_lo) * C : (e - s_lo + 1) * C],
+                    lhsT=slot_words[e].bitcast(FP8X4),
+                    lhsT_scale=slot_scales[e],
                     rhs=words[name][:, e, :].bitcast(FP4X4),
                     rhs_scale=planes[name][:, e, :],
                     start=True,
                     stop=True,
                 )
-
             sig = ring.tile([P, 2, P, 2], F32, name="sig", align_bytes=64)
             nc.scalar.activation(sig[:], sums["w1"].rearrange("p (q u v) -> p u q v", u=2, v=2), SIGMOID)
             h_t = ring.tile([P, 2, P, 2], BF16, name="h_t", align_bytes=64, bufs=E)
             nc.vector.tensor_tensor(h_t[:], sums["w3"].rearrange("p (q u v) -> p u q v", u=2, v=2), sig[:], MULT)
-
             value_pairs = h_t[:].rearrange("p u q v -> p (u q v)").bitcast(F32)
             turned = banks[e % 2][:, 0:2, :]
             for u in range(2):
                 nc.tensor.transpose(turned[:, u, :], value_pairs[:, u * P : (u + 1) * P], identity[:])
             h = ring.tile([P, 4 * C], BF16, name="h", align_bytes=64)
             nc.scalar.copy(h[:].bitcast(F32).rearrange("p (c u) -> p c u", u=2), turned.rearrange("p u c -> p c u"))
-            h_words = ring.tile([P, C], U32, name="h_words", align_bytes=64)
-            h_scales = ring.tile([P, C], U8, name="h_scales", align_bytes=64)
+            h_words = ring.tile([P, C], U32, name="h_words", align_bytes=64, bufs=E)
+            h_scales = ring.tile([P, C], U8, name="h_scales", align_bytes=64, bufs=E)
             nc.vector.quantize_mx(out=h_words[:].bitcast(FP8X4), scales=h_scales[:], in_=h[:])
             quantised[e] = (h_words, h_scales)
 
-        def second_layer(e):
+        def product(y, e, t):
             h_words, h_scales = quantised[e]
-            y = banks[(e + 1) % 2]
-            early = banks[0][:, 0, :]
-            for t in range(NT):
-                nc.tensor.matmul_mx(
-                    out=early if (e, t) == (0, 0) else y[:, t, :],
-                    lhsT=words["w2"][:, e, 2 * P * t : 2 * P * (t + 1)].bitcast(FP4X4),
-                    lhsT_scale=planes["w2"][:, e, P * t : P * (t + 1)],
-                    rhs=h_words[:].bitcast(FP8X4),
-                    rhs_scale=h_scales[:],
-                    start=True,
-                    stop=True,
-                )
-            t0 = 1 if e == 0 else 0
-            if e == 0:
-                nc.scalar.copy(results[:, 0, 0:C], early)
-            nc.scalar.copy(results[:, t0:NT, e * C : (e + 1) * C], y[:, t0:NT, :])
+            nc.tensor.matmul_mx(
+                out=y,
+                lhsT=words["w2"][:, e, 2 * P * t : 2 * P * (t + 1)].bitcast(FP4X4),
+                lhsT_scale=planes["w2"][:, e, P * t : P * (t + 1)],
+                rhs=h_words[:].bitcast(FP8X4),
+                rhs_scale=h_scales[:],
+                start=True,
+                stop=True,
+            )
 
-        first_layer(0)
-        for e in range(E):
-            if e + 1 < E:
-                first_layer(e + 1)
-            second_layer(e)
+        def second_layer(e, bank, cuts):
+            for t in range(NT):
+                product(bank[:, t, :], e, t)
+            for lo, hi in cuts:
+                nc.scalar.copy(results[:, lo:hi, e * C : (e + 1) * C], bank[:, lo:hi, :])
+
+        def scatter(lo, hi):
+            for t in range(NT):
+                entries = dst_sb[:, lo * LIST_COLS : hi * LIST_COLS]
+                cols = slice(lo * C, hi * C)
+                nc.vector.tensor_tensor(windows[t][:].indirect(entries), results[:, t, cols], gates[:, cols], MULT)
+                if hi == E:
+                    nc.sync.dma_start(out[t * P : (t + 1) * P, :], windows[t][:])
 
         for t in range(NT):
             nc.scalar.copy(windows[t][:], zero[:, 0:1].to_broadcast([P, T]))
-        for t, lo, hi in SCATTERS:
-            entries = dst_sb[:, lo * LIST_COLS : hi * LIST_COLS]
-            cols = slice(lo * C, hi * C)
-            nc.vector.tensor_tensor(windows[t][:].indirect(entries), results[:, t, cols], gates[:, t, cols], MULT)
-        for t in range(NT):
-            nc.sync.dma_start(out[t * P : (t + 1) * P, :], windows[t][:])
+
+        for e in range(E):
+            first_layer(e)
+            if e == 2:
+                second_layer(0, banks[1], ((0, 1), (1, NT)))
+            if e == 3:
+                second_layer(1, banks[0], ((0, NT),))
+        for e in range(2, E):
+            second_layer(e, banks[e % 2], ((0, NT),))
+        for lo, hi in SCATTER_GROUPS:
+            scatter(lo, hi)

@@ -46,6 +46,7 @@ def tile_moe_two_glu_sigmoid_kernel(
             planes[name] = keep.tile([P, E, H], U8, name=name + "_plane", align_bytes=64)
         zero = keep.tile([P, 8], F32, name="zero")
         warm = keep.tile([P, 8], F32, name="warm")
+        nc.gpsimd.memset(x_plane[:].bitcast(I32), 0)
         nc.gpsimd.memset(zero[:], 0.0)
         nc.scalar.activation(warm[:, 0:1], zero[:, 0:1], SIGMOID)
         gates = keep.tile([P, E * C], F32, name="gates", align_bytes=64)
@@ -69,7 +70,6 @@ def tile_moe_two_glu_sigmoid_kernel(
         def load_gate(lo, hi):
             nc.sync.dma_start(gates[:, lo * C : hi * C], gate[0:P, lo * C : hi * C])
 
-        nc.vector.memset(x_plane[:].bitcast(I32), 0)
         for name in ("w1", "w3", "w2"):
             nc.vector.memset(planes[name][:].bitcast(I32), 0)
         make_identity(nc, identity[:])
@@ -109,8 +109,7 @@ def tile_moe_two_glu_sigmoid_kernel(
         quantised = {}
 
         def first_layer(e):
-            pair = psum.tile([P, 2, H], F32, name="pair")
-            sums = {"w1": pair[:, 0, :], "w3": pair[:, 1, :]}
+            sums = {name: psum.tile([P, H], F32, name="sum_" + name)[:] for name in ("w1", "w3")}
             for name in ("w1", "w3"):
                 nc.tensor.matmul_mx(
                     out=sums[name],

@@ -21,11 +21,11 @@ P = 128
 NT = N // P
 LIST_COLS = C // 16
 PLANE_ROWS = 4
+HALF = E // 2
 PAIR_BUFS = 3
 RING_BUFS = 3
 
 GATHER_GROUPS = ((0, 2), (2, 6))
-SCATTER_GROUPS = ((0, 1), (1, 3), (3, 6))
 
 
 def tile_moe_two_glu_sigmoid_kernel(
@@ -43,7 +43,8 @@ def tile_moe_two_glu_sigmoid_kernel(
         x_plane = keep.tile([P, T], U8, name="x_plane", tag="x_plane", align_bytes=64)
         planes = {}
         for name in ("w1", "w3", "w2"):
-            planes[name] = keep.tile([P, E, H], U8, name=name + "_plane", align_bytes=64)
+            for half in range(2):
+                planes[name, half] = keep.tile([P, HALF, H], U8, name="%s_plane%d" % (name, half), align_bytes=64)
         zero = keep.tile([P, 8], F32, name="zero")
         warm = keep.tile([P, 8], F32, name="warm")
         nc.gpsimd.memset(x_plane[:].bitcast(I32), 0)
@@ -57,12 +58,13 @@ def tile_moe_two_glu_sigmoid_kernel(
         windows = [keep.tile([P, T], F32, name="window%d" % t, align_bytes=64) for t in range(NT)]
         identity = keep.tile([P, P], F32, name="identity", align_bytes=64)
 
-        def load_plane(plane, rows, lo, hi):
-            for r in range(lo, hi):
-                nc.sync.dma_start(plane.bitcast(I32)[r:P:32], rows.bitcast(I32)[r])
+        def load_plane(plane, rows):
+            for r in range(PLANE_ROWS):
+                nc.sync.dma_start(plane[r:P:32], rows[r])
 
-        def load_weight_plane(name, scales, lo=0, hi=PLANE_ROWS):
-            load_plane(planes[name][:], scales.rearrange("e s (q r) n -> r q (e s) n", r=PLANE_ROWS), lo, hi)
+        def load_weight_plane(name, scales, half):
+            rows = scales.bitcast(I32)[half * HALF : (half + 1) * HALF].rearrange("e s (q r) n -> r q (e s) n", r=PLANE_ROWS)
+            load_plane(planes[name, half][:].bitcast(I32), rows)
 
         def load_words(name, dram, lo, hi):
             nc.sync.dma_start(words[name][:, lo:hi, :].bitcast(I32), dram.bitcast(I32)[lo:hi].rearrange("e s p b -> p (e s) b"))
@@ -70,45 +72,54 @@ def tile_moe_two_glu_sigmoid_kernel(
         def load_gate(lo, hi):
             nc.sync.dma_start(gates[:, lo * C : hi * C], gate[0:P, lo * C : hi * C])
 
-        for name in ("w1", "w3", "w2"):
-            nc.vector.memset(planes[name][:].bitcast(I32), 0)
+        for half in range(2):
+            for name in ("w1", "w3", "w2"):
+                nc.vector.memset(planes[name, half][:].bitcast(I32), 0)
         make_identity(nc, identity[:])
 
         nc.sync.dma_start(offs_sb[:], offs)
+        load_plane(x_plane[:].bitcast(I32), x_scales.bitcast(I32).rearrange("o (q r) n -> r q (o n)", r=PLANE_ROWS))
         nc.sync.dma_start(x_sb[:], x_words[0].rearrange("p n t -> p (n t)").bitcast(I32))
-        load_plane(x_plane[:], x_scales.rearrange("o (q r) n -> r q (o n)", r=PLANE_ROWS), 0, PLANE_ROWS)
+        load_weight_plane("w1", w1_scales, 0)
         load_words("w1", w1_words, 0, 2)
-        load_weight_plane("w1", w1_scales)
         load_words("w3", w3_words, 0, 2)
-        load_weight_plane("w3", w3_scales)
-        for lo in (2, 4):
-            load_words("w1", w1_words, lo, lo + 2)
-            load_words("w3", w3_words, lo, lo + 2)
-        load_weight_plane("w2", w2_scales)
+        load_weight_plane("w3", w3_scales, 0)
+        load_words("w1", w1_words, 2, 3)
+        load_words("w3", w3_words, 2, 3)
+        load_weight_plane("w2", w2_scales, 0)
         load_words("w2", w2_words, 0, 2)
-        nc.sync.dma_start(dst_sb[:], dst)
         load_gate(0, 2)
+        nc.sync.dma_start(dst_sb[:], dst)
+        load_weight_plane("w1", w1_scales, 1)
+        load_words("w1", w1_words, 3, 4)
+        load_weight_plane("w3", w3_scales, 1)
+        load_words("w3", w3_words, 3, 4)
+        load_words("w1", w1_words, 4, E)
+        load_words("w3", w3_words, 4, E)
         load_words("w2", w2_words, 2, E)
         load_gate(2, E)
+        load_weight_plane("w2", w2_scales, 1)
 
         slot_words = {}
         slot_scales = {}
 
-        def gather(into, name, dtype, window, lo, hi, tag):
-            gathered = keep.tile([P, (hi - lo) * C], dtype, name="%s%d" % (name, lo), tag=tag, align_bytes=64)
+        def gather(into, name, dtype, window, lo, hi):
+            gathered = keep.tile([P, (hi - lo) * C], dtype, name="%s%d" % (name, lo), align_bytes=64)
             nc.vector.tensor_copy(gathered[:], window.indirect(offs_sb[:, lo * LIST_COLS : hi * LIST_COLS]))
             for e in range(lo, hi):
                 into[e] = gathered[:, (e - lo) * C : (e - lo + 1) * C]
 
-        gather(slot_words, "slot_words", U32, x_sb[:].bitcast(U32), *GATHER_GROUPS[0], "slot_words0")
+        gather(slot_scales, "slot_scales", U8, x_plane[:], 0, E)
         for lo, hi in GATHER_GROUPS:
-            gather(slot_scales, "slot_scales", U8, x_plane[:], lo, hi, "slot_scales%d" % lo)
-        gather(slot_words, "slot_words", U32, x_sb[:].bitcast(U32), *GATHER_GROUPS[1], "x_plane")
+            gather(slot_words, "slot_words", U32, x_sb[:].bitcast(U32), lo, hi)
+
+        for t in range(NT):
+            nc.scalar.copy(windows[t][:], zero[:, 0:1].to_broadcast([P, T]))
 
         banks = [psum.tile([P, NT, C], F32, name="bank%d" % b, bufs=1) for b in range(2)]
         quantised = {}
 
-        def first_layer(e):
+        def first_layer(e, h, on_gpsimd):
             sums = {name: psum.tile([P, H], F32, name="sum_" + name)[:] for name in ("w1", "w3")}
             for name in ("w1", "w3"):
                 nc.tensor.matmul_mx(
@@ -116,61 +127,94 @@ def tile_moe_two_glu_sigmoid_kernel(
                     lhsT=slot_words[e].bitcast(FP8X4),
                     lhsT_scale=slot_scales[e],
                     rhs=words[name][:, e, :].bitcast(FP4X4),
-                    rhs_scale=planes[name][:, e, :],
+                    rhs_scale=planes[name, e // HALF][:, e % HALF, :],
                     start=True,
                     stop=True,
                 )
             sig = ring.tile([P, 2, P, 2], F32, name="sig", align_bytes=64)
             nc.scalar.activation(sig[:], sums["w1"].rearrange("p (q u v) -> p u q v", u=2, v=2), SIGMOID)
             h_t = ring.tile([P, 2, P, 2], BF16, name="h_t", align_bytes=64, bufs=E)
-            nc.vector.tensor_tensor(h_t[:], sums["w3"].rearrange("p (q u v) -> p u q v", u=2, v=2), sig[:], MULT)
+            b = sums["w3"].rearrange("p (q u v) -> p u q v", u=2, v=2)
+            if on_gpsimd:
+                b_sb = ring.tile([P, 2, P, 2], F32, name="b_sb", align_bytes=64)
+                nc.scalar.copy(b_sb[:], b)
+                nc.gpsimd.tensor_tensor(h_t[:], b_sb[:], sig[:], MULT)
+            else:
+                nc.vector.tensor_tensor(h_t[:], b, sig[:], MULT)
             value_pairs = h_t[:].rearrange("p u q v -> p (u q v)").bitcast(F32)
             turned = banks[e % 2][:, 0:2, :]
             for u in range(2):
                 nc.tensor.transpose(turned[:, u, :], value_pairs[:, u * P : (u + 1) * P], identity[:])
-            h = ring.tile([P, 4 * C], BF16, name="h", align_bytes=64)
-            nc.scalar.copy(h[:].bitcast(F32).rearrange("p (c u) -> p c u", u=2), turned.rearrange("p u c -> p c u"))
-            h_words = ring.tile([P, C], U32, name="h_words", align_bytes=64, bufs=E)
-            h_scales = ring.tile([P, C], U8, name="h_scales", align_bytes=64, bufs=E)
-            nc.vector.quantize_mx(out=h_words[:].bitcast(FP8X4), scales=h_scales[:], in_=h[:])
-            quantised[e] = (h_words, h_scales)
+            nc.scalar.copy(h.bitcast(F32).rearrange("p (c u) -> p c u", u=2), turned.rearrange("p u c -> p c u"))
 
-        def product(y, e, t):
+        def quantise(h, experts):
+            h_words = keep.tile([P, len(experts) * C], U32, name="h_words%d" % experts[0], align_bytes=64)
+            h_scales = keep.tile([P, len(experts) * C], U8, name="h_scales%d" % experts[0], align_bytes=64)
+            nc.vector.quantize_mx(out=h_words[:].bitcast(FP8X4), scales=h_scales[:], in_=h)
+            for j, e in enumerate(experts):
+                quantised[e] = (h_words[:, j * C : (j + 1) * C], h_scales[:, j * C : (j + 1) * C])
+
+        def products(e, bank, lo, hi):
             h_words, h_scales = quantised[e]
-            nc.tensor.matmul_mx(
-                out=y,
-                lhsT=words["w2"][:, e, 2 * P * t : 2 * P * (t + 1)].bitcast(FP4X4),
-                lhsT_scale=planes["w2"][:, e, P * t : P * (t + 1)],
-                rhs=h_words[:].bitcast(FP8X4),
-                rhs_scale=h_scales[:],
-                start=True,
-                stop=True,
-            )
+            for t in range(lo, hi):
+                nc.tensor.matmul_mx(
+                    out=bank[:, t, :],
+                    lhsT=words["w2"][:, e, 2 * P * t : 2 * P * (t + 1)].bitcast(FP4X4),
+                    lhsT_scale=planes["w2", e // HALF][:, e % HALF, P * t : P * (t + 1)],
+                    rhs=h_words.bitcast(FP8X4),
+                    rhs_scale=h_scales,
+                    start=True,
+                    stop=True,
+                )
 
-        def second_layer(e, bank, cuts):
-            for t in range(NT):
-                product(bank[:, t, :], e, t)
-            for lo, hi in cuts:
-                nc.scalar.copy(results[:, lo:hi, e * C : (e + 1) * C], bank[:, lo:hi, :])
+        def second_layer(e, bank, lo, hi):
+            products(e, bank, lo, hi)
+            nc.scalar.copy(results[:, lo:hi, e * C : (e + 1) * C], bank[:, lo:hi, :])
 
-        def scatter(lo, hi):
-            for t in range(NT):
-                entries = dst_sb[:, lo * LIST_COLS : hi * LIST_COLS]
-                cols = slice(lo * C, hi * C)
-                nc.vector.tensor_tensor(windows[t][:].indirect(entries), results[:, t, cols], gates[:, cols], MULT)
-                if hi == E:
-                    nc.sync.dma_start(out[t * P : (t + 1) * P, :], windows[t][:])
+        def gate_of(e, n):
+            return gates[:, e * C : (e + 1) * C].unsqueeze(1).to_broadcast([P, n, C])
+
+        def scatter_gated(t, e, values):
+            nc.vector.tensor_copy(windows[t][:].indirect(dst_sb[:, e * LIST_COLS : (e + 1) * LIST_COLS]), values)
+
+        def scatter(t, lo, hi):
+            entries = dst_sb[:, lo * LIST_COLS : hi * LIST_COLS]
+            cols = slice(lo * C, hi * C)
+            nc.vector.tensor_tensor(windows[t][:].indirect(entries), results[:, t, cols], gates[:, cols], MULT)
+            if hi == E:
+                nc.sync.dma_start(out[t * P : (t + 1) * P, :], windows[t][:])
+
+        for e in range(3):
+            h = keep.tile([P, 4 * C], BF16, name="h%d" % e, tag="h%d" % e, align_bytes=64)
+            first_layer(e, h[:], False)
+            quantise(h[:], (e,))
+        gated0 = keep.tile([P, NT, C], F32, name="gated0", align_bytes=64)
+        products(0, banks[1], 0, NT)
+        nc.vector.tensor_tensor(gated0[:], banks[1][:], gate_of(0, NT), MULT)
+        second_layer(1, banks[0], 0, NT)
+        gated1 = []
+        for half in range(2):
+            gated = keep.tile([P, 2, C], F32, name="gated1%d" % half, tag="h%d" % (2 - half), align_bytes=64)
+            nc.gpsimd.tensor_tensor(gated[:], results[:, 2 * half : 2 * half + 2, C : 2 * C], gate_of(1, 2), MULT)
+            gated1.extend([gated[:, 0, :], gated[:, 1, :]])
+
+        h35 = keep.tile([P, 2 * 4 * C], BF16, name="h35", align_bytes=64)
+        h4 = keep.tile([P, 4 * C], BF16, name="h4", align_bytes=64)
+        first_layer(3, h35[:, 0 : 4 * C], True)
+        second_layer(2, banks[0], 0, 2)
+        first_layer(4, h4[:], True)
+        first_layer(5, h35[:, 4 * C : 8 * C], True)
+        quantise(h4[:], (4,))
+        quantise(h35[:], (3, 5))
+        second_layer(2, banks[1], 2, NT)
+        for e in range(3, E):
+            second_layer(e, banks[(e + 1) % 2], 0, NT)
 
         for t in range(NT):
-            nc.scalar.copy(windows[t][:], zero[:, 0:1].to_broadcast([P, T]))
-
-        for e in range(E):
-            first_layer(e)
-            if e == 2:
-                second_layer(0, banks[1], ((0, 1), (1, NT)))
-            if e == 3:
-                second_layer(1, banks[0], ((0, NT),))
-        for e in range(2, E):
-            second_layer(e, banks[e % 2], ((0, NT),))
-        for lo, hi in SCATTER_GROUPS:
-            scatter(lo, hi)
+            scatter_gated(t, 0, gated0[:, t, :])
+        for t in range(NT):
+            scatter_gated(t, 1, gated1[t])
+        for t in range(NT):
+            scatter(t, 2, 3)
+        for t, lo, hi in ((0, 3, 4), (1, 3, 4), (2, 3, E), (3, 3, E), (0, 4, E), (1, 4, E)):
+            scatter(t, lo, hi)

@@ -78,40 +78,38 @@ def tile_moe_two_glu_sigmoid_kernel(
         make_identity(nc, identity[:])
 
         nc.sync.dma_start(offs_sb[:], offs)
-        load_plane(x_plane[:].bitcast(I32), x_scales.bitcast(I32).rearrange("o (q r) n -> r q (o n)", r=PLANE_ROWS))
         nc.sync.dma_start(x_sb[:], x_words[0].rearrange("p n t -> p (n t)").bitcast(I32))
-        load_weight_plane("w1", w1_scales, 0)
+        load_plane(x_plane[:].bitcast(I32), x_scales.bitcast(I32).rearrange("o (q r) n -> r q (o n)", r=PLANE_ROWS))
         load_words("w1", w1_words, 0, 2)
+        load_weight_plane("w1", w1_scales, 0)
         load_words("w3", w3_words, 0, 2)
         load_weight_plane("w3", w3_scales, 0)
-        load_words("w1", w1_words, 2, 3)
-        load_words("w3", w3_words, 2, 3)
+        load_words("w1", w1_words, 2, HALF)
+        load_words("w3", w3_words, 2, HALF)
         load_weight_plane("w2", w2_scales, 0)
         load_words("w2", w2_words, 0, 2)
-        load_gate(0, 2)
         nc.sync.dma_start(dst_sb[:], dst)
-        load_weight_plane("w1", w1_scales, 1)
-        load_words("w1", w1_words, 3, 4)
-        load_weight_plane("w3", w3_scales, 1)
-        load_words("w3", w3_words, 3, 4)
-        load_words("w1", w1_words, 4, E)
-        load_words("w3", w3_words, 4, E)
+        load_gate(0, 1)
+        for name, dram, scales in (("w1", w1_words, w1_scales), ("w3", w3_words, w3_scales)):
+            load_weight_plane(name, scales, 1)
+            load_words(name, dram, HALF, E)
         load_words("w2", w2_words, 2, E)
-        load_gate(2, E)
+        load_gate(1, E)
         load_weight_plane("w2", w2_scales, 1)
 
         slot_words = {}
         slot_scales = {}
 
-        def gather(into, name, dtype, window, lo, hi):
-            gathered = keep.tile([P, (hi - lo) * C], dtype, name="%s%d" % (name, lo), align_bytes=64)
+        def gather(into, name, dtype, window, lo, hi, tag):
+            gathered = keep.tile([P, (hi - lo) * C], dtype, name="%s%d" % (name, lo), tag=tag, align_bytes=64)
             nc.vector.tensor_copy(gathered[:], window.indirect(offs_sb[:, lo * LIST_COLS : hi * LIST_COLS]))
             for e in range(lo, hi):
                 into[e] = gathered[:, (e - lo) * C : (e - lo + 1) * C]
 
-        gather(slot_scales, "slot_scales", U8, x_plane[:], 0, E)
+        gather(slot_words, "slot_words", U32, x_sb[:].bitcast(U32), *GATHER_GROUPS[0], "slot_words0")
         for lo, hi in GATHER_GROUPS:
-            gather(slot_words, "slot_words", U32, x_sb[:].bitcast(U32), lo, hi)
+            gather(slot_scales, "slot_scales", U8, x_plane[:], lo, hi, "slot_scales%d" % lo)
+        gather(slot_words, "slot_words", U32, x_sb[:].bitcast(U32), *GATHER_GROUPS[1], "x_plane")
 
         for t in range(NT):
             nc.scalar.copy(windows[t][:], zero[:, 0:1].to_broadcast([P, T]))
@@ -119,7 +117,7 @@ def tile_moe_two_glu_sigmoid_kernel(
         banks = [psum.tile([P, NT, C], F32, name="bank%d" % b, bufs=1) for b in range(2)]
         quantised = {}
 
-        def first_layer(e, h, on_gpsimd):
+        def first_layer(e, bank):
             sums = {name: psum.tile([P, H], F32, name="sum_" + name)[:] for name in ("w1", "w3")}
             for name in ("w1", "w3"):
                 nc.tensor.matmul_mx(
@@ -134,25 +132,17 @@ def tile_moe_two_glu_sigmoid_kernel(
             sig = ring.tile([P, 2, P, 2], F32, name="sig", align_bytes=64)
             nc.scalar.activation(sig[:], sums["w1"].rearrange("p (q u v) -> p u q v", u=2, v=2), SIGMOID)
             h_t = ring.tile([P, 2, P, 2], BF16, name="h_t", align_bytes=64, bufs=E)
-            b = sums["w3"].rearrange("p (q u v) -> p u q v", u=2, v=2)
-            if on_gpsimd:
-                b_sb = ring.tile([P, 2, P, 2], F32, name="b_sb", align_bytes=64)
-                nc.scalar.copy(b_sb[:], b)
-                nc.gpsimd.tensor_tensor(h_t[:], b_sb[:], sig[:], MULT)
-            else:
-                nc.vector.tensor_tensor(h_t[:], b, sig[:], MULT)
+            nc.vector.tensor_tensor(h_t[:], sums["w3"].rearrange("p (q u v) -> p u q v", u=2, v=2), sig[:], MULT)
             value_pairs = h_t[:].rearrange("p u q v -> p (u q v)").bitcast(F32)
-            turned = banks[e % 2][:, 0:2, :]
+            turned = bank[:, 0:2, :]
             for u in range(2):
                 nc.tensor.transpose(turned[:, u, :], value_pairs[:, u * P : (u + 1) * P], identity[:])
-            nc.scalar.copy(h.bitcast(F32).rearrange("p (c u) -> p c u", u=2), turned.rearrange("p u c -> p c u"))
-
-        def quantise(h, experts):
-            h_words = keep.tile([P, len(experts) * C], U32, name="h_words%d" % experts[0], align_bytes=64)
-            h_scales = keep.tile([P, len(experts) * C], U8, name="h_scales%d" % experts[0], align_bytes=64)
-            nc.vector.quantize_mx(out=h_words[:].bitcast(FP8X4), scales=h_scales[:], in_=h)
-            for j, e in enumerate(experts):
-                quantised[e] = (h_words[:, j * C : (j + 1) * C], h_scales[:, j * C : (j + 1) * C])
+            h = ring.tile([P, 4 * C], BF16, name="h", align_bytes=64)
+            nc.scalar.copy(h[:].bitcast(F32).rearrange("p (c u) -> p c u", u=2), turned.rearrange("p u c -> p c u"))
+            h_words = ring.tile([P, C], U32, name="h_words", align_bytes=64, bufs=E)
+            h_scales = ring.tile([P, C], U8, name="h_scales", align_bytes=64, bufs=E)
+            nc.vector.quantize_mx(out=h_words[:].bitcast(FP8X4), scales=h_scales[:], in_=h[:])
+            quantised[e] = (h_words[:], h_scales[:])
 
         def products(e, bank, lo, hi):
             h_words, h_scales = quantised[e]
@@ -167,15 +157,10 @@ def tile_moe_two_glu_sigmoid_kernel(
                     stop=True,
                 )
 
-        def second_layer(e, bank, lo, hi):
-            products(e, bank, lo, hi)
-            nc.scalar.copy(results[:, lo:hi, e * C : (e + 1) * C], bank[:, lo:hi, :])
-
-        def gate_of(e, n):
-            return gates[:, e * C : (e + 1) * C].unsqueeze(1).to_broadcast([P, n, C])
-
-        def scatter_gated(t, e, values):
-            nc.vector.tensor_copy(windows[t][:].indirect(dst_sb[:, e * LIST_COLS : (e + 1) * LIST_COLS]), values)
+        def second_layer(e, bank, cuts):
+            products(e, bank, cuts[0], cuts[-1])
+            for lo, hi in zip(cuts, cuts[1:]):
+                nc.scalar.copy(results[:, lo:hi, e * C : (e + 1) * C], bank[:, lo:hi, :])
 
         def scatter(t, lo, hi):
             entries = dst_sb[:, lo * LIST_COLS : hi * LIST_COLS]
@@ -184,37 +169,12 @@ def tile_moe_two_glu_sigmoid_kernel(
             if hi == E:
                 nc.sync.dma_start(out[t * P : (t + 1) * P, :], windows[t][:])
 
-        for e in range(3):
-            h = keep.tile([P, 4 * C], BF16, name="h%d" % e, tag="h%d" % e, align_bytes=64)
-            first_layer(e, h[:], False)
-            quantise(h[:], (e,))
-        gated0 = keep.tile([P, NT, C], F32, name="gated0", align_bytes=64)
-        products(0, banks[1], 0, NT)
-        nc.vector.tensor_tensor(gated0[:], banks[1][:], gate_of(0, NT), MULT)
-        second_layer(1, banks[0], 0, NT)
-        gated1 = []
-        for half in range(2):
-            gated = keep.tile([P, 2, C], F32, name="gated1%d" % half, tag="h%d" % (2 - half), align_bytes=64)
-            nc.gpsimd.tensor_tensor(gated[:], results[:, 2 * half : 2 * half + 2, C : 2 * C], gate_of(1, 2), MULT)
-            gated1.extend([gated[:, 0, :], gated[:, 1, :]])
+        steps = [(first_layer, 0), (first_layer, 1), (first_layer, 2), (second_layer, 0, (0, 1, NT)), (second_layer, 1, (0, NT))]
+        steps.extend([(first_layer, 3), (second_layer, 2, (0, 2)), (first_layer, 4), (first_layer, 5), (second_layer, 2, (2, NT))])
+        steps.extend([(second_layer, e, (0, NT)) for e in range(HALF, E)])
+        for i, step in enumerate(steps):
+            step[0](step[1], banks[i % 2], *step[2:])
 
-        h35 = keep.tile([P, 2 * 4 * C], BF16, name="h35", align_bytes=64)
-        h4 = keep.tile([P, 4 * C], BF16, name="h4", align_bytes=64)
-        first_layer(3, h35[:, 0 : 4 * C], True)
-        second_layer(2, banks[0], 0, 2)
-        first_layer(4, h4[:], True)
-        first_layer(5, h35[:, 4 * C : 8 * C], True)
-        quantise(h4[:], (4,))
-        quantise(h35[:], (3, 5))
-        second_layer(2, banks[1], 2, NT)
-        for e in range(3, E):
-            second_layer(e, banks[(e + 1) % 2], 0, NT)
-
-        for t in range(NT):
-            scatter_gated(t, 0, gated0[:, t, :])
-        for t in range(NT):
-            scatter_gated(t, 1, gated1[t])
-        for t in range(NT):
-            scatter(t, 2, 3)
-        for t, lo, hi in ((0, 3, 4), (1, 3, 4), (2, 3, E), (3, 3, E), (0, 4, E), (1, 4, E)):
-            scatter(t, lo, hi)
+        for lo, hi in ((0, 1), (1, HALF), (HALF, E)):
+            for t in range(NT):
+                scatter(t, lo, hi)

@@ -58,13 +58,13 @@ def tile_moe_two_glu_sigmoid_kernel(
         windows = [keep.tile([P, T], F32, name="window%d" % t, align_bytes=64) for t in range(NT)]
         identity = keep.tile([P, P], F32, name="identity", align_bytes=64)
 
-        def load_plane(plane, rows):
-            for r in range(PLANE_ROWS):
+        def load_plane(plane, rows, lo=0, hi=PLANE_ROWS):
+            for r in range(lo, hi):
                 nc.sync.dma_start(plane[r:P:32], rows[r])
 
-        def load_weight_plane(name, scales, half):
+        def load_weight_plane(name, scales, half, lo=0, hi=PLANE_ROWS):
             rows = scales.bitcast(I32)[half * HALF : (half + 1) * HALF].rearrange("e s (q r) n -> r q (e s) n", r=PLANE_ROWS)
-            load_plane(planes[name, half][:].bitcast(I32), rows)
+            load_plane(planes[name, half][:].bitcast(I32), rows, lo, hi)
 
         def load_words(name, dram, lo, hi):
             nc.sync.dma_start(words[name][:, lo:hi, :].bitcast(I32), dram.bitcast(I32)[lo:hi].rearrange("e s p b -> p (e s) b"))
@@ -77,16 +77,16 @@ def tile_moe_two_glu_sigmoid_kernel(
                 nc.vector.memset(planes[name, half][:].bitcast(I32), 0)
         make_identity(nc, identity[:])
 
-        nc.sync.dma_start(offs_sb[:], offs)
         nc.sync.dma_start(x_sb[:], x_words[0].rearrange("p n t -> p (n t)").bitcast(I32))
+        nc.sync.dma_start(offs_sb[:], offs)
         load_plane(x_plane[:].bitcast(I32), x_scales.bitcast(I32).rearrange("o (q r) n -> r q (o n)", r=PLANE_ROWS))
         load_words("w1", w1_words, 0, 2)
         load_weight_plane("w1", w1_scales, 0)
         load_words("w3", w3_words, 0, 2)
         load_weight_plane("w3", w3_scales, 0)
         load_words("w1", w1_words, 2, HALF)
-        load_words("w3", w3_words, 2, HALF)
         load_weight_plane("w2", w2_scales, 0)
+        load_words("w3", w3_words, 2, HALF)
         load_words("w2", w2_words, 0, 2)
         nc.sync.dma_start(dst_sb[:], dst)
         load_gate(0, 1)
@@ -169,7 +169,8 @@ def tile_moe_two_glu_sigmoid_kernel(
             if hi == E:
                 nc.sync.dma_start(out[t * P : (t + 1) * P, :], windows[t][:])
 
-        steps = [(first_layer, 0), (first_layer, 1), (first_layer, 2), (second_layer, 0, (0, 1, NT)), (second_layer, 1, (0, NT))]
+        steps = [(first_layer, 0), (first_layer, 1), (second_layer, 0, (0, 1)), (second_layer, 0, (1, NT))]
+        steps.extend([(first_layer, 2), (second_layer, 1, (0, NT))])
         steps.extend([(first_layer, 3), (second_layer, 2, (0, 2)), (first_layer, 4), (first_layer, 5), (second_layer, 2, (2, NT))])
         steps.extend([(second_layer, e, (0, NT)) for e in range(HALF, E)])
         for i, step in enumerate(steps):

@@ -16,6 +16,7 @@ FP8X4 = mybir.dt.float8_e4m3fn_x4
 FP4X4 = mybir.dt.float4_e2m1fn_x4
 MULT = mybir.AluOpType.mult
 SIGMOID = mybir.ActivationFunctionType.Sigmoid
+COPY = mybir.ActivationFunctionType.Copy
 
 P = 128
 NT = N // P
@@ -50,7 +51,8 @@ def tile_moe_two_glu_sigmoid_kernel(
         nc.gpsimd.memset(x_plane[:].bitcast(I32), 0)
         nc.gpsimd.memset(zero[:], 0.0)
         nc.scalar.activation(warm[:, 0:1], zero[:, 0:1], SIGMOID)
-        gates = keep.tile([P, E * C], F32, name="gates", align_bytes=64)
+        gates = keep.tile([P, C], F32, name="gates", align_bytes=64)
+        slot_gates = keep.tile([P, E], F32, name="slot_gates", align_bytes=64)
         words = {}
         for name in ("w1", "w3", "w2"):
             words[name] = keep.tile([P, E, 2 * H], U8, name=name + "_words", align_bytes=64)
@@ -69,9 +71,6 @@ def tile_moe_two_glu_sigmoid_kernel(
         def load_words(name, dram, lo, hi):
             nc.sync.dma_start(words[name][:, lo:hi, :].bitcast(I32), dram.bitcast(I32)[lo:hi].rearrange("e s p b -> p (e s) b"))
 
-        def load_gate(lo, hi):
-            nc.sync.dma_start(gates[:, lo * C : hi * C], gate[0:P, lo * C : hi * C])
-
         for half in range(2):
             for name in ("w1", "w3", "w2"):
                 nc.vector.memset(planes[name, half][:].bitcast(I32), 0)
@@ -89,12 +88,13 @@ def tile_moe_two_glu_sigmoid_kernel(
         load_words("w3", w3_words, 2, HALF)
         load_words("w2", w2_words, 0, 2)
         nc.sync.dma_start(dst_sb[:], dst)
-        load_gate(0, 1)
+        nc.sync.dma_start(gates[:], gate[0:P, 0:C])
+        with nc.allow_non_contiguous_dma(reason="one gate value a slot, slots on the partitions"):
+            nc.sync.dma_start(slot_gates[:, 1:E], gate[0, C:].rearrange("(e c) -> c e", c=C))
         for name, dram, scales in (("w1", w1_words, w1_scales), ("w3", w3_words, w3_scales)):
             load_weight_plane(name, scales, 1)
             load_words(name, dram, HALF, E)
         load_words("w2", w2_words, 2, E)
-        load_gate(1, E)
         load_weight_plane("w2", w2_scales, 1)
 
         slot_words = {}
@@ -115,10 +115,15 @@ def tile_moe_two_glu_sigmoid_kernel(
             nc.scalar.copy(windows[t][:], zero[:, 0:1].to_broadcast([P, T]))
 
         banks = [psum.tile([P, NT, C], F32, name="bank%d" % b, bufs=1) for b in range(2)]
+        pairs = {}
+        for name in ("w1", "w3"):
+            pairs[name] = [psum.tile([P, NT, C], F32, name="sum_%s_%d" % (name, b), bufs=1) for b in range(PAIR_BUFS)]
         quantised = {}
 
-        def first_layer(e, bank):
-            sums = {name: psum.tile([P, H], F32, name="sum_" + name)[:] for name in ("w1", "w3")}
+        hidden = {}
+
+        def first_layer(e):
+            sums = {name: pairs[name][e % PAIR_BUFS][:].rearrange("p t c -> p (t c)") for name in ("w1", "w3")}
             for name in ("w1", "w3"):
                 nc.tensor.matmul_mx(
                     out=sums[name],
@@ -131,9 +136,11 @@ def tile_moe_two_glu_sigmoid_kernel(
                 )
             sig = ring.tile([P, 2, P, 2], F32, name="sig", align_bytes=64)
             nc.scalar.activation(sig[:], sums["w1"].rearrange("p (q u v) -> p u q v", u=2, v=2), SIGMOID)
-            h_t = ring.tile([P, 2, P, 2], BF16, name="h_t", align_bytes=64, bufs=E)
-            nc.vector.tensor_tensor(h_t[:], sums["w3"].rearrange("p (q u v) -> p u q v", u=2, v=2), sig[:], MULT)
-            value_pairs = h_t[:].rearrange("p u q v -> p (u q v)").bitcast(F32)
+            hidden[e] = ring.tile([P, 2, P, 2], BF16, name="h_t", align_bytes=64, bufs=E)
+            nc.vector.tensor_tensor(hidden[e][:], sums["w3"].rearrange("p (q u v) -> p u q v", u=2, v=2), sig[:], MULT)
+
+        def quantise(e, bank):
+            value_pairs = hidden[e][:].rearrange("p u q v -> p (u q v)").bitcast(F32)
             turned = bank[:, 0:2, :]
             for u in range(2):
                 nc.tensor.transpose(turned[:, u, :], value_pairs[:, u * P : (u + 1) * P], identity[:])
@@ -162,20 +169,70 @@ def tile_moe_two_glu_sigmoid_kernel(
             for lo, hi in zip(cuts, cuts[1:]):
                 nc.scalar.copy(results[:, lo:hi, e * C : (e + 1) * C], bank[:, lo:hi, :])
 
+        gated = {}
+
+        def gated_by_slot(e, bank):
+            h_words, h_scales = quantised[e]
+            y_t = bank[:].rearrange("p t c -> p (t c)")
+            nc.tensor.matmul_mx(
+                out=y_t,
+                lhsT=h_words.bitcast(FP8X4),
+                lhsT_scale=h_scales,
+                rhs=words["w2"][:, e, :].bitcast(FP4X4),
+                rhs_scale=planes["w2", e // HALF][:, e % HALF, :],
+                start=True,
+                stop=True,
+            )
+            gated[e] = ring.tile([P, N], F32, name="gated", align_bytes=64)
+            nc.scalar.activation(gated[e][:], y_t, COPY, scale=slot_gates[:, e : e + 1])
+
+        def turn_back(e, bank, lo, hi):
+            for t in range(lo, hi):
+                nc.tensor.transpose(bank[:, t, :], gated[e][:, t * P : (t + 1) * P], identity[:])
+            nc.scalar.copy(results[:, lo:hi, e * C : (e + 1) * C], bank[:, lo:hi, :])
+
         def scatter(t, lo, hi):
             entries = dst_sb[:, lo * LIST_COLS : hi * LIST_COLS]
             cols = slice(lo * C, hi * C)
-            nc.vector.tensor_tensor(windows[t][:].indirect(entries), results[:, t, cols], gates[:, cols], MULT)
+            if lo == 0:
+                nc.vector.tensor_tensor(windows[t][:].indirect(entries), results[:, t, cols], gates[:], MULT)
+            else:
+                nc.vector.tensor_copy(windows[t][:].indirect(entries), results[:, t, cols])
             if hi == E:
                 nc.sync.dma_start(out[t * P : (t + 1) * P, :], windows[t][:])
 
-        steps = [(first_layer, 0), (first_layer, 1), (second_layer, 0, (0, 1)), (second_layer, 0, (1, NT))]
-        steps.extend([(first_layer, 2), (second_layer, 1, (0, NT))])
-        steps.extend([(first_layer, 3), (second_layer, 2, (0, 2)), (first_layer, 4), (first_layer, 5), (second_layer, 2, (2, NT))])
-        steps.extend([(second_layer, e, (0, NT)) for e in range(HALF, E)])
-        for i, step in enumerate(steps):
-            step[0](step[1], banks[i % 2], *step[2:])
-
-        for lo, hi in ((0, 1), (1, HALF), (HALF, E)):
+        def scatter_all(lo, hi):
             for t in range(NT):
                 scatter(t, lo, hi)
+
+        a_banks, b_banks = pairs["w1"], pairs["w3"]
+        first_layer(0)
+        first_layer(1)
+        quantise(0, banks[0])
+        quantise(1, banks[1])
+        second_layer(0, banks[0], (0, 1))
+        second_layer(0, banks[1], (1, NT))
+        first_layer(2)
+        scatter_all(0, 1)
+        quantise(2, banks[0])
+        gated_by_slot(1, banks[1])
+        turn_back(1, banks[0], 0, 2)
+        for t in range(2):
+            scatter(t, 1, 2)
+        for e in range(HALF, E):
+            first_layer(e)
+        gated_by_slot(2, banks[1])
+        turn_back(1, b_banks[0], 2, NT)
+        for t in range(2, NT):
+            scatter(t, 1, 2)
+        for e in range(HALF, E):
+            quantise(e, a_banks[e - HALF])
+        turn_back(2, a_banks[0], 0, NT)
+        scatter_all(2, 3)
+        gated_by_slot(3, banks[1])
+        turn_back(3, banks[0], 0, NT)
+        scatter_all(3, 4)
+        for e in range(4, E):
+            gated_by_slot(e, a_banks[e - HALF])
+            turn_back(e, b_banks[e - HALF], 0, NT)
+        scatter_all(4, E)

@@ -27,6 +27,7 @@ PAIR_BUFS = 3
 RING_BUFS = 3
 
 GATHER_GROUPS = ((0, 2), (2, 6))
+ON_GPSIMD = (3, 4)
 
 
 def tile_moe_two_glu_sigmoid_kernel(
@@ -48,10 +49,10 @@ def tile_moe_two_glu_sigmoid_kernel(
                 planes[name, half] = keep.tile([P, HALF, H], U8, name="%s_plane%d" % (name, half), align_bytes=64)
         zero = keep.tile([P, 8], F32, name="zero")
         warm = keep.tile([P, 8], F32, name="warm")
-        nc.gpsimd.memset(x_plane[:].bitcast(I32), 0)
-        nc.gpsimd.memset(zero[:], 0.0)
+        nc.vector.memset(zero[:], 0.0)
+        nc.vector.memset(x_plane[:].bitcast(I32), 0)
         nc.scalar.activation(warm[:, 0:1], zero[:, 0:1], SIGMOID)
-        gates = keep.tile([P, C], F32, name="gates", align_bytes=64)
+        gates = keep.tile([P, E * C], F32, name="gates", align_bytes=64)
         slot_gates = keep.tile([P, E], F32, name="slot_gates", align_bytes=64)
         words = {}
         for name in ("w1", "w3", "w2"):
@@ -74,6 +75,7 @@ def tile_moe_two_glu_sigmoid_kernel(
         for half in range(2):
             for name in ("w1", "w3", "w2"):
                 nc.vector.memset(planes[name, half][:].bitcast(I32), 0)
+        nc.vector.memset(windows[NT - 1][:].bitcast(I32), 0)
         make_identity(nc, identity[:])
 
         nc.sync.dma_start(x_sb[:], x_words[0].rearrange("p n t -> p (n t)").bitcast(I32))
@@ -88,13 +90,18 @@ def tile_moe_two_glu_sigmoid_kernel(
         load_words("w3", w3_words, 2, HALF)
         load_words("w2", w2_words, 0, 2)
         nc.sync.dma_start(dst_sb[:], dst)
-        nc.sync.dma_start(gates[:], gate[0:P, 0:C])
+        nc.sync.dma_start(gates[:, 0:C], gate[0:P, 0:C])
+        load_weight_plane("w1", w1_scales, 1)
+        load_weight_plane("w3", w3_scales, 1)
         with nc.allow_non_contiguous_dma(reason="one gate value a slot, slots on the partitions"):
-            nc.sync.dma_start(slot_gates[:, 1:E], gate[0, C:].rearrange("(e c) -> c e", c=C))
-        for name, dram, scales in (("w1", w1_words, w1_scales), ("w3", w3_words, w3_scales)):
-            load_weight_plane(name, scales, 1)
-            load_words(name, dram, HALF, E)
-        load_words("w2", w2_words, 2, E)
+            nc.sync.dma_start(slot_gates[:, 1:HALF], gate[0, C : HALF * C].rearrange("(e c) -> c e", c=C))
+        for e in range(HALF, E):
+            if e == E - 1:
+                load_words("w2", w2_words, 2, HALF)
+            load_words("w1", w1_words, e, e + 1)
+            load_words("w3", w3_words, e, e + 1)
+        load_words("w2", w2_words, HALF, E)
+        nc.sync.dma_start(gates[:, HALF * C :], gate[0:P, HALF * C :])
         load_weight_plane("w2", w2_scales, 1)
 
         slot_words = {}
@@ -111,7 +118,7 @@ def tile_moe_two_glu_sigmoid_kernel(
             gather(slot_scales, "slot_scales", U8, x_plane[:], lo, hi, "slot_scales%d" % lo)
         gather(slot_words, "slot_words", U32, x_sb[:].bitcast(U32), *GATHER_GROUPS[1], "x_plane")
 
-        for t in range(NT):
+        for t in range(NT - 1):
             nc.scalar.copy(windows[t][:], zero[:, 0:1].to_broadcast([P, T]))
 
         banks = [psum.tile([P, NT, C], F32, name="bank%d" % b, bufs=1) for b in range(2)]
@@ -136,15 +143,29 @@ def tile_moe_two_glu_sigmoid_kernel(
                 )
             sig = ring.tile([P, 2, P, 2], F32, name="sig", align_bytes=64)
             nc.scalar.activation(sig[:], sums["w1"].rearrange("p (q u v) -> p u q v", u=2, v=2), SIGMOID)
-            hidden[e] = ring.tile([P, 2, P, 2], BF16, name="h_t", align_bytes=64, bufs=E)
-            nc.vector.tensor_tensor(hidden[e][:], sums["w3"].rearrange("p (q u v) -> p u q v", u=2, v=2), sig[:], MULT)
+            b_view = sums["w3"].rearrange("p (q u v) -> p u q v", u=2, v=2)
+            if e == ON_GPSIMD[0]:
+                hidden[e] = keep.tile([P, 2, P, 2], BF16, name="h_t_held", tag="h_held", align_bytes=64)
+            else:
+                hidden[e] = ring.tile([P, 2, P, 2], BF16, name="h_t", align_bytes=64, bufs=E)
+            if e in ON_GPSIMD:
+                b_sb = ring.tile([P, 2, P, 2], F32, name="b_sb", align_bytes=64)
+                nc.scalar.copy(b_sb[:], b_view)
+                flat = "p u q v -> p (u q v)"
+                nc.gpsimd.tensor_tensor(hidden[e][:].rearrange(flat), b_sb[:].rearrange(flat), sig[:].rearrange(flat), MULT)
+            else:
+                nc.vector.tensor_tensor(hidden[e][:], b_view, sig[:], MULT)
 
-        def quantise(e, bank):
+        def turn(e, turned):
             value_pairs = hidden[e][:].rearrange("p u q v -> p (u q v)").bitcast(F32)
-            turned = bank[:, 0:2, :]
             for u in range(2):
                 nc.tensor.transpose(turned[:, u, :], value_pairs[:, u * P : (u + 1) * P], identity[:])
-            h = ring.tile([P, 4 * C], BF16, name="h", align_bytes=64)
+
+        def quantise(e, turned):
+            if e == ON_GPSIMD[0] - 1:
+                h = keep.tile([P, 4 * C], BF16, name="h_held", tag="h_held", align_bytes=64)
+            else:
+                h = ring.tile([P, 4 * C], BF16, name="h", align_bytes=64)
             nc.scalar.copy(h[:].bitcast(F32).rearrange("p (c u) -> p c u", u=2), turned.rearrange("p u c -> p c u"))
             h_words = ring.tile([P, C], U32, name="h_words", align_bytes=64, bufs=E)
             h_scales = ring.tile([P, C], U8, name="h_scales", align_bytes=64, bufs=E)
@@ -189,13 +210,15 @@ def tile_moe_two_glu_sigmoid_kernel(
         def turn_back(e, bank, lo, hi):
             for t in range(lo, hi):
                 nc.tensor.transpose(bank[:, t, :], gated[e][:, t * P : (t + 1) * P], identity[:])
+
+        def empty(e, bank, lo, hi):
             nc.scalar.copy(results[:, lo:hi, e * C : (e + 1) * C], bank[:, lo:hi, :])
 
         def scatter(t, lo, hi):
             entries = dst_sb[:, lo * LIST_COLS : hi * LIST_COLS]
             cols = slice(lo * C, hi * C)
-            if lo == 0:
-                nc.vector.tensor_tensor(windows[t][:].indirect(entries), results[:, t, cols], gates[:], MULT)
+            if lo not in gated:
+                nc.vector.tensor_tensor(windows[t][:].indirect(entries), results[:, t, cols], gates[:, cols], MULT)
             else:
                 nc.vector.tensor_copy(windows[t][:].indirect(entries), results[:, t, cols])
             if hi == E:
@@ -205,34 +228,56 @@ def tile_moe_two_glu_sigmoid_kernel(
             for t in range(NT):
                 scatter(t, lo, hi)
 
+        def last_half(t, bank):
+            for e in range(HALF, E):
+                h_words, h_scales = quantised[e]
+                nc.tensor.matmul_mx(
+                    out=bank[:, e - HALF, :],
+                    lhsT=words["w2"][:, e, 2 * P * t : 2 * P * (t + 1)].bitcast(FP4X4),
+                    lhsT_scale=planes["w2", 1][:, e - HALF, P * t : P * (t + 1)],
+                    rhs=h_words.bitcast(FP8X4),
+                    rhs_scale=h_scales,
+                    start=True,
+                    stop=True,
+                )
+            nc.scalar.copy(results[:, t, HALF * C :].rearrange("p (e c) -> p e c", c=C), bank[:, 0:HALF, :])
+            scatter(t, HALF, E)
+
         a_banks, b_banks = pairs["w1"], pairs["w3"]
+        low, high = slice(0, 2), slice(2, NT)
         first_layer(0)
         first_layer(1)
-        quantise(0, banks[0])
-        quantise(1, banks[1])
+        for e in range(2):
+            turn(e, banks[e][:, low, :])
+            quantise(e, banks[e][:, low, :])
         second_layer(0, banks[0], (0, 1))
         second_layer(0, banks[1], (1, NT))
         first_layer(2)
         scatter_all(0, 1)
-        quantise(2, banks[0])
-        gated_by_slot(1, banks[1])
-        turn_back(1, banks[0], 0, 2)
-        for t in range(2):
-            scatter(t, 1, 2)
-        for e in range(HALF, E):
-            first_layer(e)
+        turn(2, banks[0][:, low, :])
+        quantise(2, banks[0][:, low, :])
+        gated_by_slot(1, a_banks[1])
+        for bank, part in zip(banks, (low, high)):
+            turn_back(1, bank, part.start, part.stop)
+            empty(1, bank, part.start, part.stop)
+        scatter_all(1, 2)
+        first_layer(3)
+        first_layer(4)
         gated_by_slot(2, banks[1])
-        turn_back(1, b_banks[0], 2, NT)
+        first_layer(5)
+        for t in range(2):
+            turn_back(2, banks[t], t, t + 1)
+            empty(2, banks[t], t, t + 1)
+            scatter(t, 2, 3)
+        turn(3, banks[0][:, low, :])
+        turn(4, banks[0][:, high, :])
+        turn(5, banks[1][:, low, :])
+        turn_back(2, banks[1], 2, NT)
+        quantise(3, banks[0][:, low, :])
+        quantise(4, banks[0][:, high, :])
+        quantise(5, banks[1][:, low, :])
+        empty(2, banks[1], 2, NT)
         for t in range(2, NT):
-            scatter(t, 1, 2)
-        for e in range(HALF, E):
-            quantise(e, a_banks[e - HALF])
-        turn_back(2, a_banks[0], 0, NT)
-        scatter_all(2, 3)
-        gated_by_slot(3, banks[1])
-        turn_back(3, banks[0], 0, NT)
-        scatter_all(3, 4)
-        for e in range(4, E):
-            gated_by_slot(e, a_banks[e - HALF])
-            turn_back(e, b_banks[e - HALF], 0, NT)
-        scatter_all(4, E)
+            scatter(t, 2, 3)
+        for t in range(NT):
+            last_half(t, (a_banks + b_banks)[t])

@@ -27,7 +27,8 @@ PAIR_BUFS = 3
 RING_BUFS = 3
 
 GATHER_GROUPS = ((0, 2), (2, 6))
-ON_GPSIMD = (3, 4)
+ON_GPSIMD = (3, 4, 5)
+HELD = {3: 2, 5: 4}
 
 
 def tile_moe_two_glu_sigmoid_kernel(
@@ -95,12 +96,13 @@ def tile_moe_two_glu_sigmoid_kernel(
         load_weight_plane("w3", w3_scales, 1)
         with nc.allow_non_contiguous_dma(reason="one gate value a slot, slots on the partitions"):
             nc.sync.dma_start(slot_gates[:, 1:HALF], gate[0, C : HALF * C].rearrange("(e c) -> c e", c=C))
-        for e in range(HALF, E):
-            if e == E - 1:
-                load_words("w2", w2_words, 2, HALF)
+        for e in range(HALF, E - 1):
             load_words("w1", w1_words, e, e + 1)
             load_words("w3", w3_words, e, e + 1)
+        load_words("w2", w2_words, 2, HALF)
+        load_words("w1", w1_words, E - 1, E)
         load_words("w2", w2_words, HALF, E)
+        load_words("w3", w3_words, E - 1, E)
         nc.sync.dma_start(gates[:, HALF * C :], gate[0:P, HALF * C :])
         load_weight_plane("w2", w2_scales, 1)
 
@@ -128,6 +130,7 @@ def tile_moe_two_glu_sigmoid_kernel(
         quantised = {}
 
         hidden = {}
+        factors = {}
 
         def first_layer(e):
             sums = {name: pairs[name][e % PAIR_BUFS][:].rearrange("p t c -> p (t c)") for name in ("w1", "w3")}
@@ -144,17 +147,23 @@ def tile_moe_two_glu_sigmoid_kernel(
             sig = ring.tile([P, 2, P, 2], F32, name="sig", align_bytes=64)
             nc.scalar.activation(sig[:], sums["w1"].rearrange("p (q u v) -> p u q v", u=2, v=2), SIGMOID)
             b_view = sums["w3"].rearrange("p (q u v) -> p u q v", u=2, v=2)
-            if e == ON_GPSIMD[0]:
-                hidden[e] = keep.tile([P, 2, P, 2], BF16, name="h_t_held", tag="h_held", align_bytes=64)
-            else:
-                hidden[e] = ring.tile([P, 2, P, 2], BF16, name="h_t", align_bytes=64, bufs=E)
             if e in ON_GPSIMD:
                 b_sb = ring.tile([P, 2, P, 2], F32, name="b_sb", align_bytes=64)
                 nc.scalar.copy(b_sb[:], b_view)
-                flat = "p u q v -> p (u q v)"
-                nc.gpsimd.tensor_tensor(hidden[e][:].rearrange(flat), b_sb[:].rearrange(flat), sig[:].rearrange(flat), MULT)
+                b_view = b_sb[:]
+            factors[e] = (b_view, sig[:])
+
+        def product(e):
+            b_view, sig = factors[e]
+            if e in HELD:
+                hidden[e] = keep.tile([P, 2, P, 2], BF16, name="h_t_held", tag="h%d" % HELD[e], align_bytes=64)
             else:
-                nc.vector.tensor_tensor(hidden[e][:], b_view, sig[:], MULT)
+                hidden[e] = ring.tile([P, 2, P, 2], BF16, name="h_t", align_bytes=64, bufs=E)
+            if e in ON_GPSIMD:
+                flat = "p u q v -> p (u q v)"
+                nc.gpsimd.tensor_tensor(hidden[e][:].rearrange(flat), b_view.rearrange(flat), sig.rearrange(flat), MULT)
+            else:
+                nc.vector.tensor_tensor(hidden[e][:], b_view, sig, MULT)
 
         def turn(e, turned):
             value_pairs = hidden[e][:].rearrange("p u q v -> p (u q v)").bitcast(F32)
@@ -162,8 +171,8 @@ def tile_moe_two_glu_sigmoid_kernel(
                 nc.tensor.transpose(turned[:, u, :], value_pairs[:, u * P : (u + 1) * P], identity[:])
 
         def quantise(e, turned):
-            if e == ON_GPSIMD[0] - 1:
-                h = keep.tile([P, 4 * C], BF16, name="h_held", tag="h_held", align_bytes=64)
+            if e in HELD.values():
+                h = keep.tile([P, 4 * C], BF16, name="h_held", tag="h%d" % e, align_bytes=64)
             else:
                 h = ring.tile([P, 4 * C], BF16, name="h", align_bytes=64)
             nc.scalar.copy(h[:].bitcast(F32).rearrange("p (c u) -> p c u", u=2), turned.rearrange("p u c -> p c u"))
@@ -228,11 +237,11 @@ def tile_moe_two_glu_sigmoid_kernel(
             for t in range(NT):
                 scatter(t, lo, hi)
 
-        def last_half(t, bank):
-            for e in range(HALF, E):
+        def last_pair(t, bank):
+            for e in range(E - 2, E):
                 h_words, h_scales = quantised[e]
                 nc.tensor.matmul_mx(
-                    out=bank[:, e - HALF, :],
+                    out=bank[:, e - (E - 2), :],
                     lhsT=words["w2"][:, e, 2 * P * t : 2 * P * (t + 1)].bitcast(FP4X4),
                     lhsT_scale=planes["w2", 1][:, e - HALF, P * t : P * (t + 1)],
                     rhs=h_words.bitcast(FP8X4),
@@ -240,19 +249,21 @@ def tile_moe_two_glu_sigmoid_kernel(
                     start=True,
                     stop=True,
                 )
-            nc.scalar.copy(results[:, t, HALF * C :].rearrange("p (e c) -> p e c", c=C), bank[:, 0:HALF, :])
-            scatter(t, HALF, E)
+            nc.scalar.copy(results[:, t, (E - 2) * C :].rearrange("p (e c) -> p e c", c=C), bank[:, 0:2, :])
+            scatter(t, E - 2, E)
 
         a_banks, b_banks = pairs["w1"], pairs["w3"]
         low, high = slice(0, 2), slice(2, NT)
-        first_layer(0)
-        first_layer(1)
+        for e in range(2):
+            first_layer(e)
+            product(e)
         for e in range(2):
             turn(e, banks[e][:, low, :])
             quantise(e, banks[e][:, low, :])
         second_layer(0, banks[0], (0, 1))
         second_layer(0, banks[1], (1, NT))
         first_layer(2)
+        product(2)
         scatter_all(0, 1)
         turn(2, banks[0][:, low, :])
         quantise(2, banks[0][:, low, :])
@@ -261,23 +272,32 @@ def tile_moe_two_glu_sigmoid_kernel(
             turn_back(1, bank, part.start, part.stop)
             empty(1, bank, part.start, part.stop)
         scatter_all(1, 2)
-        first_layer(3)
-        first_layer(4)
+        for e in (3, 4):
+            first_layer(e)
+            product(e)
         gated_by_slot(2, banks[1])
-        first_layer(5)
         for t in range(2):
             turn_back(2, banks[t], t, t + 1)
             empty(2, banks[t], t, t + 1)
             scatter(t, 2, 3)
         turn(3, banks[0][:, low, :])
-        turn(4, banks[0][:, high, :])
-        turn(5, banks[1][:, low, :])
+        turn(4, banks[1][:, low, :])
         turn_back(2, banks[1], 2, NT)
         quantise(3, banks[0][:, low, :])
-        quantise(4, banks[0][:, high, :])
-        quantise(5, banks[1][:, low, :])
+        quantise(4, banks[1][:, low, :])
+        first_layer(5)
+        product(5)
         empty(2, banks[1], 2, NT)
         for t in range(2, NT):
             scatter(t, 2, 3)
+        second_layer(3, banks[0], (0, 2))
+        for t in range(2):
+            scatter(t, 3, 4)
+        turn(5, banks[0][:, low, :])
+        products(3, banks[0], 2, NT)
+        quantise(5, banks[0][:, low, :])
+        empty(3, banks[0], 2, NT)
+        for t in range(2, NT):
+            scatter(t, 3, 4)
         for t in range(NT):
-            last_half(t, (a_banks + b_banks)[t])
+            last_pair(t, (a_banks + b_banks)[t])

@@ -23,12 +23,7 @@ NT = N // P
 LIST_COLS = C // 16
 PLANE_ROWS = 4
 HALF = E // 2
-PAIR_BUFS = 3
-RING_BUFS = 3
-
-GATHER_GROUPS = ((0, 2), (2, 6))
-ON_GPSIMD = (3, 4, 5)
-HELD = {3: 2, 5: 4}
+BANKS = 8
 
 
 def tile_moe_two_glu_sigmoid_kernel(
@@ -37,175 +32,211 @@ def tile_moe_two_glu_sigmoid_kernel(
     nc = tc.nc
     with ExitStack() as ctx:
         keep = ctx.enter_context(tc.tile_pool(name="keep", bufs=1))
-        ring = ctx.enter_context(tc.tile_pool(name="ring", bufs=RING_BUFS))
-        psum = ctx.enter_context(tc.psum_pool(name="psum", bufs=PAIR_BUFS))
+        psum = ctx.enter_context(tc.psum_pool(name="psum", bufs=1))
+
+        def sbuf(name, shape, dtype, tag=None):
+            return keep.tile(shape, dtype, name=name, tag=tag or name, align_bytes=64)
 
         offs_sb = keep.tile([P, E * LIST_COLS], U16, name="offs_sb")
         dst_sb = keep.tile([P, E * LIST_COLS], U16, name="dst_sb")
-        x_sb = keep.tile([P, T], I32, name="x_sb", align_bytes=64)
-        x_plane = keep.tile([P, T], U8, name="x_plane", tag="x_plane", align_bytes=64)
+        x_sb = sbuf("x_sb", [P, T], I32)
+        x_plane = sbuf("x_plane", [P, T], U8)
         planes = {}
+        words = {}
         for name in ("w1", "w3", "w2"):
+            words[name] = sbuf(name + "_words", [P, E, 2 * H], U8)
             for half in range(2):
-                planes[name, half] = keep.tile([P, HALF, H], U8, name="%s_plane%d" % (name, half), align_bytes=64)
-        zero = keep.tile([P, 8], F32, name="zero")
-        warm = keep.tile([P, 8], F32, name="warm")
+                planes[name, half] = sbuf("%s_plane%d" % (name, half), [P, HALF, H], U8)
+        zero = sbuf("zero", [P, 8], F32)
+        warm = sbuf("warm", [P, 8], F32)
+        gates = sbuf("gates", [P, E * C], F32)
+        slot_gates = sbuf("slot_gates", [P, E], F32)
+        windows = [sbuf("window%d" % t, [P, T], F32) for t in range(NT)]
+        identity = sbuf("identity", [P, P], F32)
+        banks = [psum.tile([P, NT, C], F32, name="bank%d" % b) for b in range(BANKS)]
+
         nc.vector.memset(zero[:], 0.0)
         nc.vector.memset(x_plane[:].bitcast(I32), 0)
         nc.scalar.activation(warm[:, 0:1], zero[:, 0:1], SIGMOID)
-        gates = keep.tile([P, E * C], F32, name="gates", align_bytes=64)
-        slot_gates = keep.tile([P, E], F32, name="slot_gates", align_bytes=64)
-        words = {}
-        for name in ("w1", "w3", "w2"):
-            words[name] = keep.tile([P, E, 2 * H], U8, name=name + "_words", align_bytes=64)
-        results = keep.tile([P, NT, E * C], F32, name="results", align_bytes=64)
-        windows = [keep.tile([P, T], F32, name="window%d" % t, align_bytes=64) for t in range(NT)]
-        identity = keep.tile([P, P], F32, name="identity", align_bytes=64)
-
-        def load_plane(plane, rows, lo=0, hi=PLANE_ROWS):
-            for r in range(lo, hi):
-                nc.sync.dma_start(plane[r:P:32], rows[r])
-
-        def load_weight_plane(name, scales, half, lo=0, hi=PLANE_ROWS):
-            rows = scales.bitcast(I32)[half * HALF : (half + 1) * HALF].rearrange("e s (q r) n -> r q (e s) n", r=PLANE_ROWS)
-            load_plane(planes[name, half][:].bitcast(I32), rows, lo, hi)
-
-        def load_words(name, dram, lo, hi):
-            nc.sync.dma_start(words[name][:, lo:hi, :].bitcast(I32), dram.bitcast(I32)[lo:hi].rearrange("e s p b -> p (e s) b"))
-
         for half in range(2):
             for name in ("w1", "w3", "w2"):
                 nc.vector.memset(planes[name, half][:].bitcast(I32), 0)
         nc.vector.memset(windows[NT - 1][:].bitcast(I32), 0)
         make_identity(nc, identity[:])
 
-        nc.sync.dma_start(x_sb[:], x_words[0].rearrange("p n t -> p (n t)").bitcast(I32))
+        dram_words = {"w1": w1_words, "w3": w3_words, "w2": w2_words}
+        dram_scales = {"w1": w1_scales, "w3": w3_scales, "w2": w2_scales}
+
+        def load_plane(plane, rows, queue=nc.sync):
+            for r in range(PLANE_ROWS):
+                queue.dma_start(plane[r:P:32], rows[r])
+
+        def load_weight_plane(name, half, queue=nc.sync):
+            rows = dram_scales[name].bitcast(I32)[half * HALF : (half + 1) * HALF]
+            load_plane(planes[name, half][:].bitcast(I32), rows.rearrange("e s (q r) n -> r q (e s) n", r=PLANE_ROWS), queue)
+
+        def load_words(name, lo, hi, queue=nc.sync):
+            rows = dram_words[name].bitcast(I32)[lo:hi].rearrange("e s p b -> p (e s) b")
+            queue.dma_start(words[name][:, lo:hi, :].bitcast(I32), rows)
+
+        def load_x(queue=nc.sync):
+            queue.dma_start(x_sb[:], x_words[0].rearrange("p n t -> p (n t)").bitcast(I32))
+
+        def load_x_plane():
+            load_plane(x_plane[:].bitcast(I32), x_scales.bitcast(I32).rearrange("o (q r) n -> r q (o n)", r=PLANE_ROWS))
+
+        def load_gates(lo, hi):
+            nc.sync.dma_start(gates[:, lo * C : hi * C], gate[0:P, lo * C : hi * C])
+
+        def load_slot_gates(lo, hi):
+            with nc.allow_non_contiguous_dma(reason="one gate value a slot, slots on the partitions"):
+                nc.sync.dma_start(slot_gates[:, lo:hi], gate[0, lo * C : hi * C].rearrange("(e c) -> c e", c=C))
+
+        load_x()
         nc.sync.dma_start(offs_sb[:], offs)
-        load_plane(x_plane[:].bitcast(I32), x_scales.bitcast(I32).rearrange("o (q r) n -> r q (o n)", r=PLANE_ROWS))
-        load_words("w1", w1_words, 0, 2)
-        load_weight_plane("w1", w1_scales, 0)
-        load_words("w3", w3_words, 0, 2)
-        load_weight_plane("w3", w3_scales, 0)
-        load_words("w1", w1_words, 2, HALF)
-        load_weight_plane("w2", w2_scales, 0)
-        load_words("w3", w3_words, 2, HALF)
-        load_words("w2", w2_words, 0, 2)
+        load_x_plane()
+        load_words("w1", 0, 2)
+        load_weight_plane("w1", 0)
+        load_words("w3", 0, 2)
+        load_weight_plane("w3", 0)
+        load_words("w1", 2, 3)
+        load_words("w3", 2, 3)
+        load_weight_plane("w2", 0)
+        load_words("w2", 0, 2)
         nc.sync.dma_start(dst_sb[:], dst)
-        nc.sync.dma_start(gates[:, 0:C], gate[0:P, 0:C])
-        load_weight_plane("w1", w1_scales, 1)
-        load_weight_plane("w3", w3_scales, 1)
-        with nc.allow_non_contiguous_dma(reason="one gate value a slot, slots on the partitions"):
-            nc.sync.dma_start(slot_gates[:, 1:HALF], gate[0, C : HALF * C].rearrange("(e c) -> c e", c=C))
-        for e in range(HALF, E - 1):
-            load_words("w1", w1_words, e, e + 1)
-            load_words("w3", w3_words, e, e + 1)
-        load_words("w2", w2_words, 2, HALF)
-        load_words("w1", w1_words, E - 1, E)
-        load_words("w2", w2_words, HALF, E)
-        load_words("w3", w3_words, E - 1, E)
-        nc.sync.dma_start(gates[:, HALF * C :], gate[0:P, HALF * C :])
-        load_weight_plane("w2", w2_scales, 1)
+        load_gates(0, 1)
+        load_weight_plane("w1", 1)
+        load_weight_plane("w3", 1)
+        load_weight_plane("w2", 1)
+        load_words("w3", 3, 4)
+        load_slot_gates(1, HALF)
+        load_words("w1", 3, 4)
+        load_words("w2", 2, 3)
+        load_words("w1", 4, 5)
+        load_words("w3", 4, 5)
+        load_words("w1", 5, 6)
+        load_words("w3", 5, 6)
+        load_words("w2", HALF, E)
+        load_gates(HALF, E)
 
         slot_words = {}
         slot_scales = {}
 
-        def gather(into, name, dtype, window, lo, hi, tag):
-            gathered = keep.tile([P, (hi - lo) * C], dtype, name="%s%d" % (name, lo), tag=tag, align_bytes=64)
+        def gather(into, name, dtype, window, lo, hi, tag=None):
+            gathered = sbuf("%s%d" % (name, lo), [P, (hi - lo) * C], dtype, tag)
             nc.vector.tensor_copy(gathered[:], window.indirect(offs_sb[:, lo * LIST_COLS : hi * LIST_COLS]))
             for e in range(lo, hi):
                 into[e] = gathered[:, (e - lo) * C : (e - lo + 1) * C]
 
-        gather(slot_words, "slot_words", U32, x_sb[:].bitcast(U32), *GATHER_GROUPS[0], "slot_words0")
-        for lo, hi in GATHER_GROUPS:
-            gather(slot_scales, "slot_scales", U8, x_plane[:], lo, hi, "slot_scales%d" % lo)
-        gather(slot_words, "slot_words", U32, x_sb[:].bitcast(U32), *GATHER_GROUPS[1], "x_plane")
+        def gather_words(lo, hi, tag=None):
+            gather(slot_words, "slot_words", U32, x_sb[:].bitcast(U32), lo, hi, tag)
+
+        def gather_scales(lo, hi, tag=None):
+            gather(slot_scales, "slot_scales", U8, x_plane[:], lo, hi, tag)
+
+        gather_words(0, 2)
+        gather_scales(0, 2)
+        gather_scales(2, E)
+        gather_words(2, E, "x_plane")
 
         for t in range(NT - 1):
             nc.scalar.copy(windows[t][:], zero[:, 0:1].to_broadcast([P, T]))
 
-        banks = [psum.tile([P, NT, C], F32, name="bank%d" % b, bufs=1) for b in range(2)]
-        pairs = {}
-        for name in ("w1", "w3"):
-            pairs[name] = [psum.tile([P, NT, C], F32, name="sum_%s_%d" % (name, b), bufs=1) for b in range(PAIR_BUFS)]
-        quantised = {}
-
-        hidden = {}
+        sigmoids = {}
         factors = {}
+        hidden = {}
+        grouped = {}
+        quantised = {}
+        gated = {}
+        results = {}
 
-        def first_layer(e):
-            sums = {name: pairs[name][e % PAIR_BUFS][:].rearrange("p t c -> p (t c)") for name in ("w1", "w3")}
-            for name in ("w1", "w3"):
-                nc.tensor.matmul_mx(
-                    out=sums[name],
-                    lhsT=slot_words[e].bitcast(FP8X4),
-                    lhsT_scale=slot_scales[e],
-                    rhs=words[name][:, e, :].bitcast(FP4X4),
-                    rhs_scale=planes[name, e // HALF][:, e % HALF, :],
-                    start=True,
-                    stop=True,
-                )
-            sig = ring.tile([P, 2, P, 2], F32, name="sig", align_bytes=64)
-            nc.scalar.activation(sig[:], sums["w1"].rearrange("p (q u v) -> p u q v", u=2, v=2), SIGMOID)
-            b_view = sums["w3"].rearrange("p (q u v) -> p u q v", u=2, v=2)
-            if e in ON_GPSIMD:
-                b_sb = ring.tile([P, 2, P, 2], F32, name="b_sb", align_bytes=64)
-                nc.scalar.copy(b_sb[:], b_view)
-                b_view = b_sb[:]
-            factors[e] = (b_view, sig[:])
+        def flat(bank):
+            return bank[:].rearrange("p t c -> p (t c)")
 
-        def product(e):
-            b_view, sig = factors[e]
-            if e in HELD:
-                hidden[e] = keep.tile([P, 2, P, 2], BF16, name="h_t_held", tag="h%d" % HELD[e], align_bytes=64)
-            else:
-                hidden[e] = ring.tile([P, 2, P, 2], BF16, name="h_t", align_bytes=64, bufs=E)
-            if e in ON_GPSIMD:
-                flat = "p u q v -> p (u q v)"
-                nc.gpsimd.tensor_tensor(hidden[e][:].rearrange(flat), b_view.rearrange(flat), sig.rearrange(flat), MULT)
-            else:
-                nc.vector.tensor_tensor(hidden[e][:], b_view, sig, MULT)
+        def by_pairs(bank):
+            return flat(bank).rearrange("p (q u v) -> p u q v", u=2, v=2)
 
-        def turn(e, turned):
+        def first_sum(name, e, bank):
+            nc.tensor.matmul_mx(
+                out=flat(bank),
+                lhsT=slot_words[e].bitcast(FP8X4),
+                lhsT_scale=slot_scales[e],
+                rhs=words[name][:, e, :].bitcast(FP4X4),
+                rhs_scale=planes[name, e // HALF][:, e % HALF, :],
+                start=True,
+                stop=True,
+            )
+
+        def sigmoid(e, bank, parts=(slice(0, 2),), tag=None):
+            sigmoids[e] = sbuf("sigmoid%d" % e, [P, 2, P, 2], F32, tag)
+            for part in parts:
+                nc.scalar.activation(sigmoids[e][:, part], by_pairs(bank)[:, part], SIGMOID)
+
+        def product_on_vector(e, bank, parts=(slice(0, 2),), tag=None):
+            hidden[e] = sbuf("hidden%d" % e, [P, 2, P, 2], BF16, tag)
+            for part in parts:
+                nc.vector.tensor_tensor(hidden[e][:, part], by_pairs(bank)[:, part], sigmoids[e][:, part], MULT)
+
+        def empty_b(e, bank, tag=None):
+            factors[e] = sbuf("factor%d" % e, [P, 2, P, 2], F32, tag)
+            nc.scalar.copy(factors[e][:], by_pairs(bank))
+
+        def product_on_gpsimd(e, tag=None):
+            hidden[e] = sbuf("hidden%d" % e, [P, 2, P, 2], BF16, tag)
+            merged = "p u q v -> p (u q v)"
+            nc.gpsimd.tensor_tensor(
+                hidden[e][:].rearrange(merged), factors[e][:].rearrange(merged), sigmoids[e][:].rearrange(merged), MULT
+            )
+
+        def turn(e, bank, at=0):
             value_pairs = hidden[e][:].rearrange("p u q v -> p (u q v)").bitcast(F32)
             for u in range(2):
-                nc.tensor.transpose(turned[:, u, :], value_pairs[:, u * P : (u + 1) * P], identity[:])
+                nc.tensor.transpose(bank[:, at + u, :], value_pairs[:, u * P : (u + 1) * P], identity[:])
 
-        def quantise(e, turned):
-            if e in HELD.values():
-                h = keep.tile([P, 4 * C], BF16, name="h_held", tag="h%d" % e, align_bytes=64)
-            else:
-                h = ring.tile([P, 4 * C], BF16, name="h", align_bytes=64)
-            nc.scalar.copy(h[:].bitcast(F32).rearrange("p (c u) -> p c u", u=2), turned.rearrange("p u c -> p c u"))
-            h_words = ring.tile([P, C], U32, name="h_words", align_bytes=64, bufs=E)
-            h_scales = ring.tile([P, C], U8, name="h_scales", align_bytes=64, bufs=E)
-            nc.vector.quantize_mx(out=h_words[:].bitcast(FP8X4), scales=h_scales[:], in_=h[:])
-            quantised[e] = (h_words[:], h_scales[:])
+        def group(e, bank, into, copy=nc.scalar.copy, at=0):
+            copy(into.bitcast(F32).rearrange("p (c u) -> p c u", u=2), bank[:, at : at + 2, :].rearrange("p u c -> p c u"))
 
-        def products(e, bank, lo, hi):
+        def quantise(lo, hi, values, tag=None):
+            h_words = sbuf("h_words%d" % lo, [P, (hi - lo) * C], U32, tag)
+            h_scales = sbuf("h_scales%d" % lo, [P, (hi - lo) * C], U8)
+            nc.vector.quantize_mx(out=h_words[:].bitcast(FP8X4), scales=h_scales[:], in_=values)
+            for e in range(lo, hi):
+                cols = slice((e - lo) * C, (e - lo + 1) * C)
+                quantised[e] = (h_words[:, cols], h_scales[:, cols])
+
+        def second_sum(e, t, into):
             h_words, h_scales = quantised[e]
+            nc.tensor.matmul_mx(
+                out=into,
+                lhsT=words["w2"][:, e, 2 * P * t : 2 * P * (t + 1)].bitcast(FP4X4),
+                lhsT_scale=planes["w2", e // HALF][:, e % HALF, P * t : P * (t + 1)],
+                rhs=h_words.bitcast(FP8X4),
+                rhs_scale=h_scales,
+                start=True,
+                stop=True,
+            )
+
+        def empty(name, bank, lo, hi, tag=None):
+            emptied = sbuf(name, [P, hi - lo, C], F32, tag)
+            nc.scalar.copy(emptied[:], bank[:, lo:hi, :])
+            return emptied
+
+        def by_windows(e, bank, lo, hi, tag=None):
             for t in range(lo, hi):
-                nc.tensor.matmul_mx(
-                    out=bank[:, t, :],
-                    lhsT=words["w2"][:, e, 2 * P * t : 2 * P * (t + 1)].bitcast(FP4X4),
-                    lhsT_scale=planes["w2", e // HALF][:, e % HALF, P * t : P * (t + 1)],
-                    rhs=h_words.bitcast(FP8X4),
-                    rhs_scale=h_scales,
-                    start=True,
-                    stop=True,
-                )
+                second_sum(e, t, bank[:, t, :])
+            emptied = empty("results%d_%d" % (e, lo), bank, lo, hi, tag)
+            for t in range(lo, hi):
+                results[e, t] = emptied[:, t - lo, :]
 
-        def second_layer(e, bank, cuts):
-            products(e, bank, cuts[0], cuts[-1])
-            for lo, hi in zip(cuts, cuts[1:]):
-                nc.scalar.copy(results[:, lo:hi, e * C : (e + 1) * C], bank[:, lo:hi, :])
-
-        gated = {}
+        def by_experts(t, bank, lo, hi):
+            for e in range(lo, hi):
+                second_sum(e, t, bank[:, e - lo, :])
+            results[lo, t] = empty("results%d_%d" % (lo, t), bank, 0, hi - lo)[:].rearrange("p e c -> p (e c)")
 
         def gated_by_slot(e, bank):
             h_words, h_scales = quantised[e]
-            y_t = bank[:].rearrange("p t c -> p (t c)")
             nc.tensor.matmul_mx(
-                out=y_t,
+                out=flat(bank),
                 lhsT=h_words.bitcast(FP8X4),
                 lhsT_scale=h_scales,
                 rhs=words["w2"][:, e, :].bitcast(FP4X4),
@@ -213,91 +244,99 @@ def tile_moe_two_glu_sigmoid_kernel(
                 start=True,
                 stop=True,
             )
-            gated[e] = ring.tile([P, N], F32, name="gated", align_bytes=64)
-            nc.scalar.activation(gated[e][:], y_t, COPY, scale=slot_gates[:, e : e + 1])
+            gated[e] = sbuf("gated%d" % e, [P, N], F32)
+            nc.scalar.activation(gated[e][:], flat(bank), COPY, scale=slot_gates[:, e : e + 1])
 
-        def turn_back(e, bank, lo, hi):
+        def turn_back(e, bank, lo, hi, tag=None):
             for t in range(lo, hi):
                 nc.tensor.transpose(bank[:, t, :], gated[e][:, t * P : (t + 1) * P], identity[:])
-
-        def empty(e, bank, lo, hi):
-            nc.scalar.copy(results[:, lo:hi, e * C : (e + 1) * C], bank[:, lo:hi, :])
+            emptied = empty("results%d_%d" % (e, lo), bank, lo, hi, tag)
+            for t in range(lo, hi):
+                results[e, t] = emptied[:, t - lo, :]
 
         def scatter(t, lo, hi):
-            entries = dst_sb[:, lo * LIST_COLS : hi * LIST_COLS]
-            cols = slice(lo * C, hi * C)
-            if lo not in gated:
-                nc.vector.tensor_tensor(windows[t][:].indirect(entries), results[:, t, cols], gates[:, cols], MULT)
+            into = windows[t][:].indirect(dst_sb[:, lo * LIST_COLS : hi * LIST_COLS])
+            if lo in gated:
+                nc.vector.tensor_copy(into, results[lo, t])
             else:
-                nc.vector.tensor_copy(windows[t][:].indirect(entries), results[:, t, cols])
+                nc.vector.tensor_tensor(into, results[lo, t], gates[:, lo * C : hi * C], MULT)
             if hi == E:
                 nc.sync.dma_start(out[t * P : (t + 1) * P, :], windows[t][:])
 
-        def scatter_all(lo, hi):
-            for t in range(NT):
-                scatter(t, lo, hi)
-
-        def last_pair(t, bank):
-            for e in range(E - 2, E):
-                h_words, h_scales = quantised[e]
-                nc.tensor.matmul_mx(
-                    out=bank[:, e - (E - 2), :],
-                    lhsT=words["w2"][:, e, 2 * P * t : 2 * P * (t + 1)].bitcast(FP4X4),
-                    lhsT_scale=planes["w2", 1][:, e - HALF, P * t : P * (t + 1)],
-                    rhs=h_words.bitcast(FP8X4),
-                    rhs_scale=h_scales,
-                    start=True,
-                    stop=True,
-                )
-            nc.scalar.copy(results[:, t, (E - 2) * C :].rearrange("p (e c) -> p e c", c=C), bank[:, 0:2, :])
-            scatter(t, E - 2, E)
-
-        a_banks, b_banks = pairs["w1"], pairs["w3"]
-        low, high = slice(0, 2), slice(2, NT)
-        for e in range(2):
-            first_layer(e)
-            product(e)
-        for e in range(2):
-            turn(e, banks[e][:, low, :])
-            quantise(e, banks[e][:, low, :])
-        second_layer(0, banks[0], (0, 1))
-        second_layer(0, banks[1], (1, NT))
-        first_layer(2)
-        product(2)
-        scatter_all(0, 1)
-        turn(2, banks[0][:, low, :])
-        quantise(2, banks[0][:, low, :])
-        gated_by_slot(1, a_banks[1])
-        for bank, part in zip(banks, (low, high)):
-            turn_back(1, bank, part.start, part.stop)
-            empty(1, bank, part.start, part.stop)
-        scatter_all(1, 2)
-        for e in (3, 4):
-            first_layer(e)
-            product(e)
-        gated_by_slot(2, banks[1])
+        halves = (slice(0, 1), slice(1, 2))
+        first_sum("w1", 0, banks[0])
+        first_sum("w3", 0, banks[1])
+        sigmoid(0, banks[0], halves)
+        product_on_vector(0, banks[1], halves)
+        first_sum("w1", 1, banks[2])
+        first_sum("w3", 1, banks[3])
+        sigmoid(1, banks[2])
+        product_on_vector(1, banks[3])
+        turn(0, banks[4])
+        grouped[0] = sbuf("grouped0", [P, 4 * C], BF16)
+        group(0, banks[4], grouped[0][:], nc.vector.tensor_copy)
+        quantise(0, 1, grouped[0][:])
+        by_windows(0, banks[7], 0, 1)
+        first_sum("w1", 2, banks[6])
+        first_sum("w3", 2, banks[1])
+        sigmoid(2, banks[6])
+        turn(1, banks[5])
+        grouped[1] = sbuf("grouped1", [P, 4 * C], BF16)
+        group(1, banks[5], grouped[1][:])
+        by_windows(0, banks[0], 1, NT - 1)
+        product_on_vector(2, banks[1], tag="grouped0")
+        quantise(1, 2, grouped[1][:])
+        for t in range(NT - 1):
+            scatter(t, 0, 1)
+        turn(2, banks[7])
+        grouped[2] = sbuf("grouped2", [P, 4 * C], BF16)
+        group(2, banks[7], grouped[2][:])
+        quantise(2, 3, grouped[2][:])
+        by_windows(0, banks[4], NT - 1, NT, tag="grouped0")
+        scatter(NT - 1, 0, 1)
+        gated_by_slot(1, banks[2])
+        first_sum("w3", 3, banks[1])
+        first_sum("w1", 3, banks[6])
+        sigmoid(3, banks[6])
+        turn_back(1, banks[5], 0, 2)
+        turn_back(1, banks[3], 2, NT)
+        empty_b(3, banks[1], tag="gated1")
+        product_on_gpsimd(3, tag="grouped0")
+        for t in range(NT):
+            scatter(t, 1, 2)
+        gated_by_slot(2, banks[7])
+        first_sum("w1", 4, banks[0])
+        first_sum("w3", 4, banks[4])
+        sigmoid(4, banks[0])
+        empty_b(4, banks[4])
+        product_on_gpsimd(4)
+        turn_back(2, banks[2], 0, 2)
         for t in range(2):
-            turn_back(2, banks[t], t, t + 1)
-            empty(2, banks[t], t, t + 1)
             scatter(t, 2, 3)
-        turn(3, banks[0][:, low, :])
-        turn(4, banks[1][:, low, :])
-        turn_back(2, banks[1], 2, NT)
-        quantise(3, banks[0][:, low, :])
-        quantise(4, banks[1][:, low, :])
-        first_layer(5)
-        product(5)
-        empty(2, banks[1], 2, NT)
+        turn(3, banks[5])
+        grouped[3] = sbuf("grouped3", [P, 4 * C], BF16)
+        group(3, banks[5], grouped[3][:])
+        quantise(3, 4, grouped[3][:])
+        first_sum("w1", 5, banks[6])
+        first_sum("w3", 5, banks[3])
+        sigmoid(5, banks[6])
+        empty_b(5, banks[3])
+        product_on_gpsimd(5, tag="grouped3")
+        turn_back(2, banks[1], 2, NT, tag="grouped0")
         for t in range(2, NT):
             scatter(t, 2, 3)
-        second_layer(3, banks[0], (0, 2))
+        by_windows(3, banks[7], 0, 2)
         for t in range(2):
             scatter(t, 3, 4)
-        turn(5, banks[0][:, low, :])
-        products(3, banks[0], 2, NT)
-        quantise(5, banks[0][:, low, :])
-        empty(3, banks[0], 2, NT)
+        pair = sbuf("grouped4", [P, 2, 4 * C], BF16)
+        turn(4, banks[0])
+        group(4, banks[0], pair[:, 0, :])
+        turn(5, banks[1])
+        group(5, banks[1], pair[:, 1, :])
+        quantise(4, 6, pair[:].rearrange("p e c -> p (e c)"))
+        by_windows(3, banks[6], 2, NT, tag="grouped3")
         for t in range(2, NT):
             scatter(t, 3, 4)
         for t in range(NT):
-            last_pair(t, (a_banks + b_banks)[t])
+            by_experts(t, banks[2 + t], 4, E)
+            scatter(t, 4, E)

@@ -67,13 +67,13 @@ def tile_moe_two_glu_sigmoid_kernel(
         dram_words = {"w1": w1_words, "w3": w3_words, "w2": w2_words}
         dram_scales = {"w1": w1_scales, "w3": w3_scales, "w2": w2_scales}
 
-        def load_plane(plane, rows, queue=nc.sync):
-            for r in range(PLANE_ROWS):
-                queue.dma_start(plane[r:P:32], rows[r])
+        def load_plane(plane, rows, lo=0, hi=PLANE_ROWS):
+            for r in range(lo, hi):
+                nc.sync.dma_start(plane[r:P:32], rows[r])
 
-        def load_weight_plane(name, half, queue=nc.sync):
+        def load_weight_plane(name, half, lo=0, hi=PLANE_ROWS):
             rows = dram_scales[name].bitcast(I32)[half * HALF : (half + 1) * HALF]
-            load_plane(planes[name, half][:].bitcast(I32), rows.rearrange("e s (q r) n -> r q (e s) n", r=PLANE_ROWS), queue)
+            load_plane(planes[name, half][:].bitcast(I32), rows.rearrange("e s (q r) n -> r q (e s) n", r=PLANE_ROWS), lo, hi)
 
         def load_words(name, lo, hi, queue=nc.sync):
             rows = dram_words[name].bitcast(I32)[lo:hi].rearrange("e s p b -> p (e s) b")
@@ -104,18 +104,16 @@ def tile_moe_two_glu_sigmoid_kernel(
         load_weight_plane("w2", 0)
         load_words("w2", 0, 2)
         nc.sync.dma_start(dst_sb[:], dst)
-        load_gates(0, 1)
+        load_gates(0, 2)
         load_weight_plane("w1", 1)
+        load_words("w1", 3, 4)
         load_weight_plane("w3", 1)
-        load_weight_plane("w2", 1)
         load_words("w3", 3, 4)
         load_slot_gates(1, HALF)
-        load_words("w1", 3, 4)
         load_words("w2", 2, 3)
-        load_words("w1", 4, 5)
-        load_words("w3", 4, 5)
-        load_words("w1", 5, 6)
-        load_words("w3", 5, 6)
+        load_words("w1", 4, E)
+        load_words("w3", 4, E)
+        load_weight_plane("w2", 1)
         load_words("w2", HALF, E)
         load_gates(HALF, E)
 
@@ -148,6 +146,7 @@ def tile_moe_two_glu_sigmoid_kernel(
         grouped = {}
         quantised = {}
         gated = {}
+        already_gated = set()
         results = {}
 
         def flat(bank):
@@ -233,30 +232,35 @@ def tile_moe_two_glu_sigmoid_kernel(
                 second_sum(e, t, bank[:, e - lo, :])
             results[lo, t] = empty("results%d_%d" % (lo, t), bank, 0, hi - lo)[:].rearrange("p e c -> p (e c)")
 
-        def gated_by_slot(e, bank):
+        def gated_by_slot(e, bank, cuts=(0, NT)):
             h_words, h_scales = quantised[e]
-            nc.tensor.matmul_mx(
-                out=flat(bank),
-                lhsT=h_words.bitcast(FP8X4),
-                lhsT_scale=h_scales,
-                rhs=words["w2"][:, e, :].bitcast(FP4X4),
-                rhs_scale=planes["w2", e // HALF][:, e % HALF, :],
-                start=True,
-                stop=True,
-            )
+            for lo, hi in zip(cuts, cuts[1:]):
+                nc.tensor.matmul_mx(
+                    out=flat(bank)[:, P * lo : P * hi],
+                    lhsT=h_words.bitcast(FP8X4),
+                    lhsT_scale=h_scales,
+                    rhs=words["w2"][:, e, 2 * P * lo : 2 * P * hi].bitcast(FP4X4),
+                    rhs_scale=planes["w2", e // HALF][:, e % HALF, P * lo : P * hi],
+                    start=True,
+                    stop=True,
+                )
             gated[e] = sbuf("gated%d" % e, [P, N], F32)
-            nc.scalar.activation(gated[e][:], flat(bank), COPY, scale=slot_gates[:, e : e + 1])
+            cols = slice(P * cuts[0], P * cuts[-1])
+            nc.scalar.activation(gated[e][:, cols], flat(bank)[:, cols], COPY, scale=slot_gates[:, e : e + 1])
+            already_gated.update((e, t) for t in range(cuts[0], cuts[-1]))
 
-        def turn_back(e, bank, lo, hi, tag=None):
+        def turn_back(e, bank, lo, hi):
             for t in range(lo, hi):
                 nc.tensor.transpose(bank[:, t, :], gated[e][:, t * P : (t + 1) * P], identity[:])
+
+        def empty_windows(e, bank, lo, hi, tag=None):
             emptied = empty("results%d_%d" % (e, lo), bank, lo, hi, tag)
             for t in range(lo, hi):
                 results[e, t] = emptied[:, t - lo, :]
 
         def scatter(t, lo, hi):
             into = windows[t][:].indirect(dst_sb[:, lo * LIST_COLS : hi * LIST_COLS])
-            if lo in gated:
+            if (lo, t) in already_gated:
                 nc.vector.tensor_copy(into, results[lo, t])
             else:
                 nc.vector.tensor_tensor(into, results[lo, t], gates[:, lo * C : hi * C], MULT)
@@ -292,51 +296,58 @@ def tile_moe_two_glu_sigmoid_kernel(
         grouped[2] = sbuf("grouped2", [P, 4 * C], BF16)
         group(2, banks[7], grouped[2][:])
         quantise(2, 3, grouped[2][:])
-        by_windows(0, banks[4], NT - 1, NT, tag="grouped0")
+        direct = ((0, 3), (1, 0), (1, 1))
+        for place, (e, t) in enumerate(direct):
+            second_sum(e, t, banks[4][:, place, :])
+        emptied = empty("results_direct", banks[4], 0, len(direct), tag="grouped0")
+        for place, (e, t) in enumerate(direct):
+            results[e, t] = emptied[:, place, :]
         scatter(NT - 1, 0, 1)
-        gated_by_slot(1, banks[2])
-        first_sum("w3", 3, banks[1])
-        first_sum("w1", 3, banks[6])
-        sigmoid(3, banks[6])
-        turn_back(1, banks[5], 0, 2)
-        turn_back(1, banks[3], 2, NT)
-        empty_b(3, banks[1], tag="gated1")
-        product_on_gpsimd(3, tag="grouped0")
+        gated_by_slot(1, banks[2], (2, NT))
+        turn_back(1, banks[5], 2, NT)
+        empty_windows(1, banks[5], 2, NT)
         for t in range(NT):
             scatter(t, 1, 2)
+        first_sum("w1", 3, banks[6])
+        first_sum("w3", 3, banks[1])
+        sigmoid(3, banks[6])
+        empty_b(3, banks[1])
+        product_on_gpsimd(3, tag="grouped0")
         gated_by_slot(2, banks[7])
         first_sum("w1", 4, banks[0])
-        first_sum("w3", 4, banks[4])
         sigmoid(4, banks[0])
+        first_sum("w3", 4, banks[4])
         empty_b(4, banks[4])
         product_on_gpsimd(4)
         turn_back(2, banks[2], 0, 2)
+        turn_back(2, banks[1], 2, NT)
+        empty_windows(2, banks[2], 0, 2)
         for t in range(2):
             scatter(t, 2, 3)
-        turn(3, banks[5])
+        turn(3, banks[2])
         grouped[3] = sbuf("grouped3", [P, 4 * C], BF16)
-        group(3, banks[5], grouped[3][:])
+        group(3, banks[2], grouped[3][:])
         quantise(3, 4, grouped[3][:])
-        first_sum("w1", 5, banks[6])
+        empty_windows(2, banks[1], 2, NT, tag="grouped0")
+        first_sum("w1", 5, banks[0])
         first_sum("w3", 5, banks[3])
-        sigmoid(5, banks[6])
+        sigmoid(5, banks[0])
         empty_b(5, banks[3])
         product_on_gpsimd(5, tag="grouped3")
-        turn_back(2, banks[1], 2, NT, tag="grouped0")
         for t in range(2, NT):
             scatter(t, 2, 3)
         by_windows(3, banks[7], 0, 2)
         for t in range(2):
             scatter(t, 3, 4)
         pair = sbuf("grouped4", [P, 2, 4 * C], BF16)
-        turn(4, banks[0])
-        group(4, banks[0], pair[:, 0, :])
-        turn(5, banks[1])
-        group(5, banks[1], pair[:, 1, :])
+        turn(4, banks[5])
+        group(4, banks[5], pair[:, 0, :])
+        turn(5, banks[4])
+        group(5, banks[4], pair[:, 1, :])
         quantise(4, 6, pair[:].rearrange("p e c -> p (e c)"))
         by_windows(3, banks[6], 2, NT, tag="grouped3")
         for t in range(2, NT):
             scatter(t, 3, 4)
         for t in range(NT):
-            by_experts(t, banks[2 + t], 4, E)
+            by_experts(t, banks[t], 4, E)
             scatter(t, 4, E)

@@ -23,7 +23,10 @@ NT = N // P
 LIST_COLS = C // 16
 PLANE_ROWS = 4
 HALF = E // 2
+FIRST = 2
 BANKS = 8
+WHOLE = (slice(0, 2),)
+BY_U = (slice(0, 1), slice(1, 2))
 
 
 def tile_moe_two_glu_sigmoid_kernel(
@@ -47,8 +50,8 @@ def tile_moe_two_glu_sigmoid_kernel(
             words[name] = sbuf(name + "_words", [P, E, 2 * H], U8)
             for half in range(2):
                 planes[name, half] = sbuf("%s_plane%d" % (name, half), [P, HALF, H], U8)
-        zero = sbuf("zero", [P, 8], F32)
-        warm = sbuf("warm", [P, 8], F32)
+        zero = sbuf("zero", [P, 1], F32)
+        warm = sbuf("warm", [P, 1], F32)
         gates = sbuf("gates", [P, E * C], F32)
         slot_gates = sbuf("slot_gates", [P, E], F32)
         windows = [sbuf("window%d" % t, [P, T], F32) for t in range(NT)]
@@ -57,7 +60,7 @@ def tile_moe_two_glu_sigmoid_kernel(
 
         nc.vector.memset(zero[:], 0.0)
         nc.vector.memset(x_plane[:].bitcast(I32), 0)
-        nc.scalar.activation(warm[:, 0:1], zero[:, 0:1], SIGMOID)
+        nc.scalar.activation(warm[:], zero[:], SIGMOID)
         for half in range(2):
             for name in ("w1", "w3", "w2"):
                 nc.vector.memset(planes[name, half][:].bitcast(I32), 0)
@@ -67,52 +70,42 @@ def tile_moe_two_glu_sigmoid_kernel(
         dram_words = {"w1": w1_words, "w3": w3_words, "w2": w2_words}
         dram_scales = {"w1": w1_scales, "w3": w3_scales, "w2": w2_scales}
 
-        def load_plane(plane, rows, lo=0, hi=PLANE_ROWS):
-            for r in range(lo, hi):
+        def load_plane(plane, rows):
+            for r in range(PLANE_ROWS):
                 nc.sync.dma_start(plane[r:P:32], rows[r])
 
-        def load_weight_plane(name, half, lo=0, hi=PLANE_ROWS):
+        def load_weight_plane(name, half):
             rows = dram_scales[name].bitcast(I32)[half * HALF : (half + 1) * HALF]
-            load_plane(planes[name, half][:].bitcast(I32), rows.rearrange("e s (q r) n -> r q (e s) n", r=PLANE_ROWS), lo, hi)
+            load_plane(planes[name, half][:].bitcast(I32), rows.rearrange("e s (q r) n -> r q (e s) n", r=PLANE_ROWS))
 
-        def load_words(name, lo, hi, queue=nc.sync):
+        def load_words(name, lo, hi):
             rows = dram_words[name].bitcast(I32)[lo:hi].rearrange("e s p b -> p (e s) b")
-            queue.dma_start(words[name][:, lo:hi, :].bitcast(I32), rows)
-
-        def load_x(queue=nc.sync):
-            queue.dma_start(x_sb[:], x_words[0].rearrange("p n t -> p (n t)").bitcast(I32))
-
-        def load_x_plane():
-            load_plane(x_plane[:].bitcast(I32), x_scales.bitcast(I32).rearrange("o (q r) n -> r q (o n)", r=PLANE_ROWS))
+            nc.sync.dma_start(words[name][:, lo:hi, :].bitcast(I32), rows)
 
         def load_gates(lo, hi):
             nc.sync.dma_start(gates[:, lo * C : hi * C], gate[0:P, lo * C : hi * C])
 
-        def load_slot_gates(lo, hi):
-            with nc.allow_non_contiguous_dma(reason="one gate value a slot, slots on the partitions"):
-                nc.sync.dma_start(slot_gates[:, lo:hi], gate[0, lo * C : hi * C].rearrange("(e c) -> c e", c=C))
-
-        load_x()
+        nc.sync.dma_start(x_sb[:], x_words[0].rearrange("p n t -> p (n t)").bitcast(I32))
         nc.sync.dma_start(offs_sb[:], offs)
-        load_x_plane()
-        load_words("w1", 0, 2)
+        load_plane(x_plane[:].bitcast(I32), x_scales.bitcast(I32).rearrange("o (q r) n -> r q (o n)", r=PLANE_ROWS))
+        load_words("w1", 0, FIRST)
         load_weight_plane("w1", 0)
-        load_words("w3", 0, 2)
+        load_words("w3", 0, 1)
         load_weight_plane("w3", 0)
-        load_words("w1", 2, 3)
-        load_words("w3", 2, 3)
+        load_words("w3", 1, HALF)
+        load_words("w1", FIRST, HALF)
         load_weight_plane("w2", 0)
         load_words("w2", 0, 2)
         nc.sync.dma_start(dst_sb[:], dst)
         load_gates(0, 2)
-        load_weight_plane("w1", 1)
-        load_words("w1", 3, 4)
-        load_weight_plane("w3", 1)
-        load_words("w3", 3, 4)
-        load_slot_gates(1, HALF)
-        load_words("w2", 2, 3)
-        load_words("w1", 4, E)
-        load_words("w3", 4, E)
+        for name in ("w1", "w3"):
+            load_weight_plane(name, 1)
+            load_words(name, HALF, HALF + 1)
+        with nc.allow_non_contiguous_dma(reason="one gate value a slot, slots on the partitions"):
+            nc.sync.dma_start(slot_gates[:, 1:HALF], gate[0, C : HALF * C].rearrange("(e c) -> c e", c=C))
+        load_words("w2", 2, HALF)
+        for name in ("w1", "w3"):
+            load_words(name, HALF + 1, E)
         load_weight_plane("w2", 1)
         load_words("w2", HALF, E)
         load_gates(HALF, E)
@@ -120,34 +113,27 @@ def tile_moe_two_glu_sigmoid_kernel(
         slot_words = {}
         slot_scales = {}
 
-        def gather(into, name, dtype, window, lo, hi, tag=None):
+        def gather(into, name, dtype, source, lo, hi, tag=None):
             gathered = sbuf("%s%d" % (name, lo), [P, (hi - lo) * C], dtype, tag)
-            nc.vector.tensor_copy(gathered[:], window.indirect(offs_sb[:, lo * LIST_COLS : hi * LIST_COLS]))
+            nc.vector.tensor_copy(gathered[:], source.indirect(offs_sb[:, lo * LIST_COLS : hi * LIST_COLS]))
             for e in range(lo, hi):
                 into[e] = gathered[:, (e - lo) * C : (e - lo + 1) * C]
 
-        def gather_words(lo, hi, tag=None):
-            gather(slot_words, "slot_words", U32, x_sb[:].bitcast(U32), lo, hi, tag)
-
-        def gather_scales(lo, hi, tag=None):
-            gather(slot_scales, "slot_scales", U8, x_plane[:], lo, hi, tag)
-
-        gather_words(0, 2)
-        gather_scales(0, 2)
-        gather_scales(2, E)
-        gather_words(2, E, "x_plane")
+        gather(slot_words, "slot_words", U32, x_sb[:].bitcast(U32), 0, FIRST)
+        gather(slot_scales, "slot_scales", U8, x_plane[:], 0, FIRST)
+        gather(slot_scales, "slot_scales", U8, x_plane[:], FIRST, E)
+        gather(slot_words, "slot_words", U32, x_sb[:].bitcast(U32), FIRST, E, tag="x_plane")
 
         for t in range(NT - 1):
-            nc.scalar.copy(windows[t][:], zero[:, 0:1].to_broadcast([P, T]))
+            nc.scalar.copy(windows[t][:], zero[:].to_broadcast([P, T]))
 
         sigmoids = {}
         factors = {}
         hidden = {}
-        grouped = {}
         quantised = {}
         gated = {}
-        already_gated = set()
         results = {}
+        is_gated = set()
 
         def flat(bank):
             return bank[:].rearrange("p t c -> p (t c)")
@@ -166,18 +152,18 @@ def tile_moe_two_glu_sigmoid_kernel(
                 stop=True,
             )
 
-        def sigmoid(e, bank, parts=(slice(0, 2),), tag=None):
-            sigmoids[e] = sbuf("sigmoid%d" % e, [P, 2, P, 2], F32, tag)
+        def sigmoid(e, bank, parts=WHOLE):
+            sigmoids[e] = sbuf("sigmoid%d" % e, [P, 2, P, 2], F32)
             for part in parts:
                 nc.scalar.activation(sigmoids[e][:, part], by_pairs(bank)[:, part], SIGMOID)
 
-        def product_on_vector(e, bank, parts=(slice(0, 2),), tag=None):
+        def product_on_vector(e, bank, parts=WHOLE, tag=None):
             hidden[e] = sbuf("hidden%d" % e, [P, 2, P, 2], BF16, tag)
             for part in parts:
                 nc.vector.tensor_tensor(hidden[e][:, part], by_pairs(bank)[:, part], sigmoids[e][:, part], MULT)
 
-        def empty_b(e, bank, tag=None):
-            factors[e] = sbuf("factor%d" % e, [P, 2, P, 2], F32, tag)
+        def empty_b(e, bank):
+            factors[e] = sbuf("factor%d" % e, [P, 2, P, 2], F32)
             nc.scalar.copy(factors[e][:], by_pairs(bank))
 
         def product_on_gpsimd(e, tag=None):
@@ -187,16 +173,16 @@ def tile_moe_two_glu_sigmoid_kernel(
                 hidden[e][:].rearrange(merged), factors[e][:].rearrange(merged), sigmoids[e][:].rearrange(merged), MULT
             )
 
-        def turn(e, bank, at=0):
+        def turn(e, bank):
             value_pairs = hidden[e][:].rearrange("p u q v -> p (u q v)").bitcast(F32)
             for u in range(2):
-                nc.tensor.transpose(bank[:, at + u, :], value_pairs[:, u * P : (u + 1) * P], identity[:])
+                nc.tensor.transpose(bank[:, u, :], value_pairs[:, u * P : (u + 1) * P], identity[:])
 
-        def group(e, bank, into, copy=nc.scalar.copy, at=0):
-            copy(into.bitcast(F32).rearrange("p (c u) -> p c u", u=2), bank[:, at : at + 2, :].rearrange("p u c -> p c u"))
+        def group(bank, into, copy=nc.scalar.copy):
+            copy(into.bitcast(F32).rearrange("p (c u) -> p c u", u=2), bank[:, 0:2, :].rearrange("p u c -> p c u"))
 
-        def quantise(lo, hi, values, tag=None):
-            h_words = sbuf("h_words%d" % lo, [P, (hi - lo) * C], U32, tag)
+        def quantise(lo, hi, values):
+            h_words = sbuf("h_words%d" % lo, [P, (hi - lo) * C], U32)
             h_scales = sbuf("h_scales%d" % lo, [P, (hi - lo) * C], U8)
             nc.vector.quantize_mx(out=h_words[:].bitcast(FP8X4), scales=h_scales[:], in_=values)
             for e in range(lo, hi):
@@ -220,100 +206,100 @@ def tile_moe_two_glu_sigmoid_kernel(
             nc.scalar.copy(emptied[:], bank[:, lo:hi, :])
             return emptied
 
-        def by_windows(e, bank, lo, hi, tag=None):
-            for t in range(lo, hi):
-                second_sum(e, t, bank[:, t, :])
-            emptied = empty("results%d_%d" % (e, lo), bank, lo, hi, tag)
-            for t in range(lo, hi):
-                results[e, t] = emptied[:, t - lo, :]
-
-        def by_experts(t, bank, lo, hi):
-            for e in range(lo, hi):
-                second_sum(e, t, bank[:, e - lo, :])
-            results[lo, t] = empty("results%d_%d" % (lo, t), bank, 0, hi - lo)[:].rearrange("p e c -> p (e c)")
-
-        def gated_by_slot(e, bank, cuts=(0, NT)):
-            h_words, h_scales = quantised[e]
-            for lo, hi in zip(cuts, cuts[1:]):
-                nc.tensor.matmul_mx(
-                    out=flat(bank)[:, P * lo : P * hi],
-                    lhsT=h_words.bitcast(FP8X4),
-                    lhsT_scale=h_scales,
-                    rhs=words["w2"][:, e, 2 * P * lo : 2 * P * hi].bitcast(FP4X4),
-                    rhs_scale=planes["w2", e // HALF][:, e % HALF, P * lo : P * hi],
-                    start=True,
-                    stop=True,
-                )
-            gated[e] = sbuf("gated%d" % e, [P, N], F32)
-            cols = slice(P * cuts[0], P * cuts[-1])
-            nc.scalar.activation(gated[e][:, cols], flat(bank)[:, cols], COPY, scale=slot_gates[:, e : e + 1])
-            already_gated.update((e, t) for t in range(cuts[0], cuts[-1]))
-
-        def turn_back(e, bank, lo, hi):
-            for t in range(lo, hi):
-                nc.tensor.transpose(bank[:, t, :], gated[e][:, t * P : (t + 1) * P], identity[:])
-
         def empty_windows(e, bank, lo, hi, tag=None):
             emptied = empty("results%d_%d" % (e, lo), bank, lo, hi, tag)
             for t in range(lo, hi):
                 results[e, t] = emptied[:, t - lo, :]
 
+        def direct_windows(e, bank, lo, hi, tag=None):
+            for t in range(lo, hi):
+                second_sum(e, t, bank[:, t, :])
+            empty_windows(e, bank, lo, hi, tag)
+
+        def direct_experts(t, bank, lo, hi):
+            for e in range(lo, hi):
+                second_sum(e, t, bank[:, e - lo, :])
+            results[lo, t] = empty("results%d_%d" % (lo, t), bank, 0, hi - lo)[:].rearrange("p e c -> p (e c)")
+
+        def gated_by_slot(e, bank, lo):
+            h_words, h_scales = quantised[e]
+            cols = slice(P * lo, N)
+            nc.tensor.matmul_mx(
+                out=flat(bank)[:, cols],
+                lhsT=h_words.bitcast(FP8X4),
+                lhsT_scale=h_scales,
+                rhs=words["w2"][:, e, 2 * P * lo :].bitcast(FP4X4),
+                rhs_scale=planes["w2", e // HALF][:, e % HALF, cols],
+                start=True,
+                stop=True,
+            )
+            gated[e] = sbuf("gated%d" % e, [P, N], F32)
+            nc.scalar.activation(gated[e][:, cols], flat(bank)[:, cols], COPY, scale=slot_gates[:, e : e + 1])
+            is_gated.update((e, t) for t in range(lo, NT))
+
+        def turn_back(e, bank, lo, hi):
+            for t in range(lo, hi):
+                nc.tensor.transpose(bank[:, t, :], gated[e][:, t * P : (t + 1) * P], identity[:])
+
         def scatter(t, lo, hi):
             into = windows[t][:].indirect(dst_sb[:, lo * LIST_COLS : hi * LIST_COLS])
-            if (lo, t) in already_gated:
+            if (lo, t) in is_gated:
                 nc.vector.tensor_copy(into, results[lo, t])
             else:
                 nc.vector.tensor_tensor(into, results[lo, t], gates[:, lo * C : hi * C], MULT)
             if hi == E:
                 nc.sync.dma_start(out[t * P : (t + 1) * P, :], windows[t][:])
 
-        halves = (slice(0, 1), slice(1, 2))
         first_sum("w1", 0, banks[0])
         first_sum("w3", 0, banks[1])
-        sigmoid(0, banks[0], halves)
-        product_on_vector(0, banks[1], halves)
+        sigmoid(0, banks[0], BY_U)
+        product_on_vector(0, banks[1], BY_U)
         first_sum("w1", 1, banks[2])
         first_sum("w3", 1, banks[3])
         sigmoid(1, banks[2])
         product_on_vector(1, banks[3])
+        first_sum("w3", 2, banks[6])
         turn(0, banks[4])
-        grouped[0] = sbuf("grouped0", [P, 4 * C], BF16)
-        group(0, banks[4], grouped[0][:], nc.vector.tensor_copy)
-        quantise(0, 1, grouped[0][:])
-        by_windows(0, banks[7], 0, 1)
-        first_sum("w1", 2, banks[6])
-        first_sum("w3", 2, banks[1])
-        sigmoid(2, banks[6])
+        grouped0 = sbuf("grouped0", [P, 4 * C], BF16)
+        group(banks[4], grouped0[:], nc.vector.tensor_copy)
+        quantise(0, 1, grouped0[:])
+        direct_windows(0, banks[7], 0, 1)
+
+        first_sum("w1", 2, banks[1])
+        sigmoid(2, banks[1], BY_U)
         turn(1, banks[5])
-        grouped[1] = sbuf("grouped1", [P, 4 * C], BF16)
-        group(1, banks[5], grouped[1][:])
-        by_windows(0, banks[0], 1, NT - 1)
-        product_on_vector(2, banks[1], tag="grouped0")
-        quantise(1, 2, grouped[1][:])
+        grouped1 = sbuf("grouped1", [P, 4 * C], BF16)
+        group(banks[5], grouped1[:])
+        direct_windows(0, banks[0], 1, NT - 1)
+        product_on_vector(2, banks[6], BY_U, tag="grouped0")
+        quantise(1, 2, grouped1[:])
         for t in range(NT - 1):
             scatter(t, 0, 1)
+
         turn(2, banks[7])
-        grouped[2] = sbuf("grouped2", [P, 4 * C], BF16)
-        group(2, banks[7], grouped[2][:])
-        quantise(2, 3, grouped[2][:])
-        direct = ((0, 3), (1, 0), (1, 1))
-        for place, (e, t) in enumerate(direct):
+        grouped2 = sbuf("grouped2", [P, 4 * C], BF16)
+        group(banks[7], grouped2[:])
+        quantise(2, 3, grouped2[:])
+        last_direct = ((0, NT - 1), (1, 0), (1, 1))
+        for place, (e, t) in enumerate(last_direct):
             second_sum(e, t, banks[4][:, place, :])
-        emptied = empty("results_direct", banks[4], 0, len(direct), tag="grouped0")
-        for place, (e, t) in enumerate(direct):
+        emptied = empty("results_direct", banks[4], 0, len(last_direct), tag="grouped0")
+        for place, (e, t) in enumerate(last_direct):
             results[e, t] = emptied[:, place, :]
         scatter(NT - 1, 0, 1)
-        gated_by_slot(1, banks[2], (2, NT))
+
+        gated_by_slot(1, banks[2], 2)
         turn_back(1, banks[5], 2, NT)
         empty_windows(1, banks[5], 2, NT)
         for t in range(NT):
             scatter(t, 1, 2)
-        first_sum("w1", 3, banks[6])
-        first_sum("w3", 3, banks[1])
-        sigmoid(3, banks[6])
-        empty_b(3, banks[1])
+
+        first_sum("w1", 3, banks[1])
+        first_sum("w3", 3, banks[6])
+        sigmoid(3, banks[1])
+        empty_b(3, banks[6])
         product_on_gpsimd(3, tag="grouped0")
-        gated_by_slot(2, banks[7])
+        gated_by_slot(2, banks[7], 0)
         first_sum("w1", 4, banks[0])
         sigmoid(4, banks[0])
         first_sum("w3", 4, banks[4])
@@ -324,10 +310,11 @@ def tile_moe_two_glu_sigmoid_kernel(
         empty_windows(2, banks[2], 0, 2)
         for t in range(2):
             scatter(t, 2, 3)
+
         turn(3, banks[2])
-        grouped[3] = sbuf("grouped3", [P, 4 * C], BF16)
-        group(3, banks[2], grouped[3][:])
-        quantise(3, 4, grouped[3][:])
+        grouped3 = sbuf("grouped3", [P, 4 * C], BF16)
+        group(banks[2], grouped3[:])
+        quantise(3, 4, grouped3[:])
         empty_windows(2, banks[1], 2, NT, tag="grouped0")
         first_sum("w1", 5, banks[0])
         first_sum("w3", 5, banks[3])
@@ -336,18 +323,20 @@ def tile_moe_two_glu_sigmoid_kernel(
         product_on_gpsimd(5, tag="grouped3")
         for t in range(2, NT):
             scatter(t, 2, 3)
-        by_windows(3, banks[7], 0, 2)
+
+        direct_windows(3, banks[7], 0, 1)
+        direct_windows(3, banks[0], 1, 2)
         for t in range(2):
             scatter(t, 3, 4)
-        pair = sbuf("grouped4", [P, 2, 4 * C], BF16)
-        turn(4, banks[5])
-        group(4, banks[5], pair[:, 0, :])
-        turn(5, banks[4])
-        group(5, banks[4], pair[:, 1, :])
-        quantise(4, 6, pair[:].rearrange("p e c -> p (e c)"))
-        by_windows(3, banks[6], 2, NT, tag="grouped3")
+        grouped_pair = sbuf("grouped4", [P, 2, 4 * C], BF16)
+        for place, bank in enumerate((banks[5], banks[4])):
+            turn(4 + place, bank)
+            group(bank, grouped_pair[:, place, :])
+        quantise(4, E, grouped_pair[:].rearrange("p e c -> p (e c)"))
+        direct_windows(3, banks[6], 2, NT, tag="grouped3")
         for t in range(2, NT):
             scatter(t, 3, 4)
+
         for t in range(NT):
-            by_experts(t, banks[t], 4, E)
+            direct_experts(t, banks[t], 4, E)
             scatter(t, 4, E)

@@ -22,11 +22,8 @@ P = 128
 NT = N // P
 LIST_COLS = C // 16
 PLANE_ROWS = 4
-HALF = E // 2
-FIRST = 2
 BANKS = 8
-WHOLE = (slice(0, 2),)
-BY_U = (slice(0, 1), slice(1, 2))
+PAIR = 2
 
 
 def tile_moe_two_glu_sigmoid_kernel(
@@ -44,16 +41,12 @@ def tile_moe_two_glu_sigmoid_kernel(
         dst_sb = keep.tile([P, E * LIST_COLS], U16, name="dst_sb")
         x_sb = sbuf("x_sb", [P, T], I32)
         x_plane = sbuf("x_plane", [P, T], U8)
-        planes = {}
-        words = {}
-        for name in ("w1", "w3", "w2"):
-            words[name] = sbuf(name + "_words", [P, E, 2 * H], U8)
-            for half in range(2):
-                planes[name, half] = sbuf("%s_plane%d" % (name, half), [P, HALF, H], U8)
+        planes = {name: sbuf(name + "_plane", [P, E, H], U8) for name in ("w1", "w3", "w2")}
+        words = {name: sbuf(name + "_words", [P, E, 2 * H], U8) for name in ("w1", "w3")}
+        w2_sb = [sbuf("w2_words%d" % half, [P, E, H], U8) for half in range(2)]
         zero = sbuf("zero", [P, 1], F32)
         warm = sbuf("warm", [P, 1], F32)
         gates = sbuf("gates", [P, E * C], F32)
-        slot_gates = sbuf("slot_gates", [P, E], F32)
         windows = [sbuf("window%d" % t, [P, T], F32) for t in range(NT)]
         identity = sbuf("identity", [P, P], F32)
         banks = [psum.tile([P, NT, C], F32, name="bank%d" % b) for b in range(BANKS)]
@@ -61,54 +54,41 @@ def tile_moe_two_glu_sigmoid_kernel(
         nc.vector.memset(zero[:], 0.0)
         nc.vector.memset(x_plane[:].bitcast(I32), 0)
         nc.scalar.activation(warm[:], zero[:], SIGMOID)
-        for half in range(2):
-            for name in ("w1", "w3", "w2"):
-                nc.vector.memset(planes[name, half][:].bitcast(I32), 0)
+        for name in ("w1", "w3", "w2"):
+            nc.vector.memset(planes[name][:].bitcast(I32), 0)
         nc.vector.memset(windows[NT - 1][:].bitcast(I32), 0)
         make_identity(nc, identity[:])
 
-        dram_words = {"w1": w1_words, "w3": w3_words, "w2": w2_words}
+        dram_words = {"w1": w1_words, "w3": w3_words}
         dram_scales = {"w1": w1_scales, "w3": w3_scales, "w2": w2_scales}
 
         def load_plane(plane, rows):
             for r in range(PLANE_ROWS):
                 nc.sync.dma_start(plane[r:P:32], rows[r])
 
-        def load_weight_plane(name, half):
-            rows = dram_scales[name].bitcast(I32)[half * HALF : (half + 1) * HALF]
-            load_plane(planes[name, half][:].bitcast(I32), rows.rearrange("e s (q r) n -> r q (e s) n", r=PLANE_ROWS))
+        def load_weight_plane(name):
+            rows = dram_scales[name].bitcast(I32)
+            load_plane(planes[name][:].bitcast(I32), rows.rearrange("e s (q r) n -> r q (e s) n", r=PLANE_ROWS))
 
         def load_words(name, lo, hi):
             rows = dram_words[name].bitcast(I32)[lo:hi].rearrange("e s p b -> p (e s) b")
             nc.sync.dma_start(words[name][:, lo:hi, :].bitcast(I32), rows)
 
-        def load_gates(lo, hi):
-            nc.sync.dma_start(gates[:, lo * C : hi * C], gate[0:P, lo * C : hi * C])
-
         nc.sync.dma_start(x_sb[:], x_words[0].rearrange("p n t -> p (n t)").bitcast(I32))
         nc.sync.dma_start(offs_sb[:], offs)
         load_plane(x_plane[:].bitcast(I32), x_scales.bitcast(I32).rearrange("o (q r) n -> r q (o n)", r=PLANE_ROWS))
-        load_words("w1", 0, FIRST)
-        load_weight_plane("w1", 0)
-        load_words("w3", 0, 1)
-        load_weight_plane("w3", 0)
-        load_words("w3", 1, HALF)
-        load_words("w1", FIRST, HALF)
-        load_weight_plane("w2", 0)
-        load_words("w2", 0, 2)
+        for name in ("w1", "w3"):
+            load_words(name, 0, PAIR)
+            load_weight_plane(name)
+        for lo in range(PAIR, E, PAIR):
+            for name in ("w1", "w3"):
+                load_words(name, lo, lo + PAIR)
+        load_weight_plane("w2")
         nc.sync.dma_start(dst_sb[:], dst)
-        load_gates(0, 2)
-        for name in ("w1", "w3"):
-            load_weight_plane(name, 1)
-            load_words(name, HALF, HALF + 1)
-        with nc.allow_non_contiguous_dma(reason="one gate value a slot, slots on the partitions"):
-            nc.sync.dma_start(slot_gates[:, 1:HALF], gate[0, C : HALF * C].rearrange("(e c) -> c e", c=C))
-        load_words("w2", 2, HALF)
-        for name in ("w1", "w3"):
-            load_words(name, HALF + 1, E)
-        load_weight_plane("w2", 1)
-        load_words("w2", HALF, E)
-        load_gates(HALF, E)
+        nc.sync.dma_start(gates[:], gate[0:P, :])
+        w2_rows = w2_words.bitcast(I32).rearrange("e s p b -> p (e s) b")
+        for half in range(2):
+            nc.sync.dma_start(w2_sb[half][:].bitcast(I32), w2_rows[:, :, half * P : (half + 1) * P])
 
         slot_words = {}
         slot_scales = {}
@@ -119,21 +99,15 @@ def tile_moe_two_glu_sigmoid_kernel(
             for e in range(lo, hi):
                 into[e] = gathered[:, (e - lo) * C : (e - lo + 1) * C]
 
-        gather(slot_words, "slot_words", U32, x_sb[:].bitcast(U32), 0, FIRST)
-        gather(slot_scales, "slot_scales", U8, x_plane[:], 0, FIRST)
-        gather(slot_scales, "slot_scales", U8, x_plane[:], FIRST, E)
-        gather(slot_words, "slot_words", U32, x_sb[:].bitcast(U32), FIRST, E, tag="x_plane")
+        gather(slot_words, "slot_words", U32, x_sb[:].bitcast(U32), 0, PAIR)
+        gather(slot_scales, "slot_scales", U8, x_plane[:], 0, PAIR)
+        gather(slot_scales, "slot_scales", U8, x_plane[:], PAIR, E)
+        gather(slot_words, "slot_words", U32, x_sb[:].bitcast(U32), PAIR, E, tag="x_plane")
 
         for t in range(NT - 1):
             nc.scalar.copy(windows[t][:], zero[:].to_broadcast([P, T]))
 
-        sigmoids = {}
-        factors = {}
-        hidden = {}
         quantised = {}
-        gated = {}
-        results = {}
-        is_gated = set()
 
         def flat(bank):
             return bank[:].rearrange("p t c -> p (t c)")
@@ -147,196 +121,74 @@ def tile_moe_two_glu_sigmoid_kernel(
                 lhsT=slot_words[e].bitcast(FP8X4),
                 lhsT_scale=slot_scales[e],
                 rhs=words[name][:, e, :].bitcast(FP4X4),
-                rhs_scale=planes[name, e // HALF][:, e % HALF, :],
+                rhs_scale=planes[name][:, e, :],
                 start=True,
                 stop=True,
             )
 
-        def sigmoid(e, bank, parts=WHOLE):
-            sigmoids[e] = sbuf("sigmoid%d" % e, [P, 2, P, 2], F32)
-            for part in parts:
-                nc.scalar.activation(sigmoids[e][:, part], by_pairs(bank)[:, part], SIGMOID)
+        hidden = {}
 
-        def product_on_vector(e, bank, parts=WHOLE, tag=None):
-            hidden[e] = sbuf("hidden%d" % e, [P, 2, P, 2], BF16, tag)
-            for part in parts:
-                nc.vector.tensor_tensor(hidden[e][:, part], by_pairs(bank)[:, part], sigmoids[e][:, part], MULT)
+        def first_layer(e):
+            bank_a, bank_b = banks[e % 3], banks[3 + e % 3]
+            first_sum("w1", e, bank_a)
+            first_sum("w3", e, bank_b)
+            sigmoid = sbuf("sigmoid%d" % e, [P, 2, P, 2], F32)
+            nc.scalar.activation(sigmoid[:], by_pairs(bank_a), SIGMOID)
+            hidden[e] = sbuf("hidden%d" % e, [P, 2, P, 2], BF16)
+            nc.vector.tensor_tensor(hidden[e][:], by_pairs(bank_b), sigmoid[:], MULT)
 
-        def empty_b(e, bank):
-            factors[e] = sbuf("factor%d" % e, [P, 2, P, 2], F32)
-            nc.scalar.copy(factors[e][:], by_pairs(bank))
-
-        def product_on_gpsimd(e, tag=None):
-            hidden[e] = sbuf("hidden%d" % e, [P, 2, P, 2], BF16, tag)
-            merged = "p u q v -> p (u q v)"
-            nc.gpsimd.tensor_tensor(
-                hidden[e][:].rearrange(merged), factors[e][:].rearrange(merged), sigmoids[e][:].rearrange(merged), MULT
-            )
-
-        def turn(e, bank):
+        def turn_and_quantise(e):
+            bank = banks[6 + e % 2]
             value_pairs = hidden[e][:].rearrange("p u q v -> p (u q v)").bitcast(F32)
             for u in range(2):
                 nc.tensor.transpose(bank[:, u, :], value_pairs[:, u * P : (u + 1) * P], identity[:])
-
-        def group(bank, into, copy=nc.scalar.copy):
-            copy(into.bitcast(F32).rearrange("p (c u) -> p c u", u=2), bank[:, 0:2, :].rearrange("p u c -> p c u"))
-
-        def quantise(lo, hi, values):
-            h_words = sbuf("h_words%d" % lo, [P, (hi - lo) * C], U32)
-            h_scales = sbuf("h_scales%d" % lo, [P, (hi - lo) * C], U8)
-            nc.vector.quantize_mx(out=h_words[:].bitcast(FP8X4), scales=h_scales[:], in_=values)
-            for e in range(lo, hi):
-                cols = slice((e - lo) * C, (e - lo + 1) * C)
-                quantised[e] = (h_words[:, cols], h_scales[:, cols])
-
-        def second_sum(e, t, into):
-            h_words, h_scales = quantised[e]
-            nc.tensor.matmul_mx(
-                out=into,
-                lhsT=words["w2"][:, e, 2 * P * t : 2 * P * (t + 1)].bitcast(FP4X4),
-                lhsT_scale=planes["w2", e // HALF][:, e % HALF, P * t : P * (t + 1)],
-                rhs=h_words.bitcast(FP8X4),
-                rhs_scale=h_scales,
-                start=True,
-                stop=True,
+            grouped = sbuf("grouped%d" % e, [P, 4 * C], BF16)
+            nc.scalar.copy(
+                grouped[:].bitcast(F32).rearrange("p (c u) -> p c u", u=2), bank[:, 0:2, :].rearrange("p u c -> p c u")
             )
+            h_words = sbuf("h_words%d" % e, [P, C], U32)
+            h_scales = sbuf("h_scales%d" % e, [P, C], U8)
+            nc.vector.quantize_mx(out=h_words[:].bitcast(FP8X4), scales=h_scales[:], in_=grouped[:])
+            quantised[e] = (h_words, h_scales)
 
-        def empty(name, bank, lo, hi, tag=None):
-            emptied = sbuf(name, [P, hi - lo, C], F32, tag)
-            nc.scalar.copy(emptied[:], bank[:, lo:hi, :])
-            return emptied
-
-        def empty_windows(e, bank, lo, hi, tag=None):
-            emptied = empty("results%d_%d" % (e, lo), bank, lo, hi, tag)
-            for t in range(lo, hi):
-                results[e, t] = emptied[:, t - lo, :]
-
-        def direct_windows(e, bank, lo, hi, tag=None):
-            for t in range(lo, hi):
-                second_sum(e, t, bank[:, t, :])
-            empty_windows(e, bank, lo, hi, tag)
-
-        def direct_experts(t, bank, lo, hi):
+        def second_sums(t, lo, hi, bank):
             for e in range(lo, hi):
-                second_sum(e, t, bank[:, e - lo, :])
-            results[lo, t] = empty("results%d_%d" % (lo, t), bank, 0, hi - lo)[:].rearrange("p e c -> p (e c)")
+                h_words, h_scales = quantised[e]
+                cols = slice(2 * P * (t % 2), 2 * P * (t % 2 + 1))
+                nc.tensor.matmul_mx(
+                    out=bank[:, e - lo, :],
+                    lhsT=w2_sb[t // 2][:, e, cols].bitcast(FP4X4),
+                    lhsT_scale=planes["w2"][:, e, P * t : P * (t + 1)],
+                    rhs=h_words[:].bitcast(FP8X4),
+                    rhs_scale=h_scales[:],
+                    start=True,
+                    stop=True,
+                )
+            return flat(bank)[:, 0 : (hi - lo) * C]
 
-        def gated_by_slot(e, bank, lo):
-            h_words, h_scales = quantised[e]
-            cols = slice(P * lo, N)
-            nc.tensor.matmul_mx(
-                out=flat(bank)[:, cols],
-                lhsT=h_words.bitcast(FP8X4),
-                lhsT_scale=h_scales,
-                rhs=words["w2"][:, e, 2 * P * lo :].bitcast(FP4X4),
-                rhs_scale=planes["w2", e // HALF][:, e % HALF, cols],
-                start=True,
-                stop=True,
-            )
-            gated[e] = sbuf("gated%d" % e, [P, N], F32)
-            nc.scalar.activation(gated[e][:, cols], flat(bank)[:, cols], COPY, scale=slot_gates[:, e : e + 1])
-            is_gated.update((e, t) for t in range(lo, NT))
-
-        def turn_back(e, bank, lo, hi):
-            for t in range(lo, hi):
-                nc.tensor.transpose(bank[:, t, :], gated[e][:, t * P : (t + 1) * P], identity[:])
-
-        def scatter(t, lo, hi):
+        def piece(t, lo, hi, bank, tag):
+            sums = second_sums(t, lo, hi, bank)
+            staged = sbuf("staged%d_%d" % (t, lo), [P, (hi - lo) * C], F32, tag)
             into = windows[t][:].indirect(dst_sb[:, lo * LIST_COLS : hi * LIST_COLS])
-            if (lo, t) in is_gated:
-                nc.vector.tensor_copy(into, results[lo, t])
+            piece_gates = gates[:, lo * C : hi * C]
+            if t % 2 == 0:
+                nc.vector.tensor_tensor(staged[:], sums, piece_gates, MULT)
+                nc.scalar.activation(into, staged[:], COPY)
             else:
-                nc.vector.tensor_tensor(into, results[lo, t], gates[:, lo * C : hi * C], MULT)
+                nc.scalar.copy(staged[:], sums)
+                nc.vector.tensor_tensor(into, staged[:], piece_gates, MULT)
             if hi == E:
                 nc.sync.dma_start(out[t * P : (t + 1) * P, :], windows[t][:])
 
-        first_sum("w1", 0, banks[0])
-        first_sum("w3", 0, banks[1])
-        sigmoid(0, banks[0], BY_U)
-        product_on_vector(0, banks[1], BY_U)
-        first_sum("w1", 1, banks[2])
-        first_sum("w3", 1, banks[3])
-        sigmoid(1, banks[2])
-        product_on_vector(1, banks[3])
-        first_sum("w3", 2, banks[6])
-        turn(0, banks[4])
-        grouped0 = sbuf("grouped0", [P, 4 * C], BF16)
-        group(banks[4], grouped0[:], nc.vector.tensor_copy)
-        quantise(0, 1, grouped0[:])
-        direct_windows(0, banks[7], 0, 1)
+        first_layer(0)
+        for e in range(1, E):
+            first_layer(e)
+            turn_and_quantise(e - 1)
+        turn_and_quantise(E - 1)
 
-        first_sum("w1", 2, banks[1])
-        sigmoid(2, banks[1], BY_U)
-        turn(1, banks[5])
-        grouped1 = sbuf("grouped1", [P, 4 * C], BF16)
-        group(banks[5], grouped1[:])
-        direct_windows(0, banks[0], 1, NT - 1)
-        product_on_vector(2, banks[6], BY_U, tag="grouped0")
-        quantise(1, 2, grouped1[:])
-        for t in range(NT - 1):
-            scatter(t, 0, 1)
-
-        turn(2, banks[7])
-        grouped2 = sbuf("grouped2", [P, 4 * C], BF16)
-        group(banks[7], grouped2[:])
-        quantise(2, 3, grouped2[:])
-        last_direct = ((0, NT - 1), (1, 0), (1, 1))
-        for place, (e, t) in enumerate(last_direct):
-            second_sum(e, t, banks[4][:, place, :])
-        emptied = empty("results_direct", banks[4], 0, len(last_direct), tag="grouped0")
-        for place, (e, t) in enumerate(last_direct):
-            results[e, t] = emptied[:, place, :]
-        scatter(NT - 1, 0, 1)
-
-        gated_by_slot(1, banks[2], 2)
-        turn_back(1, banks[5], 2, NT)
-        empty_windows(1, banks[5], 2, NT)
-        for t in range(NT):
-            scatter(t, 1, 2)
-
-        first_sum("w1", 3, banks[1])
-        first_sum("w3", 3, banks[6])
-        sigmoid(3, banks[1])
-        empty_b(3, banks[6])
-        product_on_gpsimd(3, tag="grouped0")
-        gated_by_slot(2, banks[7], 0)
-        first_sum("w1", 4, banks[0])
-        sigmoid(4, banks[0])
-        first_sum("w3", 4, banks[4])
-        empty_b(4, banks[4])
-        product_on_gpsimd(4)
-        turn_back(2, banks[2], 0, 2)
-        turn_back(2, banks[1], 2, NT)
-        empty_windows(2, banks[2], 0, 2)
-        for t in range(2):
-            scatter(t, 2, 3)
-
-        turn(3, banks[2])
-        grouped3 = sbuf("grouped3", [P, 4 * C], BF16)
-        group(banks[2], grouped3[:])
-        quantise(3, 4, grouped3[:])
-        empty_windows(2, banks[1], 2, NT, tag="grouped0")
-        first_sum("w1", 5, banks[0])
-        first_sum("w3", 5, banks[3])
-        sigmoid(5, banks[0])
-        empty_b(5, banks[3])
-        product_on_gpsimd(5, tag="grouped3")
-        for t in range(2, NT):
-            scatter(t, 2, 3)
-
-        direct_windows(3, banks[7], 0, 1)
-        direct_windows(3, banks[0], 1, 2)
-        for t in range(2):
-            scatter(t, 3, 4)
-        grouped_pair = sbuf("grouped4", [P, 2, 4 * C], BF16)
-        for place, bank in enumerate((banks[5], banks[4])):
-            turn(4 + place, bank)
-            group(bank, grouped_pair[:, place, :])
-        quantise(4, E, grouped_pair[:].rearrange("p e c -> p (e c)"))
-        direct_windows(3, banks[6], 2, NT, tag="grouped3")
-        for t in range(2, NT):
-            scatter(t, 3, 4)
-
-        for t in range(NT):
-            direct_experts(t, banks[t], 4, E)
-            scatter(t, 4, E)
+        step = 0
+        for half in range(2):
+            for lo in range(0, E, PAIR):
+                piece(2 * half, lo, lo + PAIR, banks[step % 2], "for_scalar%d" % (step % 2))
+                piece(2 * half + 1, lo, lo + PAIR, banks[3 + step % 2], "for_vector%d" % (step % 2))
+                step = step + 1

@@ -24,6 +24,8 @@ LIST_COLS = C // 16
 PLANE_ROWS = 4
 BANKS = 8
 PAIR = 2
+A_BANKS = (0, 1, 2, 6, 7, 0)
+B_BANKS = (3, 4, 5, 3, 4, 5)
 
 
 def tile_moe_two_glu_sigmoid_kernel(
@@ -42,8 +44,7 @@ def tile_moe_two_glu_sigmoid_kernel(
         x_sb = sbuf("x_sb", [P, T], I32)
         x_plane = sbuf("x_plane", [P, T], U8)
         planes = {name: sbuf(name + "_plane", [P, E, H], U8) for name in ("w1", "w3", "w2")}
-        words = {name: sbuf(name + "_words", [P, E, 2 * H], U8) for name in ("w1", "w3")}
-        w2_sb = [sbuf("w2_words%d" % half, [P, E, H], U8) for half in range(2)]
+        words = {name: sbuf(name + "_words", [P, E, 2 * H], U8) for name in ("w1", "w3", "w2")}
         zero = sbuf("zero", [P, 1], F32)
         warm = sbuf("warm", [P, 1], F32)
         gates = sbuf("gates", [P, E * C], F32)
@@ -56,10 +57,10 @@ def tile_moe_two_glu_sigmoid_kernel(
         nc.scalar.activation(warm[:], zero[:], SIGMOID)
         for name in ("w1", "w3", "w2"):
             nc.vector.memset(planes[name][:].bitcast(I32), 0)
-        nc.vector.memset(windows[NT - 1][:].bitcast(I32), 0)
         make_identity(nc, identity[:])
+        nc.gpsimd.memset(windows[NT - 1][:].bitcast(I32), 0)
 
-        dram_words = {"w1": w1_words, "w3": w3_words}
+        dram_words = {"w1": w1_words, "w3": w3_words, "w2": w2_words}
         dram_scales = {"w1": w1_scales, "w3": w3_scales, "w2": w2_scales}
 
         def load_plane(plane, rows):
@@ -78,17 +79,17 @@ def tile_moe_two_glu_sigmoid_kernel(
         nc.sync.dma_start(offs_sb[:], offs)
         load_plane(x_plane[:].bitcast(I32), x_scales.bitcast(I32).rearrange("o (q r) n -> r q (o n)", r=PLANE_ROWS))
         for name in ("w1", "w3"):
-            load_words(name, 0, PAIR)
+            load_words(name, 0, 3)
             load_weight_plane(name)
-        for lo in range(PAIR, E, PAIR):
-            for name in ("w1", "w3"):
-                load_words(name, lo, lo + PAIR)
+        load_words("w1", 3, 6)
+        load_words("w3", 3, 6)
         load_weight_plane("w2")
         nc.sync.dma_start(dst_sb[:], dst)
-        nc.sync.dma_start(gates[:], gate[0:P, :])
-        w2_rows = w2_words.bitcast(I32).rearrange("e s p b -> p (e s) b")
-        for half in range(2):
-            nc.sync.dma_start(w2_sb[half][:].bitcast(I32), w2_rows[:, :, half * P : (half + 1) * P])
+        nc.sync.dma_start(gates[:, : 4 * C], gate[0:P, : 4 * C])
+        load_words("w2", 0, 2)
+        load_words("w2", 2, 4)
+        nc.sync.dma_start(gates[:, 4 * C :], gate[0:P, 4 * C :])
+        load_words("w2", 4, 6)
 
         slot_words = {}
         slot_scales = {}
@@ -99,10 +100,10 @@ def tile_moe_two_glu_sigmoid_kernel(
             for e in range(lo, hi):
                 into[e] = gathered[:, (e - lo) * C : (e - lo + 1) * C]
 
-        gather(slot_words, "slot_words", U32, x_sb[:].bitcast(U32), 0, PAIR)
-        gather(slot_scales, "slot_scales", U8, x_plane[:], 0, PAIR)
-        gather(slot_scales, "slot_scales", U8, x_plane[:], PAIR, E)
-        gather(slot_words, "slot_words", U32, x_sb[:].bitcast(U32), PAIR, E, tag="x_plane")
+        gather(slot_words, "slot_words", U32, x_sb[:].bitcast(U32), 0, 3)
+        gather(slot_scales, "slot_scales", U8, x_plane[:], 0, 3)
+        gather(slot_scales, "slot_scales", U8, x_plane[:], 3, E)
+        gather(slot_words, "slot_words", U32, x_sb[:].bitcast(U32), 3, E, tag="x_plane")
 
         for t in range(NT - 1):
             nc.scalar.copy(windows[t][:], zero[:].to_broadcast([P, T]))
@@ -128,67 +129,115 @@ def tile_moe_two_glu_sigmoid_kernel(
 
         hidden = {}
 
-        def first_layer(e):
-            bank_a, bank_b = banks[e % 3], banks[3 + e % 3]
-            first_sum("w1", e, bank_a)
-            first_sum("w3", e, bank_b)
-            sigmoid = sbuf("sigmoid%d" % e, [P, 2, P, 2], F32)
-            nc.scalar.activation(sigmoid[:], by_pairs(bank_a), SIGMOID)
-            hidden[e] = sbuf("hidden%d" % e, [P, 2, P, 2], BF16)
-            nc.vector.tensor_tensor(hidden[e][:], by_pairs(bank_b), sigmoid[:], MULT)
+        sigmoids = {}
 
-        def turn_and_quantise(e):
-            bank = banks[6 + e % 2]
-            value_pairs = hidden[e][:].rearrange("p u q v -> p (u q v)").bitcast(F32)
-            for u in range(2):
-                nc.tensor.transpose(bank[:, u, :], value_pairs[:, u * P : (u + 1) * P], identity[:])
-            grouped = sbuf("grouped%d" % e, [P, 4 * C], BF16)
+        def product(e):
+            bank_b = banks[3 + e % 3]
+            first_sum("w3", e, bank_b)
+            hidden[e] = sbuf("hidden%d" % e, [P, 2, P, 2], BF16)
+            nc.vector.tensor_tensor(hidden[e][:], by_pairs(bank_b), sigmoids[e][:], MULT)
+
+        grouped = {lo: sbuf("grouped%d" % lo, [P, PAIR, 4 * C], BF16) for lo in range(0, E, PAIR)}
+
+        def turn(lo, bank):
+            for place in range(PAIR):
+                value_pairs = hidden[lo + place][:].rearrange("p u q v -> p (u q v)").bitcast(F32)
+                for u in range(2):
+                    nc.tensor.transpose(bank[:, 2 * place + u, :], value_pairs[:, u * P : (u + 1) * P], identity[:])
             nc.scalar.copy(
-                grouped[:].bitcast(F32).rearrange("p (c u) -> p c u", u=2), bank[:, 0:2, :].rearrange("p u c -> p c u")
+                grouped[lo][:].bitcast(F32).rearrange("p e (c u) -> p e c u", u=2),
+                bank[:].rearrange("p (e u) c -> p e c u", u=2),
             )
-            h_words = sbuf("h_words%d" % e, [P, C], U32)
-            h_scales = sbuf("h_scales%d" % e, [P, C], U8)
-            nc.vector.quantize_mx(out=h_words[:].bitcast(FP8X4), scales=h_scales[:], in_=grouped[:])
-            quantised[e] = (h_words, h_scales)
+
+        def quantise(lo, tag=None):
+            hi = lo + PAIR
+            values = grouped[lo][:].rearrange("p e c -> p (e c)")
+            h_words = sbuf("h_words%d" % lo, [P, (hi - lo) * C], U32, tag)
+            h_scales = sbuf("h_scales%d" % lo, [P, (hi - lo) * C], U8)
+            nc.vector.quantize_mx(out=h_words[:].bitcast(FP8X4), scales=h_scales[:], in_=values)
+            for e in range(lo, hi):
+                cols = slice((e - lo) * C, (e - lo + 1) * C)
+                quantised[e] = (h_words[:, cols], h_scales[:, cols])
 
         def second_sums(t, lo, hi, bank):
             for e in range(lo, hi):
                 h_words, h_scales = quantised[e]
-                cols = slice(2 * P * (t % 2), 2 * P * (t % 2 + 1))
                 nc.tensor.matmul_mx(
                     out=bank[:, e - lo, :],
-                    lhsT=w2_sb[t // 2][:, e, cols].bitcast(FP4X4),
+                    lhsT=words["w2"][:, e, 2 * P * t : 2 * P * (t + 1)].bitcast(FP4X4),
                     lhsT_scale=planes["w2"][:, e, P * t : P * (t + 1)],
-                    rhs=h_words[:].bitcast(FP8X4),
-                    rhs_scale=h_scales[:],
+                    rhs=h_words.bitcast(FP8X4),
+                    rhs_scale=h_scales,
                     start=True,
                     stop=True,
                 )
             return flat(bank)[:, 0 : (hi - lo) * C]
 
-        def piece(t, lo, hi, bank, tag):
+        staged = {}
+
+        def stage(t, lo, bank, gated, tag=None, values=None, hi=None):
+            hi = hi or lo + PAIR
             sums = second_sums(t, lo, hi, bank)
-            staged = sbuf("staged%d_%d" % (t, lo), [P, (hi - lo) * C], F32, tag)
-            into = windows[t][:].indirect(dst_sb[:, lo * LIST_COLS : hi * LIST_COLS])
-            piece_gates = gates[:, lo * C : hi * C]
-            if t % 2 == 0:
-                nc.vector.tensor_tensor(staged[:], sums, piece_gates, MULT)
-                nc.scalar.activation(into, staged[:], COPY)
+            if values is None:
+                values = sbuf("staged%d_%d" % (t, lo), [P, (hi - lo) * C], F32, tag)
+            if gated:
+                nc.vector.tensor_tensor(values[:], sums, gates[:, lo * C : hi * C], MULT)
             else:
-                nc.scalar.copy(staged[:], sums)
-                nc.vector.tensor_tensor(into, staged[:], piece_gates, MULT)
+                nc.scalar.copy(values[:], sums)
+            staged[t, lo] = (values, gated)
+
+        def scatter(t, lo, hi=None, values=None):
+            hi = hi or lo + PAIR
+            gated = staged[t, lo][1]
+            if values is None:
+                values = staged[t, lo][0]
+            into = windows[t][:].indirect(dst_sb[:, lo * LIST_COLS : hi * LIST_COLS])
+            if t % 2 == 0:
+                nc.scalar.activation(into, values[:], COPY)
+            elif gated:
+                nc.vector.tensor_copy(into, values[:])
+            else:
+                nc.vector.tensor_tensor(into, values[:], gates[:, lo * C : hi * C], MULT)
             if hi == E:
                 nc.sync.dma_start(out[t * P : (t + 1) * P, :], windows[t][:])
 
-        first_layer(0)
-        for e in range(1, E):
-            first_layer(e)
-            turn_and_quantise(e - 1)
-        turn_and_quantise(E - 1)
+        def sigmoid(e):
+            first_sum("w1", e, banks[A_BANKS[e]])
+            sigmoids[e] = sbuf("sigmoid%d" % e, [P, 2, P, 2], F32)
+            nc.scalar.activation(sigmoids[e][:], by_pairs(banks[A_BANKS[e]]), SIGMOID)
 
-        step = 0
-        for half in range(2):
-            for lo in range(0, E, PAIR):
-                piece(2 * half, lo, lo + PAIR, banks[step % 2], "for_scalar%d" % (step % 2))
-                piece(2 * half + 1, lo, lo + PAIR, banks[3 + step % 2], "for_vector%d" % (step % 2))
-                step = step + 1
+        for e in range(5):
+            sigmoid(e)
+            product(e)
+        turn(0, banks[6])
+        quantise(0, tag="sigmoid4")
+        sigmoid(5)
+        product(5)
+        turn(2, banks[7])
+        quantise(2, tag="sigmoid5")
+        stage(1, 0, banks[1], False)
+        stage(0, 0, banks[2], True)
+        scatter(0, 0)
+        scatter(1, 0)
+        turn(4, banks[1])
+        for_scalar = sbuf("for_scalar", [P, 2, PAIR * C], F32, tag="hidden5")
+        for_vector = sbuf("for_vector", [P, 2, PAIR * C], F32, tag="hidden4")
+        stage(0, 2, banks[0], True, values=for_scalar[:, 0, :])
+        stage(2, 0, banks[3], True, values=for_scalar[:, 1, :])
+        stage(1, 2, banks[6], False, values=for_vector[:, 0, :])
+        stage(3, 0, banks[4], False, values=for_vector[:, 1, :])
+        quantise(4)
+        scatter(0, 2)
+        scatter(1, 2)
+        stage(0, 4, banks[2], True)
+        stage(1, 4, banks[5], False)
+        scatter(2, 0)
+        scatter(3, 0)
+        stage(2, 2, banks[7], True, tag="hidden5")
+        scatter(0, 4)
+        scatter(1, 4)
+        stage(2, 4, banks[2], True)
+        stage(3, 2, banks[6], True, tag="staged1_4", hi=E)
+        scatter(2, 2)
+        scatter(2, 4)
+        scatter(3, 2, E)

@@ -186,13 +186,15 @@ def tile_moe_two_glu_sigmoid_kernel(
                 nc.scalar.copy(values[:], sums)
             staged[t, lo] = (values, gated)
 
-        def scatter(t, lo, hi=None, values=None):
+        def scatter(t, lo, hi=None, values=None, on_scalar=None):
             hi = hi or lo + PAIR
-            gated = staged[t, lo][1]
+            gated = True
             if values is None:
-                values = staged[t, lo][0]
+                values, gated = staged[t, lo]
+            if on_scalar is None:
+                on_scalar = t % 2 == 0
             into = windows[t][:].indirect(dst_sb[:, lo * LIST_COLS : hi * LIST_COLS])
-            if t % 2 == 0:
+            if on_scalar:
                 nc.scalar.activation(into, values[:], COPY)
             elif gated:
                 nc.vector.tensor_copy(into, values[:])
@@ -234,10 +236,11 @@ def tile_moe_two_glu_sigmoid_kernel(
         scatter(2, 0)
         scatter(3, 0)
         stage(2, 2, banks[7], True, tag="hidden5")
-        scatter(0, 4)
+        scatter(0, 4, 5, staged[0, 4][0][:, :C])
         scatter(1, 4)
         stage(2, 4, banks[2], True)
         stage(3, 2, banks[6], True, tag="staged1_4", hi=E)
+        scatter(0, 5, E, staged[0, 4][0][:, C:], on_scalar=False)
         scatter(2, 2)
         scatter(2, 4)
         scatter(3, 2, E)

@@ -48,7 +48,7 @@ def tile_moe_two_glu_sigmoid_kernel(
         zero = sbuf("zero", [P, 1], F32)
         warm = sbuf("warm", [P, 1], F32)
         gates = sbuf("gates", [P, E * C], F32)
-        windows = [sbuf("window%d" % t, [P, T], F32) for t in range(NT)]
+        windows = [sbuf("window%d" % t, [P, T], F32) for t in range(NT - 1)]
         identity = sbuf("identity", [P, P], F32)
         banks = [psum.tile([P, NT, C], F32, name="bank%d" % b) for b in range(BANKS)]
 
@@ -58,7 +58,6 @@ def tile_moe_two_glu_sigmoid_kernel(
         for name in ("w1", "w3", "w2"):
             nc.vector.memset(planes[name][:].bitcast(I32), 0)
         make_identity(nc, identity[:])
-        nc.gpsimd.memset(windows[NT - 1][:].bitcast(I32), 0)
 
         dram_words = {"w1": w1_words, "w3": w3_words, "w2": w2_words}
         dram_scales = {"w1": w1_scales, "w3": w3_scales, "w2": w2_scales}
@@ -105,6 +104,8 @@ def tile_moe_two_glu_sigmoid_kernel(
         gather(slot_scales, "slot_scales", U8, x_plane[:], 3, E)
         gather(slot_words, "slot_words", U32, x_sb[:].bitcast(U32), 3, E, tag="x_plane")
 
+        windows.append(sbuf("window3", [P, T], F32, tag="x_sb"))
+        nc.gpsimd.memset(windows[NT - 1][:].bitcast(I32), 0)
         for t in range(NT - 1):
             nc.scalar.copy(windows[t][:], zero[:].to_broadcast([P, T]))
 

@@ -83,11 +83,11 @@ def tile_moe_two_glu_sigmoid_kernel(
         load_words("w1", 3, 6)
         load_words("w3", 3, 6)
         load_weight_plane("w2")
-        nc.sync.dma_start(dst_sb[:], dst)
-        nc.sync.dma_start(gates[:, : 4 * C], gate[0:P, : 4 * C])
         load_words("w2", 0, 2)
+        nc.sync.dma_start(dst_sb[:], dst)
+        nc.sync.dma_start(gates[:, : 2 * C], gate[0:P, : 2 * C])
         load_words("w2", 2, 4)
-        nc.sync.dma_start(gates[:, 4 * C :], gate[0:P, 4 * C :])
+        nc.sync.dma_start(gates[:, 2 * C :], gate[0:P, 2 * C :])
         load_words("w2", 4, 6)
 
         slot_words = {}
@@ -218,11 +218,11 @@ def tile_moe_two_glu_sigmoid_kernel(
         product(5)
         turn(2, banks[7])
         quantise(2, tag="sigmoid5")
-        stage(1, 0, banks[1], False)
         stage(0, 0, banks[2], True)
+        stage(1, 0, banks[1], False)
         scatter(0, 0)
         scatter(1, 0)
-        turn(4, banks[1])
+        turn(4, banks[2])
         for_scalar = sbuf("for_scalar", [P, 2, PAIR * C], F32, tag="hidden5")
         for_vector = sbuf("for_vector", [P, 2, PAIR * C], F32, tag="hidden4")
         stage(0, 2, banks[0], True, values=for_scalar[:, 0, :])
@@ -232,14 +232,14 @@ def tile_moe_two_glu_sigmoid_kernel(
         quantise(4)
         scatter(0, 2)
         scatter(1, 2)
-        stage(0, 4, banks[2], True)
+        stage(0, 4, banks[1], True)
         stage(1, 4, banks[5], False)
         scatter(2, 0)
         scatter(3, 0)
         stage(2, 2, banks[7], True, tag="hidden5")
         scatter(0, 4, 5, staged[0, 4][0][:, :C])
         scatter(1, 4)
-        stage(2, 4, banks[2], True)
+        stage(2, 4, banks[1], True)
         stage(3, 2, banks[6], True, tag="staged1_4", hi=E)
         scatter(0, 5, E, staged[0, 4][0][:, C:], on_scalar=False)
         scatter(2, 2)

@@ -49,15 +49,18 @@ def tile_moe_two_glu_sigmoid_kernel(
         warm = sbuf("warm", [P, 1], F32)
         gates = sbuf("gates", [P, E * C], F32)
         windows = [sbuf("window%d" % t, [P, T], F32) for t in range(NT - 1)]
-        identity = sbuf("identity", [P, P], F32)
         banks = [psum.tile([P, NT, C], F32, name="bank%d" % b) for b in range(BANKS)]
 
         nc.vector.memset(zero[:], 0.0)
         nc.vector.memset(x_plane[:].bitcast(I32), 0)
         nc.scalar.activation(warm[:], zero[:], SIGMOID)
-        for name in ("w1", "w3", "w2"):
+        for name in ("w1", "w3"):
             nc.vector.memset(planes[name][:].bitcast(I32), 0)
-        make_identity(nc, identity[:])
+
+        nc.scalar.copy(
+            planes["w2"][:].rearrange("p e n -> p (e n)").bitcast(U32),
+            zero[:].bitcast(U32).to_broadcast([P, E * H // 4]),
+        )
 
         dram_words = {"w1": w1_words, "w3": w3_words, "w2": w2_words}
         dram_scales = {"w1": w1_scales, "w3": w3_scales, "w2": w2_scales}
@@ -104,8 +107,8 @@ def tile_moe_two_glu_sigmoid_kernel(
         gather(slot_scales, "slot_scales", U8, x_plane[:], 3, E)
         gather(slot_words, "slot_words", U32, x_sb[:].bitcast(U32), 3, E, tag="x_plane")
 
-        windows.append(sbuf("window3", [P, T], F32, tag="x_sb"))
-        nc.gpsimd.memset(windows[NT - 1][:].bitcast(I32), 0)
+        identity = sbuf("identity", [P, P], F32, tag="x_sb")
+        make_identity(nc, identity[:])
         for t in range(NT - 1):
             nc.scalar.copy(windows[t][:], zero[:].to_broadcast([P, T]))
 
@@ -212,6 +215,8 @@ def tile_moe_two_glu_sigmoid_kernel(
         for e in range(5):
             sigmoid(e)
             product(e)
+        windows.append(sbuf("window3", [P, T], F32, tag="slot_words0"))
+        nc.gpsimd.memset(windows[NT - 1][:].bitcast(I32), 0)
         turn(0, banks[6])
         quantise(0, tag="sigmoid4")
         sigmoid(5)

@@ -80,11 +80,14 @@ def tile_moe_two_glu_sigmoid_kernel(
         nc.sync.dma_start(x_sb[:], x_words[0].rearrange("p n t -> p (n t)").bitcast(I32))
         nc.sync.dma_start(offs_sb[:], offs)
         load_plane(x_plane[:].bitcast(I32), x_scales.bitcast(I32).rearrange("o (q r) n -> r q (o n)", r=PLANE_ROWS))
-        for name in ("w1", "w3"):
-            load_words(name, 0, 3)
-            load_weight_plane(name)
+        load_words("w1", 0, 3)
+        load_weight_plane("w1")
+        load_words("w3", 0, 1)
+        load_weight_plane("w3")
+        load_words("w3", 1, 3)
         load_words("w1", 3, 6)
-        load_words("w3", 3, 6)
+        load_words("w3", 3, 4)
+        load_words("w3", 4, 6)
         load_weight_plane("w2")
         load_words("w2", 0, 2)
         nc.sync.dma_start(dst_sb[:], dst)

@@ -23,9 +23,6 @@ NT = N // P
 LIST_COLS = C // 16
 PLANE_ROWS = 4
 BANKS = 8
-PAIR = 2
-A_BANKS = (0, 1, 2, 6, 7, 0)
-B_BANKS = (3, 4, 5, 3, 4, 5)
 
 
 def tile_moe_two_glu_sigmoid_kernel(
@@ -41,81 +38,61 @@ def tile_moe_two_glu_sigmoid_kernel(
 
         offs_sb = keep.tile([P, E * LIST_COLS], U16, name="offs_sb")
         dst_sb = keep.tile([P, E * LIST_COLS], U16, name="dst_sb")
-        x_sb = sbuf("x_sb", [P, T], I32)
-        x_plane = sbuf("x_plane", [P, T], U8)
-        planes = {name: sbuf(name + "_plane", [P, E, H], U8) for name in ("w1", "w3", "w2")}
-        words = {name: sbuf(name + "_words", [P, E, 2 * H], U8) for name in ("w1", "w3", "w2")}
-        zero = sbuf("zero", [P, 1], F32)
-        warm = sbuf("warm", [P, 1], F32)
-        gates = sbuf("gates", [P, E * C], F32)
-        windows = [sbuf("window%d" % t, [P, T], F32) for t in range(NT - 1)]
         banks = [psum.tile([P, NT, C], F32, name="bank%d" % b) for b in range(BANKS)]
-
-        nc.vector.memset(zero[:], 0.0)
-        nc.vector.memset(x_plane[:].bitcast(I32), 0)
-        nc.scalar.activation(warm[:], zero[:], SIGMOID)
-        for name in ("w1", "w3"):
-            nc.vector.memset(planes[name][:].bitcast(I32), 0)
-
-        nc.scalar.copy(
-            planes["w2"][:].rearrange("p e n -> p (e n)").bitcast(U32),
-            zero[:].bitcast(U32).to_broadcast([P, E * H // 4]),
-        )
-
         dram_words = {"w1": w1_words, "w3": w3_words, "w2": w2_words}
         dram_scales = {"w1": w1_scales, "w3": w3_scales, "w2": w2_scales}
+        zero = sbuf("zero", [P, 1], F32)
+        warm = sbuf("warm", [P, 1], F32)
+        one = sbuf("one", [P, 1], F32)
+        plane_tiles, planes, words, gates, windows = {}, {}, {}, {}, {}
+        slot_words, slot_scales, sigmoids, hidden, grouped, quantised = {}, {}, {}, {}, {}, {}
 
-        def load_plane(plane, rows):
+        def zero_on_scalar(tile, columns):
+            nc.scalar.copy(tile.bitcast(U32), zero[:].bitcast(U32).to_broadcast([P, columns]))
+
+        def new_plane(name, lo, hi, on_scalar=False):
+            tile = sbuf("%s_plane%d" % (name, lo), [P, hi - lo, H], U8)
+            plane_tiles[name, lo] = tile
+            for e in range(lo, hi):
+                planes[name, e] = tile[:, e - lo, :]
+            if on_scalar:
+                zero_on_scalar(tile[:].rearrange("p e n -> p (e n)"), (hi - lo) * H // 4)
+            else:
+                nc.vector.memset(tile[:].bitcast(I32), 0)
+
+        def load_rows(plane, rows):
             for r in range(PLANE_ROWS):
                 nc.sync.dma_start(plane[r:P:32], rows[r])
 
-        def load_weight_plane(name):
-            rows = dram_scales[name].bitcast(I32)
-            load_plane(planes[name][:].bitcast(I32), rows.rearrange("e s (q r) n -> r q (e s) n", r=PLANE_ROWS))
+        def load_plane(name, lo, hi):
+            rows = dram_scales[name].bitcast(I32)[lo:hi].rearrange("e s (q r) n -> r q (e s) n", r=PLANE_ROWS)
+            load_rows(plane_tiles[name, lo][:].bitcast(I32), rows)
 
-        def load_words(name, lo, hi):
+        def load_words(name, lo, hi, t0=0, t1=NT):
+            width = 2 * P * (t1 - t0)
+            tile = sbuf("%s_words%d_%d" % (name, lo, t0), [P, hi - lo, width], U8)
             rows = dram_words[name].bitcast(I32)[lo:hi].rearrange("e s p b -> p (e s) b")
-            nc.sync.dma_start(words[name][:, lo:hi, :].bitcast(I32), rows)
+            nc.sync.dma_start(tile[:].bitcast(I32), rows[:, :, t0 * P // 2 : t1 * P // 2])
+            for e in range(lo, hi):
+                words[name, e] = tile[:, e - lo, :]
+                for t in range(t0, t1):
+                    words[name, e, t] = tile[:, e - lo, 2 * P * (t - t0) : 2 * P * (t - t0 + 1)]
 
-        nc.sync.dma_start(x_sb[:], x_words[0].rearrange("p n t -> p (n t)").bitcast(I32))
-        nc.sync.dma_start(offs_sb[:], offs)
-        load_plane(x_plane[:].bitcast(I32), x_scales.bitcast(I32).rearrange("o (q r) n -> r q (o n)", r=PLANE_ROWS))
-        load_words("w1", 0, 3)
-        load_weight_plane("w1")
-        load_words("w3", 0, 1)
-        load_weight_plane("w3")
-        load_words("w3", 1, 3)
-        load_words("w1", 3, 6)
-        load_words("w3", 3, 4)
-        load_words("w3", 4, 6)
-        load_weight_plane("w2")
-        load_words("w2", 0, 2)
-        nc.sync.dma_start(dst_sb[:], dst)
-        nc.sync.dma_start(gates[:, : 2 * C], gate[0:P, : 2 * C])
-        load_words("w2", 2, 4)
-        nc.sync.dma_start(gates[:, 2 * C :], gate[0:P, 2 * C :])
-        load_words("w2", 4, 6)
+        def load_gates(lo, hi):
+            tile = sbuf("gates%d" % lo, [P, (hi - lo) * C], F32)
+            nc.sync.dma_start(tile[:], gate[0:P, lo * C : hi * C])
+            for e in range(lo, hi):
+                gates[e] = (tile, lo)
 
-        slot_words = {}
-        slot_scales = {}
+        def gates_of(lo, hi):
+            tile, first = gates[lo]
+            return tile[:, (lo - first) * C : (hi - first) * C]
 
         def gather(into, name, dtype, source, lo, hi, tag=None):
             gathered = sbuf("%s%d" % (name, lo), [P, (hi - lo) * C], dtype, tag)
             nc.vector.tensor_copy(gathered[:], source.indirect(offs_sb[:, lo * LIST_COLS : hi * LIST_COLS]))
             for e in range(lo, hi):
                 into[e] = gathered[:, (e - lo) * C : (e - lo + 1) * C]
-
-        gather(slot_words, "slot_words", U32, x_sb[:].bitcast(U32), 0, 3)
-        gather(slot_scales, "slot_scales", U8, x_plane[:], 0, 3)
-        gather(slot_scales, "slot_scales", U8, x_plane[:], 3, E)
-        gather(slot_words, "slot_words", U32, x_sb[:].bitcast(U32), 3, E, tag="x_plane")
-
-        identity = sbuf("identity", [P, P], F32, tag="x_sb")
-        make_identity(nc, identity[:])
-        for t in range(NT - 1):
-            nc.scalar.copy(windows[t][:], zero[:].to_broadcast([P, T]))
-
-        quantised = {}
 
         def flat(bank):
             return bank[:].rearrange("p t c -> p (t c)")
@@ -128,36 +105,35 @@ def tile_moe_two_glu_sigmoid_kernel(
                 out=flat(bank),
                 lhsT=slot_words[e].bitcast(FP8X4),
                 lhsT_scale=slot_scales[e],
-                rhs=words[name][:, e, :].bitcast(FP4X4),
-                rhs_scale=planes[name][:, e, :],
+                rhs=words[name, e].bitcast(FP4X4),
+                rhs_scale=planes[name, e],
                 start=True,
                 stop=True,
             )
 
-        hidden = {}
+        def sigmoid(e, bank, tag=None):
+            first_sum("w1", e, banks[bank])
+            sigmoids[e] = sbuf("sigmoid%d" % e, [P, 2, P, 2], F32, tag)
+            nc.scalar.activation(sigmoids[e][:], by_pairs(banks[bank]), SIGMOID)
 
-        sigmoids = {}
+        def product(e, bank, tag=None):
+            first_sum("w3", e, banks[bank])
+            hidden[e] = sbuf("hidden%d" % e, [P, 2, P, 2], BF16, tag)
+            nc.vector.tensor_tensor(hidden[e][:], by_pairs(banks[bank]), sigmoids[e][:], MULT)
 
-        def product(e):
-            bank_b = banks[3 + e % 3]
-            first_sum("w3", e, bank_b)
-            hidden[e] = sbuf("hidden%d" % e, [P, 2, P, 2], BF16)
-            nc.vector.tensor_tensor(hidden[e][:], by_pairs(bank_b), sigmoids[e][:], MULT)
-
-        grouped = {lo: sbuf("grouped%d" % lo, [P, PAIR, 4 * C], BF16) for lo in range(0, E, PAIR)}
-
-        def turn(lo, bank):
-            for place in range(PAIR):
-                value_pairs = hidden[lo + place][:].rearrange("p u q v -> p (u q v)").bitcast(F32)
+        def turn(lo, hi, bank, tag=None):
+            bank = banks[bank]
+            grouped[lo] = sbuf("grouped%d" % lo, [P, hi - lo, 4 * C], BF16, tag)
+            for e in range(lo, hi):
+                value_pairs = hidden[e][:].rearrange("p u q v -> p (u q v)").bitcast(F32)
                 for u in range(2):
-                    nc.tensor.transpose(bank[:, 2 * place + u, :], value_pairs[:, u * P : (u + 1) * P], identity[:])
+                    nc.tensor.transpose(bank[:, 2 * (e - lo) + u, :], value_pairs[:, u * P : (u + 1) * P], identity[:])
             nc.scalar.copy(
                 grouped[lo][:].bitcast(F32).rearrange("p e (c u) -> p e c u", u=2),
-                bank[:].rearrange("p (e u) c -> p e c u", u=2),
+                bank[:, 0 : 2 * (hi - lo), :].rearrange("p (e u) c -> p e c u", u=2),
             )
 
-        def quantise(lo, tag=None):
-            hi = lo + PAIR
+        def quantise(lo, hi, tag=None):
             values = grouped[lo][:].rearrange("p e c -> p (e c)")
             h_words = sbuf("h_words%d" % lo, [P, (hi - lo) * C], U32, tag)
             h_scales = sbuf("h_scales%d" % lo, [P, (hi - lo) * C], U8)
@@ -166,90 +142,127 @@ def tile_moe_two_glu_sigmoid_kernel(
                 cols = slice((e - lo) * C, (e - lo + 1) * C)
                 quantised[e] = (h_words[:, cols], h_scales[:, cols])
 
-        def second_sums(t, lo, hi, bank):
-            for e in range(lo, hi):
-                h_words, h_scales = quantised[e]
-                nc.tensor.matmul_mx(
-                    out=bank[:, e - lo, :],
-                    lhsT=words["w2"][:, e, 2 * P * t : 2 * P * (t + 1)].bitcast(FP4X4),
-                    lhsT_scale=planes["w2"][:, e, P * t : P * (t + 1)],
-                    rhs=h_words.bitcast(FP8X4),
-                    rhs_scale=h_scales,
-                    start=True,
-                    stop=True,
-                )
-            return flat(bank)[:, 0 : (hi - lo) * C]
+        def second_sums(ts, lo, hi, bank):
+            bank = banks[bank]
+            for place, t in enumerate(ts):
+                for e in range(lo, hi):
+                    h_words, h_scales = quantised[e]
+                    nc.tensor.matmul_mx(
+                        out=bank[:, place * (hi - lo) + e - lo, :],
+                        lhsT=words["w2", e, t].bitcast(FP4X4),
+                        lhsT_scale=planes["w2", e][:, P * t : P * (t + 1)],
+                        rhs=h_words.bitcast(FP8X4),
+                        rhs_scale=h_scales,
+                        start=True,
+                        stop=True,
+                    )
+            used = flat(bank)[:, 0 : len(ts) * (hi - lo) * C]
+            return used.rearrange("p (t c) -> p t c", t=len(ts))
 
-        staged = {}
-
-        def stage(t, lo, bank, gated, tag=None, values=None, hi=None):
-            hi = hi or lo + PAIR
-            sums = second_sums(t, lo, hi, bank)
+        def stage(ts, lo, hi, bank, gated, values=None, tag=None):
+            sums = second_sums(ts, lo, hi, bank)
+            shape = [P, len(ts), (hi - lo) * C]
             if values is None:
-                values = sbuf("staged%d_%d" % (t, lo), [P, (hi - lo) * C], F32, tag)
+                values = sbuf("staged%d_%d" % (ts[0], lo), shape, F32, tag)[:]
             if gated:
-                nc.vector.tensor_tensor(values[:], sums, gates[:, lo * C : hi * C], MULT)
+                nc.vector.tensor_tensor(values, sums, gates_of(lo, hi).unsqueeze(1).to_broadcast(shape), MULT)
             else:
-                nc.scalar.copy(values[:], sums)
-            staged[t, lo] = (values, gated)
+                nc.scalar.copy(values, sums)
+            return values
 
-        def scatter(t, lo, hi=None, values=None, on_scalar=None):
-            hi = hi or lo + PAIR
-            gated = True
-            if values is None:
-                values, gated = staged[t, lo]
-            if on_scalar is None:
-                on_scalar = t % 2 == 0
+        def scatter(t, lo, hi, values, how, last=False, queue=None):
             into = windows[t][:].indirect(dst_sb[:, lo * LIST_COLS : hi * LIST_COLS])
-            if on_scalar:
-                nc.scalar.activation(into, values[:], COPY)
-            elif gated:
-                nc.vector.tensor_copy(into, values[:])
+            if how == "scalar":
+                nc.scalar.activation(into, values, COPY)
+            elif how == "scaled":
+                nc.scalar.activation(into, values, COPY, scale=one[:])
+            elif how == "vector":
+                nc.vector.tensor_copy(into, values)
             else:
-                nc.vector.tensor_tensor(into, values[:], gates[:, lo * C : hi * C], MULT)
-            if hi == E:
-                nc.sync.dma_start(out[t * P : (t + 1) * P, :], windows[t][:])
+                nc.vector.tensor_tensor(into, values, gates_of(lo, hi), MULT)
+            if last:
+                (queue or nc.sync).dma_start(out[t * P : (t + 1) * P, :], windows[t][:])
 
-        def sigmoid(e):
-            first_sum("w1", e, banks[A_BANKS[e]])
-            sigmoids[e] = sbuf("sigmoid%d" % e, [P, 2, P, 2], F32)
-            nc.scalar.activation(sigmoids[e][:], by_pairs(banks[A_BANKS[e]]), SIGMOID)
+        def new_window(t, engine, tag=None):
+            windows[t] = sbuf("window%d" % t, [P, T], F32, tag)
+            if engine == "scalar":
+                nc.scalar.copy(windows[t][:], zero[:].to_broadcast([P, T]))
+            elif engine == "vector":
+                nc.vector.memset(windows[t][:].bitcast(I32), 0)
+            else:
+                nc.gpsimd.memset(windows[t][:].bitcast(I32), 0)
 
+        x_sb = sbuf("x_sb", [P, T], I32)
+        x_plane = sbuf("x_plane", [P, T], U8)
+
+        def load_x():
+            nc.sync.dma_start(x_sb[:], x_words[0].rearrange("p n t -> p (n t)").bitcast(I32))
+
+        def load_x_plane():
+            load_rows(x_plane[:].bitcast(I32), x_scales.bitcast(I32).rearrange("o (q r) n -> r q (o n)", r=PLANE_ROWS))
+
+        def gather_words(lo, hi, tag=None):
+            gather(slot_words, "slot_words", U32, x_sb[:].bitcast(U32), lo, hi, tag)
+
+        def gather_scales(lo, hi, tag=None):
+            gather(slot_scales, "slot_scales", U8, x_plane[:], lo, hi, tag)
+
+        nc.vector.memset(zero[:], 0.0)
+        nc.vector.memset(x_plane[:].bitcast(I32), 0)
+        nc.scalar.activation(warm[:], zero[:], SIGMOID)
+        new_plane("w1", 0, E)
+        new_plane("w3", 0, E)
+        nc.vector.memset(one[:], 1.0)
+        new_plane("w2", 0, E, on_scalar=True)
+
+        load_x()
+        nc.sync.dma_start(offs_sb[:], offs)
+        load_x_plane()
+        load_words("w1", 0, 3)
+        load_plane("w1", 0, E)
+        load_words("w3", 0, 3)
+        load_plane("w3", 0, E)
+        load_words("w1", 3, E)
+        load_words("w3", 3, E)
+        load_plane("w2", 0, E)
+        load_words("w2", 0, 2)
+        nc.sync.dma_start(dst_sb[:], dst)
+        load_gates(0, E)
+        load_words("w2", 2, E)
+
+        gather_words(0, 3)
+        gather_scales(0, 3)
+        gather_scales(3, E)
+        gather_words(3, E, tag="x_plane")
+        identity = sbuf("identity", [P, P], F32, tag="x_sb")
+        make_identity(nc, identity[:])
+        for t in range(NT - 1):
+            new_window(t, "scalar")
+
+        A_BANKS = (0, 1, 2, 6, 7, 0)
         for e in range(5):
-            sigmoid(e)
-            product(e)
-        windows.append(sbuf("window3", [P, T], F32, tag="slot_words0"))
-        nc.gpsimd.memset(windows[NT - 1][:].bitcast(I32), 0)
-        turn(0, banks[6])
-        quantise(0, tag="sigmoid4")
-        sigmoid(5)
-        product(5)
-        turn(2, banks[7])
-        quantise(2, tag="sigmoid5")
-        stage(0, 0, banks[2], True)
-        stage(1, 0, banks[1], False)
-        scatter(0, 0)
-        scatter(1, 0)
-        turn(4, banks[2])
-        for_scalar = sbuf("for_scalar", [P, 2, PAIR * C], F32, tag="hidden5")
-        for_vector = sbuf("for_vector", [P, 2, PAIR * C], F32, tag="hidden4")
-        stage(0, 2, banks[0], True, values=for_scalar[:, 0, :])
-        stage(2, 0, banks[3], True, values=for_scalar[:, 1, :])
-        stage(1, 2, banks[6], False, values=for_vector[:, 0, :])
-        stage(3, 0, banks[4], False, values=for_vector[:, 1, :])
-        quantise(4)
-        scatter(0, 2)
-        scatter(1, 2)
-        stage(0, 4, banks[1], True)
-        stage(1, 4, banks[5], False)
-        scatter(2, 0)
-        scatter(3, 0)
-        stage(2, 2, banks[7], True, tag="hidden5")
-        scatter(0, 4, 5, staged[0, 4][0][:, :C])
-        scatter(1, 4)
-        stage(2, 4, banks[1], True)
-        stage(3, 2, banks[6], True, tag="staged1_4", hi=E)
-        scatter(0, 5, E, staged[0, 4][0][:, C:], on_scalar=False)
-        scatter(2, 2)
-        scatter(2, 4)
-        scatter(3, 2, E)
+            sigmoid(e, A_BANKS[e])
+            product(e, 3 + e % 3)
+        turn(0, 2, 6)
+        quantise(0, 2, tag="sigmoid4")
+        sigmoid(5, A_BANKS[5])
+        product(5, 5)
+        turn(2, 4, 7)
+        quantise(2, 4, tag="sigmoid5")
+        y10 = stage((1, 3), 0, 2, 1, False)
+        y00 = stage((0, 2), 0, 2, 2, True)
+        turn(4, E, 1)
+        new_window(3, "gpsimd", tag="hidden5")
+        scatter(1, 0, 2, y10[:, 0, :], "gating")
+        quantise(4, E)
+        scatter(0, 0, 2, y00[:, 0, :], "scalar")
+        scatter(2, 0, 2, y00[:, 1, :], "scalar")
+        scatter(3, 0, 2, y10[:, 1, :], "gating")
+        y12 = stage((1,), 2, E, 0, False)
+        y02 = stage((0,), 2, E, 3, True)
+        y22 = stage((2,), 2, E, 4, True)
+        y32 = stage((3,), 2, E, 5, True)
+        scatter(0, 2, E, y02[:, 0, :], "scaled", last=True)
+        scatter(1, 2, E, y12[:, 0, :], "gating", last=True)
+        scatter(2, 2, E, y22[:, 0, :], "scaled", last=True)
+        scatter(3, 2, E, y32[:, 0, :], "vector", last=True)

@@ -121,20 +121,22 @@ def tile_moe_two_glu_sigmoid_kernel(
             hidden[e] = sbuf("hidden%d" % e, [P, 2, P, 2], BF16, tag)
             nc.vector.tensor_tensor(hidden[e][:], by_pairs(banks[bank]), sigmoids[e][:], MULT)
 
-        def turn(lo, hi, bank, tag=None):
+        def turn(lo, hi, bank, tag=None, into=None):
             bank = banks[bank]
-            grouped[lo] = sbuf("grouped%d" % lo, [P, hi - lo, 4 * C], BF16, tag)
+            if into is None:
+                into = sbuf("grouped%d" % lo, [P, hi - lo, 4 * C], BF16, tag)[:]
+                grouped[lo] = into
             for e in range(lo, hi):
                 value_pairs = hidden[e][:].rearrange("p u q v -> p (u q v)").bitcast(F32)
                 for u in range(2):
                     nc.tensor.transpose(bank[:, 2 * (e - lo) + u, :], value_pairs[:, u * P : (u + 1) * P], identity[:])
             nc.scalar.copy(
-                grouped[lo][:].bitcast(F32).rearrange("p e (c u) -> p e c u", u=2),
+                into.bitcast(F32).rearrange("p e (c u) -> p e c u", u=2),
                 bank[:, 0 : 2 * (hi - lo), :].rearrange("p (e u) c -> p e c u", u=2),
             )
 
         def quantise(lo, hi, tag=None):
-            values = grouped[lo][:].rearrange("p e c -> p (e c)")
+            values = grouped[lo].rearrange("p e c -> p (e c)")
             h_words = sbuf("h_words%d" % lo, [P, (hi - lo) * C], U32, tag)
             h_scales = sbuf("h_scales%d" % lo, [P, (hi - lo) * C], U8)
             nc.vector.quantize_mx(out=h_words[:].bitcast(FP8X4), scales=h_scales[:], in_=values)
@@ -226,9 +228,9 @@ def tile_moe_two_glu_sigmoid_kernel(
         load_words("w3", 3, E)
         load_plane("w2", 0, E)
         load_words("w2", 0, 2)
-        nc.sync.dma_start(dst_sb[:], dst)
         load_gates(0, E)
         load_words("w2", 2, E)
+        nc.sync.dma_start(dst_sb[:], dst)
 
         gather_words(0, 3)
         gather_scales(0, 3)
@@ -243,25 +245,27 @@ def tile_moe_two_glu_sigmoid_kernel(
         for e in range(5):
             sigmoid(e, A_BANKS[e])
             product(e, 3 + e % 3)
+        new_window(3, "gpsimd", tag="slot_words0")
         turn(0, 2, 6)
         quantise(0, 2, tag="sigmoid4")
         sigmoid(5, A_BANKS[5])
         product(5, 5)
         turn(2, 4, 7)
         quantise(2, 4, tag="sigmoid5")
-        y10 = stage((1, 3), 0, 2, 1, False)
-        y00 = stage((0, 2), 0, 2, 2, True)
-        turn(4, E, 1)
-        new_window(3, "gpsimd", tag="hidden5")
-        scatter(1, 0, 2, y10[:, 0, :], "gating")
+        turn(4, E, 3)
         quantise(4, E)
+        y00 = stage((0,), 0, 2, 2, True)
+        y10 = stage((1,), 0, 2, 1, False)
+        y30 = stage((3,), 0, 2, 0, False)
+        y20 = stage((2,), 0, 2, 4, True)
+        y02 = stage((0,), 2, E, 7, True)
+        scatter(1, 0, 2, y10[:, 0, :], "gating")
         scatter(0, 0, 2, y00[:, 0, :], "scalar")
-        scatter(2, 0, 2, y00[:, 1, :], "scalar")
-        scatter(3, 0, 2, y10[:, 1, :], "gating")
-        y12 = stage((1,), 2, E, 0, False)
-        y02 = stage((0,), 2, E, 3, True)
-        y22 = stage((2,), 2, E, 4, True)
+        scatter(2, 0, 2, y20[:, 0, :], "scalar")
+        y12 = stage((1,), 2, E, 6, False)
+        y22 = stage((2,), 2, E, 3, True)
         y32 = stage((3,), 2, E, 5, True)
+        scatter(3, 0, 2, y30[:, 0, :], "gating")
         scatter(0, 2, E, y02[:, 0, :], "scaled", last=True)
         scatter(1, 2, E, y12[:, 0, :], "gating", last=True)
         scatter(2, 2, E, y22[:, 0, :], "scaled", last=True)

@@ -93,6 +93,7 @@ def tile_moe_two_glu_sigmoid_kernel(
             nc.vector.tensor_copy(gathered[:], source.indirect(offs_sb[:, lo * LIST_COLS : hi * LIST_COLS]))
             for e in range(lo, hi):
                 into[e] = gathered[:, (e - lo) * C : (e - lo + 1) * C]
+            return gathered
 
         def flat(bank):
             return bank[:].rearrange("p t c -> p (t c)")
@@ -207,7 +208,7 @@ def tile_moe_two_glu_sigmoid_kernel(
             gather(slot_words, "slot_words", U32, x_sb[:].bitcast(U32), lo, hi, tag)
 
         def gather_scales(lo, hi, tag=None):
-            gather(slot_scales, "slot_scales", U8, x_plane[:], lo, hi, tag)
+            return gather(slot_scales, "slot_scales", U8, x_plane[:], lo, hi, tag)
 
         nc.vector.memset(zero[:], 0.0)
         nc.vector.memset(x_plane[:].bitcast(I32), 0)
@@ -252,7 +253,9 @@ def tile_moe_two_glu_sigmoid_kernel(
         product(5, 5)
         turn(2, 4, 7)
         quantise(2, 4, tag="sigmoid5")
-        turn(4, E, 3)
+        grouped[4] = sbuf("grouped4", [P, 2, 4 * C], BF16)[:]
+        turn(4, 5, 3, into=grouped[4][:, 0:1, :])
+        turn(5, E, 4, into=grouped[4][:, 1:2, :])
         quantise(4, E)
         y00 = stage((0,), 0, 2, 2, True)
         y10 = stage((1,), 0, 2, 1, False)

from contextlib import ExitStack

import concourse.mybir as mybir
from concourse.masks import make_identity

K, T, E, C, H, N = 512, 1024, 6, 128, 512, 512
FLOPS = 2 * E * C * (2 * K * H + H * N)

F32 = mybir.dt.float32
BF16 = mybir.dt.bfloat16
I32 = mybir.dt.int32
U32 = mybir.dt.uint32
U16 = mybir.dt.uint16
U8 = mybir.dt.uint8
FP8X4 = mybir.dt.float8_e4m3fn_x4
FP4X4 = mybir.dt.float4_e2m1fn_x4
MULT = mybir.AluOpType.mult
SIGMOID = mybir.ActivationFunctionType.Sigmoid
COPY = mybir.ActivationFunctionType.Copy

P = 128
NT = N // P
LIST_COLS = C // 16
PLANE_ROWS = 4
BANKS = 8


def tile_moe_two_glu_sigmoid_kernel(
    tc, x_words, x_scales, w1_words, w1_scales, w3_words, w3_scales, w2_words, w2_scales, gate, offs, dst, out
):
    nc = tc.nc
    with ExitStack() as ctx:
        keep = ctx.enter_context(tc.tile_pool(name="keep", bufs=1))
        psum = ctx.enter_context(tc.psum_pool(name="psum", bufs=1))

        def sbuf(name, shape, dtype, tag=None):
            return keep.tile(shape, dtype, name=name, tag=tag or name, align_bytes=64)

        offs_sb = keep.tile([P, E * LIST_COLS], U16, name="offs_sb")
        dst_sb = keep.tile([P, E * LIST_COLS], U16, name="dst_sb")
        banks = [psum.tile([P, NT, C], F32, name="bank%d" % b) for b in range(BANKS)]
        dram_words = {"w1": w1_words, "w3": w3_words, "w2": w2_words}
        dram_scales = {"w1": w1_scales, "w3": w3_scales, "w2": w2_scales}
        zero = sbuf("zero", [P, 1], F32)
        warm = sbuf("warm", [P, 1], F32)
        one = sbuf("one", [P, 1], F32)
        plane_tiles, planes, words, gates, windows = {}, {}, {}, {}, {}
        slot_words, slot_scales, sigmoids, hidden, grouped, quantised = {}, {}, {}, {}, {}, {}

        def zero_on_scalar(tile, columns):
            nc.scalar.copy(tile.bitcast(U32), zero[:].bitcast(U32).to_broadcast([P, columns]))

        def new_plane(name, lo, hi, on_scalar=False):
            tile = sbuf("%s_plane%d" % (name, lo), [P, hi - lo, H], U8)
            plane_tiles[name, lo] = tile
            for e in range(lo, hi):
                planes[name, e] = tile[:, e - lo, :]
            if on_scalar:
                zero_on_scalar(tile[:].rearrange("p e n -> p (e n)"), (hi - lo) * H // 4)
            else:
                nc.vector.memset(tile[:].bitcast(I32), 0)

        def load_rows(plane, rows):
            for r in range(PLANE_ROWS):
                nc.sync.dma_start(plane[r:P:32], rows[r])

        def load_plane(name, lo, hi):
            rows = dram_scales[name].bitcast(I32)[lo:hi].rearrange("e s (q r) n -> r q (e s) n", r=PLANE_ROWS)
            load_rows(plane_tiles[name, lo][:].bitcast(I32), rows)

        def load_words(name, lo, hi, t0=0, t1=NT):
            width = 2 * P * (t1 - t0)
            tile = sbuf("%s_words%d_%d" % (name, lo, t0), [P, hi - lo, width], U8)
            rows = dram_words[name].bitcast(I32)[lo:hi].rearrange("e s p b -> p (e s) b")
            nc.sync.dma_start(tile[:].bitcast(I32), rows[:, :, t0 * P // 2 : t1 * P // 2])
            for e in range(lo, hi):
                words[name, e] = tile[:, e - lo, :]
                for t in range(t0, t1):
                    words[name, e, t] = tile[:, e - lo, 2 * P * (t - t0) : 2 * P * (t - t0 + 1)]

        def load_gates(lo, hi):
            tile = sbuf("gates%d" % lo, [P, (hi - lo) * C], F32)
            nc.sync.dma_start(tile[:], gate[0:P, lo * C : hi * C])
            for e in range(lo, hi):
                gates[e] = (tile, lo)

        def gates_of(lo, hi):
            tile, first = gates[lo]
            return tile[:, (lo - first) * C : (hi - first) * C]

        def gather(into, name, dtype, source, lo, hi, tag=None):
            gathered = sbuf("%s%d" % (name, lo), [P, (hi - lo) * C], dtype, tag)
            nc.vector.tensor_copy(gathered[:], source.indirect(offs_sb[:, lo * LIST_COLS : hi * LIST_COLS]))
            for e in range(lo, hi):
                into[e] = gathered[:, (e - lo) * C : (e - lo + 1) * C]
            return gathered

        def flat(bank):
            return bank[:].rearrange("p t c -> p (t c)")

        def by_pairs(bank):
            return flat(bank).rearrange("p (q u v) -> p u q v", u=2, v=2)

        def first_sum(name, e, bank):
            nc.tensor.matmul_mx(
                out=flat(bank),
                lhsT=slot_words[e].bitcast(FP8X4),
                lhsT_scale=slot_scales[e],
                rhs=words[name, e].bitcast(FP4X4),
                rhs_scale=planes[name, e],
                start=True,
                stop=True,
            )

        def sigmoid(e, bank, tag=None):
            first_sum("w1", e, banks[bank])
            sigmoids[e] = sbuf("sigmoid%d" % e, [P, 2, P, 2], F32, tag)
            nc.scalar.activation(sigmoids[e][:], by_pairs(banks[bank]), SIGMOID)

        def product(e, bank, tag=None):
            first_sum("w3", e, banks[bank])
            hidden[e] = sbuf("hidden%d" % e, [P, 2, P, 2], BF16, tag)
            nc.vector.tensor_tensor(hidden[e][:], by_pairs(banks[bank]), sigmoids[e][:], MULT)

        def turn(lo, hi, bank, tag=None, into=None):
            bank = banks[bank]
            if into is None:
                into = sbuf("grouped%d" % lo, [P, hi - lo, 4 * C], BF16, tag)[:]
                grouped[lo] = into
            for e in range(lo, hi):
                value_pairs = hidden[e][:].rearrange("p u q v -> p (u q v)").bitcast(F32)
                for u in range(2):
                    nc.tensor.transpose(bank[:, 2 * (e - lo) + u, :], value_pairs[:, u * P : (u + 1) * P], identity[:])
            nc.scalar.copy(
                into.bitcast(F32).rearrange("p e (c u) -> p e c u", u=2),
                bank[:, 0 : 2 * (hi - lo), :].rearrange("p (e u) c -> p e c u", u=2),
            )

        def quantise(lo, hi, tag=None):
            values = grouped[lo].rearrange("p e c -> p (e c)")
            h_words = sbuf("h_words%d" % lo, [P, (hi - lo) * C], U32, tag)
            h_scales = sbuf("h_scales%d" % lo, [P, (hi - lo) * C], U8)
            nc.vector.quantize_mx(out=h_words[:].bitcast(FP8X4), scales=h_scales[:], in_=values)
            for e in range(lo, hi):
                cols = slice((e - lo) * C, (e - lo + 1) * C)
                quantised[e] = (h_words[:, cols], h_scales[:, cols])

        def second_sums(ts, lo, hi, bank):
            bank = banks[bank]
            for place, t in enumerate(ts):
                for e in range(lo, hi):
                    h_words, h_scales = quantised[e]
                    nc.tensor.matmul_mx(
                        out=bank[:, place * (hi - lo) + e - lo, :],
                        lhsT=words["w2", e, t].bitcast(FP4X4),
                        lhsT_scale=planes["w2", e][:, P * t : P * (t + 1)],
                        rhs=h_words.bitcast(FP8X4),
                        rhs_scale=h_scales,
                        start=True,
                        stop=True,
                    )
            used = flat(bank)[:, 0 : len(ts) * (hi - lo) * C]
            return used.rearrange("p (t c) -> p t c", t=len(ts))

        def stage(ts, lo, hi, bank, gated, values=None, tag=None):
            sums = second_sums(ts, lo, hi, bank)
            shape = [P, len(ts), (hi - lo) * C]
            if values is None:
                values = sbuf("staged%d_%d" % (ts[0], lo), shape, F32, tag)[:]
            if gated:
                nc.vector.tensor_tensor(values, sums, gates_of(lo, hi).unsqueeze(1).to_broadcast(shape), MULT)
            else:
                nc.scalar.copy(values, sums)
            return values

        def scatter(t, lo, hi, values, how, last=False, queue=None):
            into = windows[t][:].indirect(dst_sb[:, lo * LIST_COLS : hi * LIST_COLS])
            if how == "scalar":
                nc.scalar.activation(into, values, COPY)
            elif how == "scaled":
                nc.scalar.activation(into, values, COPY, scale=one[:])
            elif how == "vector":
                nc.vector.tensor_copy(into, values)
            else:
                nc.vector.tensor_tensor(into, values, gates_of(lo, hi), MULT)
            if last:
                (queue or nc.sync).dma_start(out[t * P : (t + 1) * P, :], windows[t][:])

        def new_window(t, engine, tag=None):
            windows[t] = sbuf("window%d" % t, [P, T], F32, tag)
            if engine == "scalar":
                nc.scalar.copy(windows[t][:], zero[:].to_broadcast([P, T]))
            elif engine == "vector":
                nc.vector.memset(windows[t][:].bitcast(I32), 0)
            else:
                nc.gpsimd.memset(windows[t][:].bitcast(I32), 0)

        x_sb = sbuf("x_sb", [P, T], I32)
        x_plane = sbuf("x_plane", [P, T], U8)

        def load_x():
            nc.sync.dma_start(x_sb[:], x_words[0].rearrange("p n t -> p (n t)").bitcast(I32))

        def load_x_plane():
            load_rows(x_plane[:].bitcast(I32), x_scales.bitcast(I32).rearrange("o (q r) n -> r q (o n)", r=PLANE_ROWS))

        def gather_words(lo, hi, tag=None):
            gather(slot_words, "slot_words", U32, x_sb[:].bitcast(U32), lo, hi, tag)

        def gather_scales(lo, hi, tag=None):
            return gather(slot_scales, "slot_scales", U8, x_plane[:], lo, hi, tag)

        nc.vector.memset(zero[:], 0.0)
        nc.vector.memset(x_plane[:].bitcast(I32), 0)
        nc.scalar.activation(warm[:], zero[:], SIGMOID)
        new_plane("w1", 0, E)
        new_plane("w3", 0, E)
        nc.vector.memset(one[:], 1.0)
        new_plane("w2", 0, E, on_scalar=True)

        load_x()
        nc.sync.dma_start(offs_sb[:], offs)
        load_x_plane()
        load_words("w1", 0, 3)
        load_plane("w1", 0, E)
        load_words("w3", 0, 3)
        load_plane("w3", 0, E)
        load_words("w1", 3, E)
        load_words("w3", 3, E)
        load_plane("w2", 0, E)
        load_words("w2", 0, 2)
        load_gates(0, E)
        load_words("w2", 2, E)
        nc.sync.dma_start(dst_sb[:], dst)

        gather_words(0, 3)
        gather_scales(0, 3)
        gather_scales(3, E)
        gather_words(3, E, tag="x_plane")
        identity = sbuf("identity", [P, P], F32, tag="x_sb")
        make_identity(nc, identity[:])
        for t in range(NT - 1):
            new_window(t, "scalar")

        A_BANKS = (0, 1, 2, 6, 7, 0)
        for e in range(5):
            sigmoid(e, A_BANKS[e])
            product(e, 3 + e % 3)
        new_window(3, "gpsimd", tag="slot_words0")
        turn(0, 2, 6)
        quantise(0, 2, tag="sigmoid4")
        sigmoid(5, A_BANKS[5])
        product(5, 5)
        turn(2, 4, 7)
        quantise(2, 4, tag="sigmoid5")
        grouped[4] = sbuf("grouped4", [P, 2, 4 * C], BF16)[:]
        turn(4, 5, 3, into=grouped[4][:, 0:1, :])
        turn(5, E, 4, into=grouped[4][:, 1:2, :])
        quantise(4, E)
        y00 = stage((0,), 0, 2, 2, True)
        y10 = stage((1,), 0, 2, 1, False)
        y30 = stage((3,), 0, 2, 0, False)
        y20 = stage((2,), 0, 2, 4, True)
        y02 = stage((0,), 2, E, 7, True)
        scatter(1, 0, 2, y10[:, 0, :], "gating")
        scatter(0, 0, 2, y00[:, 0, :], "scalar")
        scatter(2, 0, 2, y20[:, 0, :], "scalar")
        y12 = stage((1,), 2, E, 6, False)
        y22 = stage((2,), 2, E, 3, True)
        y32 = stage((3,), 2, E, 5, True)
        scatter(3, 0, 2, y30[:, 0, :], "gating")
        scatter(0, 2, E, y02[:, 0, :], "scaled", last=True)
        scatter(1, 2, E, y12[:, 0, :], "gating", last=True)
        scatter(2, 2, E, y22[:, 0, :], "scaled", last=True)
        scatter(3, 2, E, y32[:, 0, :], "vector", last=True)
